import numpy as np, ml_dtypes
CORES = [40,41,42,43,44,45,46,47]
N = 8
BF = ml_dtypes.bfloat16
def gentries(a):
    return np.ascontiguousarray(a.reshape(8, 16, -1).transpose(0, 2, 1)).reshape(8, -1)
def gtable(e):
    e = np.asarray(e); return np.ascontiguousarray(e.reshape(8, -1, 16).transpose(0, 2, 1)).reshape(128, -1).astype(np.int32)
S, K, W, C, RO = 512, 8, 4096, 8, 4
def H(e, v):
    return ((e * v >> 5) + e + 37 * v) & (W - 1)
def U(x, w):
    return np.add.reduce(x * w, axis=-1, dtype=np.int32) & (W - 1)
def applies(d, x, least):
    return np.add.reduce(d > x, axis=-1, dtype=np.int32) >= least
def parts(rng):
    lev = rng.choice(np.array([96, 160, 256]), (N, 8, 1, W))
    d = (rng.random((N, 8, 16, W)) * lev).astype(np.int64)
    return d, rng.integers(0, W, (N, 8, S, K)), rng.integers(0, 256, (N, 8, 16, S)), rng.integers(1, 256, (N, 8, 16))
def pack(d, e, z, w):
    return {"dv": d.reshape(N, 128, W).astype(np.float32).astype(BF), "ef": np.stack([gtable(a.reshape(8, -1)) for a in e]),
            "zv": z.reshape(N, 128, S).astype(np.float32).astype(BF), "wt": w.reshape(N, 128, 1).astype(np.int32)}
def stage(rng, d, w, r, g):
    o = rng.permutation(16); w[r, g] = 1; w[r, g, o[:8]] = 255
    m = np.zeros(16, np.int64); m[o[:4]] = 255; m[o[8:12]] = 255
    q = np.zeros(16, np.int64); q[rng.permutation(o[:15])[:9]] = 255
    row = int(o[15]); one = np.zeros(16, np.int64); one[row] = 255
    d[r, g, :, 0] = m; d[r, g, :, W - 1] = q; d[r, g, :, H(W - 1, 255 * 1024 & (W - 1))] = 255
    d[r, g, :, H(0, 255)] = m + one; d[r, g, :, H(W - 1, 255)] = q + one
    return row
def setup_inputs(rng):
    return pack(*parts(rng))
def setup_inputs_corners(rng):
    d, e, z, w = parts(rng); i = np.arange(S); kk = np.arange(K)
    for r in range(N):
        for g in range(8):
            if (r + g) % 2 == 1:
                stage(rng, d, w, r, g)
                few = np.argsort(np.argsort(rng.random((16, 64)), axis=0), axis=0) < np.where(np.arange(64) % 4 == 1, 0, 7)
                d[r, g, :, 16:80] = few * rng.integers(1, 256, (16, 64))
                goal = rng.choice(np.array([0, 1, 2, K - 2, K - 1]), S)[:, None]
                cold = rng.integers(16, 80, (S, K))
                v = np.where((kk < goal) | (goal == 0), cold, np.where(kk == goal, W - 1, e[r, g])); v[:, 0] = 0
                m = i % 4 != 3
                e[r, g] = np.where(m[:, None], v, e[r, g]); z[r, g] = np.where(m, 0, z[r, g])
            else:
                e[r, g, ::4] = e[r, g, ::4, :1]; e[r, g, 1::4] = (W - 1) * rng.integers(0, 2, e[r, g, 1::4].shape)
                z[r, g, :, 5::8] = 255; z[r, g, :, 6::8] = 0
    return pack(d, e, z, w)
def setup_inputs_ends(rng):
    p = rng.choice(np.array([0.0, 0.25, 0.5, 0.75, 0.9, 1.0]), (N, 8, 1, W)); d = 255 * (rng.random((N, 8, 16, W)) < p).astype(np.int64)
    d[..., 2::4] = rng.integers(0, 256, d[..., 2::4].shape)
    p = rng.choice(np.array([0.0, 0.1, 0.3, 0.5, 1.0]), (N, 8, 1, S)); z = 255 * (rng.random((N, 8, 16, S)) < p).astype(np.int64)
    z[..., 2::5] = rng.integers(0, 256, z[..., 2::5].shape)
    e = (W - 1) * rng.integers(0, 2, (N, 8, S, K)); w = np.where(rng.random((N, 8, 16)) < 0.5, 1, 255)
    for r in range(N):
        for g in range(8):
            if r < 2:
                row = stage(rng, d, w, r, g); z[r, g] = 0; z[r, g, row] = 255 * rng.integers(0, 2, S); z[r, g, row, 0] = 255; z[r, g, row, S - 1] = 0
                e[r, g, :, 0] = 0; e[r, g, :, 1:3] = 2 + 4 * rng.integers(0, W // 4, (S, 2)); e[r, g, :, K - 1] = W - 1
            elif (r == N - 1 and g == 7) or (r == N - 2 and g == 6):
                w[r, g] = 255; z[r, g, :, 1] = 255; z[r, g, :, S - 1] = 255; z[r, g, :, 3] = 0
            else:
                w[r, g, 13:15] = 1; w[r, g, 15] = 255
                for j in (1, S - 1):
                    z[r, g, :, j] = 0; z[r, g, 13:, j] = 255; e[r, g, j, 0] = W - 1; e[r, g, j, K - 1] = W - 1
    z[0, 7, :, S - 1] = 255
    return pack(d, e, z, w)
def setup_inputs_full(rng):
    d, e, z, w = parts(rng); i = np.arange(S); kk = np.arange(K); quiet = int(rng.integers(0, N)); turn = int(rng.integers(0, 8))
    for r in range(N):
        for g in range(8):
            kind = (5, 1, 5, 3)[g % 4] if r == quiet else (g + 3 * r + turn) % 8
            if kind == 1:
                o = np.argsort(np.argsort(rng.random((16, S)), axis=0), axis=0)
                z[r, g] = np.where(o < rng.integers(9, 17, S), 255, z[r, g])
            elif kind == 2:
                stage(rng, d, w, r, g)
                few = np.argsort(np.argsort(rng.random((16, 64)), axis=0), axis=0) < np.where(np.arange(64) % 4 == 1, 0, 7)
                d[r, g, :, 16:80] = few * rng.integers(1, 256, (16, 64))
                goal = rng.integers(4, K, S)[:, None]
                v = np.where(kk < goal, rng.integers(16, 80, (S, K)), np.where(kk == goal, W - 1, e[r, g])); v[:, 0] = 0
                m = i % 8 != 5
                e[r, g] = np.where(m[:, None], v, e[r, g]); z[r, g] = np.where(m, 0, z[r, g])
            elif kind == 3 or kind == 6:
                d[r, g] = rng.integers(160, 256, (16, W)); z[r, g] = rng.integers(100, 160, (16, S))
                if kind == 6: d[r, g] = np.where(rng.random(W) < 0.04, rng.integers(0, 100, (16, W)), d[r, g])
            elif kind == 4:
                w[r, g] = 255; half = (rng.permutation(16) < 8)[:, None]
                low = half ^ (rng.random(S) < 0.5)
                z[r, g] = np.where(low, rng.integers(0, 5, (16, S)), rng.integers(251, 256, (16, S)))
                t = rng.random(W); top = np.where(t < 0.3, half, np.where(t < 0.6, ~half, t < 0.85))
                v = np.where(top, rng.integers(251, 256, (16, W)), rng.integers(0, 5, (16, W)))
                d[r, g] = np.where((t >= 0.6) & (t < 0.85), 255, v)
            elif kind == 5:
                e[r, g] = e[r, g, :, :1]
            elif kind == 7:
                w[r, g] = 255; z[r, g] = rng.integers(244, 255, (16, S))
                o = np.argsort(np.argsort(rng.random((16, W)), axis=0), axis=0)
                d[r, g] = np.where((o < rng.integers(8, 17, W)) & (rng.random(W) < 0.6), 255, d[r, g])
    return pack(d, e, z, w)
def setup_inputs_spread(rng):
    d = (np.exp2(8 * rng.random((N, 8, 1, W))) * rng.random((N, 8, 16, W))).astype(np.int64)
    z = (np.exp2(8 * rng.random((N, 8, 1, S))) * rng.random((N, 8, 16, S))).astype(np.int64)
    e = np.minimum((np.exp2((W.bit_length() - 1) * rng.random((N, 8, S, K))) * rng.random((N, 8, S, K))).astype(np.int64), W - 1)
    e = np.where(rng.random((N, 8, S, 1)) < 0.5, W - 1 - e, e)
    w = np.minimum(1 + (np.exp2(8 * rng.random((N, 8, 16))) * rng.random((N, 8, 16))).astype(np.int64), 255)
    return pack(np.minimum(d, 255), e, np.minimum(z, 255), w)
def setup_inputs_ties(rng):
    d, e, z, w = parts(rng)
    d = rng.choice(np.array([0, 0, 100, 252]), (N, 8, 1, W)) + rng.integers(0, 4, d.shape)
    z = rng.choice(np.array([0, 100, 100, 252]), (N, 8, 1, S)) + rng.integers(0, 4, z.shape)
    e[:, :, ::4] = e[:, :, ::4, :1]; e[:, :, 1::4] = rng.choice(np.array([0, 1, W - 2, W - 1]), e[:, :, 1::4].shape)
    e[:, :, 2::4, K // 2:] = e[:, :, 2::4, :K // 2]
    return pack(d, e, z, w)
def check_inputs(d):
    bad = []
    for k, lo, hi in (("dv", 0, 255), ("ef", 0, W - 1), ("zv", 0, 255), ("wt", 1, 255)):
        x = np.asarray(d[k]).astype(np.float32)
        if not np.all((x >= lo) & (x <= hi) & (x == np.floor(x))): bad.append("range of " + k)
    return bad
def reference(dv, ef, zv, wt):
    g2 = np.arange(8)[:, None]; g3 = g2[:, :, None]; kk = np.arange(K - 1)
    D = [np.ascontiguousarray(a.astype(np.float32).astype(np.int32).reshape(8, 16, W).transpose(0, 2, 1)) for a in dv]
    E = [gentries(a).astype(np.int32).reshape(8, S, K) for a in ef]
    z = [np.ascontiguousarray(a.astype(np.float32).astype(np.int32).reshape(8, 16, S).transpose(0, 2, 1)) for a in zv]
    w = wt.astype(np.int32).reshape(N, 8, 1, 1, 16)
    A = [0] * N
    for t in range(RO):
        name = []
        for r in range(N):
            least = 8 + (A[r] & 1); e = E[r]; x = z[r][:, :, None, :]
            n = H(e, U(x, w[r]))
            d = D[r][g3, n]
            a = applies(d, x, least)
            zk = np.where(a[..., None], np.abs(x - d), x); z0 = zk[:, :, :1]
            b = applies(D[r][g3, H(e[:, :, :1], U(zk, w[r]))], zk, least)
            c = applies(D[r][g3, H(e, U(z0, w[r]))], z0, least)
            ok = (b != a[:, :, :1]) & (c == a); ok[:, :, 0] = False
            s = np.argmax(ok, axis=2)
            name.append(np.take_along_axis(n, s[:, :, None], 2)[:, :, 0])
            z[r] = np.take_along_axis(zk, s[:, :, None, None], 2)[:, :, 0]
            E[r] = np.concatenate([np.take_along_axis(e, kk + (kk >= s[:, :, None]), 2), np.zeros((8, S, 1), np.int32)], axis=2)
            A[r] = int(np.count_nonzero(s))
        for r in range(N):
            q = (r - 1 - t % (N - 1)) % N
            E[r][:, :, K - 1] = name[q]
            col = C * np.arange(S) + (name[q] & (C - 1))
            D[r][g2, col] = (D[r][g2, col] + z[q]) >> 1
    return {"yd": np.stack([a.transpose(0, 2, 1).reshape(128, W) for a in D]).astype(np.float32).astype(BF),
            "ye": np.stack([gtable(a.reshape(8, -1)) for a in E]).astype(np.float32),
            "yz": np.stack([a.transpose(0, 2, 1).reshape(128, S) for a in z]).astype(np.float32).astype(BF)}

@@ -1,0 +1,562 @@
+from concourse.mybir import dt, AluOpType, AxisListType, ActivationFunctionType
+
+OP = AluOpType
+AF = ActivationFunctionType
+RO = 4
+BIG = 1.5 * 2.0 ** 35
+MID = 1.5 * 2.0 ** 23
+SCALE = 4194304.0
+B2, B4, I4, U2 = "bfloat16", "float32", "int32", "uint16"
+SCRATCH = {}
+for _n, _w, _d in (("D", 4096, B2), ("XA0", 4608, B2), ("XA1", 4608, B2), ("XB", 4096, B2), ("GA", 4096, B2), ("GB", 4096, B2),
+                   ("GC", 4096, B2), ("DS", 2048, B2), ("DC", 512, B2), ("FL", 512, I4), ("LN", 256, U2), ("LB", 256, U2),
+                   ("LC", 256, U2), ("LS", 32, U2), ("LD", 32, U2), ("EQ0", 256, B4), ("EQ1", 256, B4), ("VF", 256, B4), ("PP", 256, B4), ("SI", 256, I4), ("HI", 256, I4), ("NI", 256, I4),
+                   ("H0", 256, B4), ("T1", 256, B4), ("PQ", 256, B4), ("PK", 256, B4), ("KEY", 256, B4), ("TR", 256, B4),
+                   ("A0T", 32, B4), ("PKS0", 32, I4), ("PKS1", 32, I4), ("TS", 32, I4), ("S0", 32, B2), ("P2", 32, B4),
+                   ("ER", 256, B4), ("MK", 256, B4), ("AR", 8, B4), ("AJ", 32, B4), ("NM", 32, I4),
+                   ("CI", 32, I4), ("CJ", 32, I4), ("BT", 192, B2), ("BN", 192, B2), ("J8", 32, I4), ("JT", 32, I4),
+                   ("ID", 128, B2), ("NG", 128, B2), ("IDF", 128, B4), ("NGF", 128, B4), ("ON15", 128, B2), ("ONS", 128, B2),
+                   ("OL", 144, B2), ("WL", 144, B2), ("XI", 144, B4), ("CTI", 256, B4), ("PI", 8, I4), ("PJ", 16, I4),
+                   ("PF", 32, B4), ("KM", 16, B4), ("WI", 1, I4), ("WF", 1, B4), ("EFI", 256, I4), ("EF", 256, B4),
+                   ("EH", 256, B2), ("EL", 256, B2), ("EHL", 512, B2), ("J4", 32, I4), ("JU", 32, I4), ("K2", 96, B2),
+                   ("K3", 256, B2), ("RX", 256, B4), ("RR", 256, B4), ("HP", 256, B2), ("BI", 128, B2), ("FX", 256, B4),
+                   ("FB", 256, B2), ("YE", 256, B4)):
+    SCRATCH[_n] = ("sbuf", [128, _w], _d)
+for _n in ("bU0", "bU", "bCA", "bCB", "bCC", "bS0", "bS1", "bM"):
+    SCRATCH[_n] = ("psum", [128, 512], B4)
+for _k in range(8):
+    SCRATCH["Q%d" % _k] = ("sbuf", [128, 144], B2)
+    SCRATCH["R%d" % _k] = ("sbuf", [128, 144], B2)
+for _t in range(RO):
+    SCRATCH["LP%d" % _t] = ("sbuf", [128, 32], I4)
+    SCRATCH["LZ%d" % _t] = ("sbuf", [128, 512], B2)
+SEMAPHORES = (["qv", "qs", "qt", "qg"] + ["ldz", "lde", "ldw", "ldd0", "ldd1", "sd0", "sd1", "sd2", "sd3", "se", "sz"]
+              + ["%s%d" % (n, t) for t in range(RO) for n in ("an", "az", "ay", "ln", "lz", "ly")])
+
+CFG = {
+    "AS": (7, 1, 5),
+    "CS": (4, 5),
+    "BS": (3, 5),
+    "NA": "01 23 45 67", "NC": "123 45 67", "NB": "123 45 67",
+    "NU": "12 34 56 7",
+    "BM": (1, 6),
+    "V": "gaa0 gaa6 gaa3 gaa2 gaa4 sga2 sga6 sga0 sga3 HC sga4 sgc3 sgc6 sgc2 sgc1 sgc7 HB sgb1 sgb2 sgb4 PQ sgb6 sgb7 KEY1 TAIL",
+    "S": "gaa7 gaa1 abs7 abs0 sga7 gaa5 abs2 RC abs4 abs1 sga1 abs3 abs6 gac4 abs5 H0 RB sgc4 sga5 gac5 gab3 sgc5 gab5 sgb3 sgb5",
+    "T": "sta7 sta1 U7 U0 na6 na2 U1 sta5 na0 U3 stc4 U5 nc1 nc6 na4 stc5 stb3 nc4 stb5 nb1 nb4 nb6",
+}
+
+
+def rank_program(g, core, T, topo):
+    rank = T.rank_of(core)
+    if rank is None:
+        return
+    N = len(T.cores)
+    AS, CS, BS = CFG["AS"], CFG["CS"], CFG["BS"]
+    eng = {"v": g.vector, "s": g.scalar, "t": g.tensor, "g": g, "y": g.sync}
+    qsem = {"v": "qv", "s": "qs", "t": "qt", "g": "qg"}
+    cnt = {"v": 0, "s": 0, "t": 0, "g": 0}
+    known = {q: {} for q in eng}
+    log = {}
+    BANKS = [b for b in SCRATCH if SCRATCH[b][0] == "psum"]
+
+    def need(q, buf, lo, hi, wr):
+        out = []
+        for e in log.get(buf, []):
+            if e[0] < hi and lo < e[1] and (wr or e[2]):
+                out.append(e[4])
+            elif buf in BANKS and e[3] != q:
+                out.append(e[4])
+        return out
+
+    def note(q, buf, lo, hi, wr, op):
+        keep = []
+        for e in log.get(buf, []):
+            covered = lo <= e[0] and e[1] <= hi
+            if covered and (wr or (not e[2] and e[3] == q)):
+                continue
+            keep.append(e)
+        keep.append([lo, hi, wr, q, op])
+        log[buf] = keep
+
+    def settle(q, ops):
+        best = {}
+        for op in ops:
+            if known[q].get(op[0], 0) < op[1]:
+                if op[0] not in best or best[op[0]][1] < op[1]:
+                    best[op[0]] = op
+        for op in sorted(best.values(), key=lambda o: -len(o[2])):
+            if known[q].get(op[0], 0) >= op[1]:
+                continue
+            eng[q].wait_ge(T.sem[op[0]], op[1])
+            for s, v in op[2].items():
+                known[q][s] = max(known[q].get(s, 0), v)
+            known[q][op[0]] = max(known[q].get(op[0], 0), op[1])
+
+    def emit(q, calls, reads, writes, sem=None, val=None, remote=False):
+        ops = []
+        for b, lo, hi in reads:
+            ops += need(q, b, lo, hi, False)
+        for b, lo, hi in writes:
+            ops += need(q, b, lo, hi, True)
+        settle(q, ops)
+        ins = None
+        for c in calls:
+            ins = c(eng[q])
+        snap = dict(known[q])
+        if sem is None:
+            cnt[q] += 1
+            sem, val = qsem[q], cnt[q]
+            ins.then_inc(T.sem[sem], 1)
+        elif not remote:
+            ins.then_inc(T.sem[sem], val)
+        snap[sem] = max(snap.get(sem, 0), val)
+        op = (sem, val, snap)
+        for b, lo, hi in reads:
+            note(q, b, lo, hi, False, op)
+        for b, lo, hi in writes:
+            note(q, b, lo, hi, True, op)
+        return op
+
+    def ap(r):
+        if len(r) > 3:
+            return T[r[0]][:, r[1]:r[2]:r[3]]
+        return T[r[0]][:, r[1]:r[2]]
+
+    def reg(r):
+        return (r[0], r[1], r[2])
+
+    def copy(out, in_):
+        emit("v", [lambda e: e.tensor_copy(ap(out), ap(in_))], [reg(in_)], [reg(out)])
+
+    def tt(out, a, b, op):
+        emit("v", [lambda e: e.tensor_tensor(ap(out), ap(a), ap(b), op)], [reg(a), reg(b)], [reg(out)])
+
+    def ts(out, a, s1, s2, op0, op1=None):
+        rd = [reg(a)] + [reg(s) for s in (s1, s2) if isinstance(s, tuple)]
+        x1 = ap(s1) if isinstance(s1, tuple) else s1
+        x2 = ap(s2) if isinstance(s2, tuple) else s2
+        if op1 is None:
+            emit("v", [lambda e: e.tensor_scalar(ap(out), ap(a), x1, None, op0)], rd, [reg(out)])
+        else:
+            emit("v", [lambda e: e.tensor_scalar(ap(out), ap(a), x1, x2, op0, op1)], rd, [reg(out)])
+
+    def fill(out, c):
+        emit("v", [lambda e: e.memset(ap(out), c)], [], [reg(out)])
+
+    def act(out, in_, func, bias=0.0, scale=1.0):
+        rd = [reg(x) for x in (in_, bias, scale) if isinstance(x, tuple)]
+        b = ap(bias) if isinstance(bias, tuple) else bias
+        k = ap(scale) if isinstance(scale, tuple) else scale
+        emit("s", [lambda e: e.activation(ap(out), ap(in_), func, bias=b, scale=k)], rd, [reg(out)])
+
+    def vgather(out, win, off, in1, op):
+        emit("v", [lambda e: e.tensor_tensor(ap(out), ap(win).indirect(ap(off)), ap(in1), op)],
+             [reg(win), reg(off), reg(in1)], [reg(out)])
+
+    def gcopy(q, out, win, off):
+        if q == "v":
+            emit("v", [lambda e: e.tensor_copy(ap(out), ap(win).indirect(ap(off)))], [reg(win), reg(off)], [reg(out)])
+        else:
+            emit("s", [lambda e: e.activation(ap(out), ap(win).indirect(ap(off)), AF.Copy)], [reg(win), reg(off)], [reg(out)])
+
+    def mm(out, parts):
+        n = len(parts)
+        calls = []
+        rd = []
+        for i, (l, r) in enumerate(parts):
+            rd += [reg(l), reg(r)]
+            calls.append(lambda e, l=l, r=r, i=i: e.matmul(ap(out), ap(l), ap(r), i == 0, i == n - 1))
+        emit("t", calls, sorted(set(rd)), [reg(out)])
+
+    def wrapped(out, lbuf, rbuf, lo, hi, extra=()):
+        mm(out, [((lbuf, 15 - r, 143 - r), (rbuf, lo + r, hi, 16)) for r in range(16)] + list(extra))
+
+    def dma(q, out_ap, in_ap, reads, writes, sem):
+        return emit(q, [lambda e: e.dma_start(out=out_ap, in_=in_ap)], reads, writes, sem=sem, val=16)
+
+    def iota(buf, lo, hi, pattern, base, cm, flag):
+        if flag:
+            emit("g", [lambda e: e.iota(T[buf][:, lo:hi], pattern, base, cm, allow_small_or_imprecise_dtypes=True)], [], [(buf, lo, hi)])
+        else:
+            emit("g", [lambda e: e.iota(T[buf][:, lo:hi], pattern, base, cm)], [], [(buf, lo, hi)])
+
+    dma("s", T.EFI[:, :], T.ef[:, :], [], [("EFI", 0, 256)], "lde")
+    dma("y", T.WI[:, :], T.wt[:, :], [], [("WI", 0, 1)], "ldw")
+    dma("y", T.XA0[:, 4096:4608], T.zv[:, :], [], [("XA0", 4096, 4608)], "ldz")
+    dma("y", T.D[:, 0:2048], T.dv[:, 0:2048], [], [("D", 0, 2048)], "ldd0")
+    dma("s", T.D[:, 2048:4096], T.dv[:, 2048:4096], [], [("D", 2048, 4096)], "ldd1")
+
+    iota("PI", 0, 1, [[1, 1]], 0, 1, False)
+    iota("XI", 0, 144, [[1, 144]], 0, 0, True)
+    iota("JT", 0, 32, [[128, 32]], 0, 0, False)
+    iota("CTI", 32, 256, [[-32, 7], [-1, 32]], 287, 0, True)
+    iota("CTI", 0, 32, [[-1, 32]], 31, 0, True)
+    I = ("PI", 0, 1)
+    ts(("PJ", 0, 1), I, 112, None, OP.bitwise_and)
+    ts(("PJ", 1, 2), I, 15, None, OP.bitwise_and)
+    ts(("PJ", 2, 3), I, 3, 1, OP.logical_shift_right, OP.bitwise_and)
+    ts(("PJ", 3, 4), I, 7, None, OP.bitwise_and)
+    ts(("PJ", 4, 5), I, 1, None, OP.bitwise_and)
+    ts(("PJ", 5, 6), I, 1, 7, OP.logical_shift_right, OP.bitwise_and)
+    copy(("PF", 0, 6), ("PJ", 0, 6))
+    copy(("PF", 6, 7), I)
+    tt(("PF", 8, 9), ("PF", 0, 1), ("PF", 2, 3), OP.add)
+    ts(("PF", 9, 10), ("PF", 8, 9), 14.0, None, OP.add)
+    for k in range(8):
+        ts(("KM", k, k + 1), ("PF", 3, 4), float(k), None, OP.is_equal)
+    for k in range(8):
+        ts(("Q%d" % k, 0, 144), ("XI", 0, 144), ("PF", 9, 10), ("KM", k, k + 1), OP.is_equal, OP.mult)
+    copy(("EF", 0, 256), ("EFI", 0, 256))
+
+    def split(E, lo, hi, step):
+        a = ("EH", lo, hi) if step == 1 else ("EHL", 2 * lo, 2 * hi, 2)
+        b = ("EL", lo, hi) if step == 1 else ("EHL", 2 * lo + 1, 2 * hi, 2)
+        copy(a, (E, lo, hi))
+        tt(b, (E, lo, hi), a, OP.subtract)
+    split("EF", 0, 256, 1)
+
+    def bring(b, k):
+        mm((b, 32 * k, 32 * k + 32), [(("Q%d" % k, 14 - 2 * h, 142 - 2 * h), (e, h, 256, 8)) for h in range(8) for e in ("EH", "EL")])
+    for k in range(4):
+        bring("bCA", k)
+    ts(("PF", 10, 11), ("PF", 0, 1), 15.0, None, OP.add)
+    ts(("OL", 0, 144), ("XI", 0, 144), ("PF", 10, 11), SCALE, OP.is_equal, OP.mult)
+    copy(("WF", 0, 1), ("WI", 0, 1))
+    ts(("WL", 0, 144), ("XI", 0, 144), ("PF", 10, 11), ("WF", 0, 1), OP.is_equal, OP.mult)
+    ts(("ID", 0, 128), ("XI", 0, 128), ("PF", 6, 7), None, OP.is_equal)
+    ts(("NG", 0, 128), ("XI", 0, 128), ("PF", 6, 7), -1.0, OP.is_equal, OP.mult)
+    ts(("IDF", 0, 128), ("XI", 0, 128), ("PF", 6, 7), None, OP.is_equal)
+    ts(("NGF", 0, 128), ("XI", 0, 128), ("PF", 6, 7), -1.0, OP.is_equal, OP.mult)
+    fill(("BT", 0, 96), -7.5)
+    fill(("BT", 96, 192), 1.0)
+    fill(("BN", 0, 96), -1.0)
+    fill(("BN", 96, 192), -2.0)
+    fill(("ON15", 0, 128), SCALE / 128)
+    fill(("K2", 0, 96), 2048 / SCALE)
+    fill(("K3", 0, 256), -0.5 / SCALE)
+    ts(("BI", 0, 128), ("XI", 0, 128), ("PF", 6, 7), 64 * SCALE, OP.is_equal, OP.mult)
+    fill(("ONS", 0, 128), 2.0 ** -21)
+    ts(("PF", 11, 12), ("PF", 1, 2), 4592.0, None, OP.add)
+    ts(("PF", 12, 13), ("PF", 1, 2), 8.0, None, OP.mult)
+    for j, m in (("J8", 2047), ("J4", 1023)):
+        ts(("JU", 0, 32), ("JT", 0, 32), m, None, OP.bitwise_and)
+        ts((j, 0, 32), ("JU", 0, 32), ("PF", 12, 13), None, OP.add)
+    ts(("PF", 13, 14), ("PF", 4, 5), 8.0, 7.0, OP.mult, OP.add)
+    tt(("PF", 14, 15), ("PF", 13, 14), ("PF", 0, 1), OP.add)
+    for h in range(8):
+        ts(("KM", 8 + h, 9 + h), ("PF", 5, 6), float(h), None, OP.is_equal)
+        ts(("R%d" % h, 0, 144), ("XI", 0, 144), ("PF", 14, 15), ("KM", 8 + h, 9 + h), OP.is_equal, OP.mult)
+
+    def second(EQ, lo, hi):
+        act(("bU0", lo, hi), (EQ, lo, hi), AF.Identity, bias=-6722560.0, scale=2080.0)
+
+    def spread_first(EQ):
+        act(("ER", 0, 32), (EQ, 0, 32), AF.Copy)
+        act(("ER", 32, 64), (EQ, 0, 32), AF.Copy)
+        act(("ER", 64, 128), ("ER", 0, 64), AF.Copy)
+        act(("ER", 128, 224), ("ER", 0, 96), AF.Copy)
+        act(("bU0", 256, 480), ("ER", 0, 224), AF.Copy)
+        act(("bU", 288, 512), ("ER", 0, 224), AF.Identity, bias=-6722560.0, scale=2080.0)
+
+    def round_s(src, lo):
+        n = src[2] - src[1]
+        act(("RX", lo, lo + n), src, AF.Identity, bias=BIG, scale=1.0 + 2.0 ** -22)
+        act(("RR", lo, lo + n), ("RX", lo, lo + n), AF.Identity, bias=-BIG)
+
+    def value_v(src, lo):
+        n = src[2] - src[1]
+        tt(("VF", lo, lo + n), src, ("RR", lo, lo + n), OP.subtract)
+
+    def finish(lo, hi, ni, lst):
+        ts((ni, lo, hi), ("SI", lo, hi), 5, 4095, OP.arith_shift_right, OP.bitwise_and)
+        copy((lst, lo, hi), (ni, lo, hi))
+
+    def hash_many(EQ, k0, k1, ni, lst):
+        products(EQ, k0, k1)
+        names(k0, k1, ni, lst)
+
+    def products(EQ, k0, k1):
+        for k in range(k0, k1):
+            tt(("PP", 32 * k, 32 * k + 32), (EQ, 32 * k, 32 * k + 32), ("VF", 0, 32), OP.mult)
+
+    def names(k0, k1, ni, lst):
+        tt(("SI", 32 * k0, 32 * k1), ("PP", 32 * k0, 32 * k1), ("bU0", 32 * k0, 32 * k1), OP.add)
+        finish(32 * k0, 32 * k1, ni, lst)
+
+    def hash_first():
+        tt(("PP", 32, 256), ("bU0", 256, 480), ("VF", 32, 256), OP.mult)
+        tt(("SI", 32, 256), ("PP", 32, 256), ("bU", 288, 512), OP.add)
+        finish(32, 256, "HI", "LB")
+
+    def uz(XA):
+        wrapped(("bU", 256, 288), "WL", XA, 4096, 4608, [(("ON15", 0, 128), ("K2", 0, 32))])
+
+    uz("XA0")
+    for k in range(4, 8):
+        bring("bCB", k)
+    act(("bCC", 256, 512), ("CTI", 0, 256), AF.Copy, scale=4096.0)
+    for h, b in ((0, "bCA"), (1, "bCB")):
+        act(("EQ0", 128 * h, 128 * h + 128), (b, 128 * h, 128 * h + 128), AF.Identity, bias=1184.0)
+        second("EQ0", 128 * h, 128 * h + 128)
+        if h == 0:
+            round_s(("bU", 256, 288), 0)
+            value_v(("bU", 256, 288), 0)
+        hash_many("EQ0", 4 * h, 4 * h + 4, "NI", "LN")
+    spread_first("EQ0")
+
+    def packs():
+        tt(("PK", 0, 256), ("NI", 0, 256), ("bCC", 256, 512), OP.add)
+    packs()
+
+    ends = []
+    for t in range(RO):
+        last = t == RO - 1
+        XA, XN = "XA%d" % (t % 2), "XA%d" % ((t + 1) % 2)
+        EQ, EN = "EQ%d" % (t % 2), "EQ%d" % ((t + 1) % 2)
+        PKS = "PKS%d" % (t % 2)
+        ZB = (XA, 4096, 4608)
+        DW = ("D", 0, 4096)
+        tasks = {}
+        order = ["a%d" % k for k in AS] + ["c%d" % k for k in CS] + ["b%d" % k for k in BS]
+
+        def add(name, q, pre, fn):
+            tasks[name] = (q, pre, fn)
+
+        def xa(k):
+            b = (k - 1) % 8
+            return (XA, 512 * b, 512 * b + 512)
+
+        def lst(name, k):
+            return (name, 32 * k, 32 * k + 32)
+
+        def blk(name, k):
+            return (name, 512 * k, 512 * k + 512)
+
+        def bank(name):
+            return ("bS%d" % (order.index(name) % 2), 0, 512)
+
+        def ds(name):
+            i = order.index(name) % 4
+            return ("DS", 512 * i, 512 * i + 512)
+
+        def by_scalar(n, pre, L, k, y, G, extra):
+            i = order.index(n)
+            add("ga" + n, "s", pre, lambda: gcopy("s", ds(n), DW, lst(L, k)))
+            add("st" + n, "t", ["ga" + n] + (["sg" + order[i - 2]] if i >= 2 else []),
+                lambda: mm(bank(n), [(("ID", 0, 128), ds(n)), (("NG", 0, 128), y)]))
+            add("sg" + n, "s", ["st" + n] + extra, lambda: act(blk(G, k), bank(n), AF.Sign, bias=-0.5))
+        for k in range(8):
+            if k in AS:
+                n = "a%d" % k
+                add("abs%d" % k, "s", ["st" + n], lambda n=n, k=k: act(xa(k), bank(n), AF.Abs))
+                by_scalar(n, [], "LN", k, ZB, "GA", ["abs%d" % k])
+            else:
+                add("gaa%d" % k, "v", [], lambda k=k: vgather(blk("XB", k), DW, lst("LN", k), ZB, OP.subtract))
+                add("abs%d" % k, "s", ["gaa%d" % k], lambda k=k: act(xa(k), blk("XB", k), AF.Abs))
+                add("sga%d" % k, "v", ["gaa%d" % k], lambda k=k: ts(blk("GA", k), blk("XB", k), 0.0, None, OP.is_gt))
+            for w, S_, G, L, pre in (("c", CS, "GC", "LC", "HC"), ("b", BS, "GB", "LB", "HB")):
+                if k == 0:
+                    continue
+                n = w + str(k)
+                y = xa(0) if w == "c" else xa(k)
+                if k in S_:
+                    by_scalar(n, [pre], L, k, y, G, [])
+                elif w == "b" and k in CFG["BM"]:
+                    add("sg" + n, "v", [pre], lambda k=k: vgather(("GB", 512 * k, 512 * k + 1024), DW, ("LB", 32 * k, 32 * k + 64),
+                                                                  (XA, 512 * k - 512, 512 * k + 512), OP.is_gt))
+                elif w == "b" and k - 1 in CFG["BM"]:
+                    add("sg" + n, "v", ["sgb%d" % (k - 1)], lambda: None)
+                else:
+                    add("sg" + n, "v", [pre], lambda k=k, G=G, L=L, y=y: vgather(blk(G, k), DW, lst(L, k), y, OP.is_gt))
+
+        def count(w, ks):
+            G, B, S_ = {"a": ("GA", "bCA", AS), "b": ("GB", "bCB", BS), "c": ("GC", "bCC", CS)}[w]
+            kinds = [k in S_ for k in ks]
+            k0, n = ks[0], len(ks)
+            if kinds == sorted(kinds):
+                b0 = 96 - 32 * kinds.count(False)
+                o = 32 * k0
+                if w == "b" and k0 >= 6:
+                    B, o = "bM", 32 * k0 + 128
+                extra = [(("ON15", 0, 128), ("BT", b0, b0 + 32 * n))]
+                if w == "c":
+                    extra.append((("BI", 0, 128), ("HP", 32 * k0, 32 * (k0 + n))))
+                wrapped((B, o, o + 32 * n), "OL", G, 512 * k0, 512 * (k0 + n), extra)
+            else:
+                for k in ks:
+                    count(w, [k])
+        for w, c in (("a", "NA"), ("c", "NC"), ("b", "NB")):
+            for grp in CFG[c].split():
+                ks = [int(x) for x in grp]
+                add("n%s%d" % (w, ks[0]), "t", ["sg%s%d" % (w, k) for k in ks] + (["H0"] if w == "c" else []), lambda w=w, ks=ks: count(w, ks))
+        counts = ["n%s%s" % (w, grp[0]) for w, c in (("a", "NA"), ("c", "NC")) for grp in CFG[c].split()]
+        late = "nb" + CFG["NB"].split()[-1][0]
+        add("U0", "t", ["abs0"], lambda: wrapped(("bM", 288, 320), "WL", XA, 3584, 4096, [(("ON15", 0, 128), ("K2", 0, 32))]))
+        add("RC", "s", ["U0"], lambda: round_s(("bM", 288, 320), 0))
+        UG = [[int(x) for x in grp] for grp in CFG["NU"].split()]
+        for ks in UG:
+            add("U%d" % ks[0], "t", ["abs%d" % k for k in ks], lambda ks=ks: wrapped(
+                ("bU", 32 * ks[0], 32 * ks[-1] + 32), "WL", XA, 512 * (ks[0] - 1), 512 * ks[-1],
+                [(("ON15", 0, 128), ("K2", 0, 32 * len(ks)))]))
+
+        def do_par():
+            emit("s", [lambda e: e.activation(T.AJ[:, 0:32], T.bM[:, 256:288], AF.Copy, accum_out=T.AR[:, 0:1])],
+                 [("bM", 256, 288)], [("AJ", 0, 32), ("AR", 0, 1)])
+            act(("AR", 1, 2), ("AR", 0, 1), AF.Identity, bias=MID, scale=0.5)
+            act(("AR", 2, 3), ("AR", 1, 2), AF.Identity, bias=2 * MID, scale=-2.0)
+            act(("AR", 3, 4), ("AR", 2, 3), AF.Abs, bias=("AR", 0, 1))
+            for lo, b in ((0, -7.5), (96, 1.0)):
+                act(("BT", lo, lo + 96), ("BN", lo, lo + 96), AF.Identity, bias=b, scale=("AR", 3, 4))
+
+        def do_hc():
+            value_v(("bM", 288, 320), 0)
+            hash_many(EQ, 1, 8, "HI", "LC")
+        add("HC", "v", ["RC"], do_hc)
+
+        def do_rb():
+            round_s(("bU", 32, 256), 32)
+        add("RB", "s", ["U%d" % ks[0] for ks in UG], do_rb)
+
+        def do_hb():
+            value_v(("bU", 32, 256), 32)
+            hash_first()
+        add("HB", "v", ["RB", "HC"], do_hb)
+
+        def do_h0():
+            for k in range(1, 8):
+                act(("H0", 32 * k, 32 * k + 32), ("bCA", 0, 32), AF.Copy, scale=-1.0)
+            act(("HP", 32, 256), ("H0", 32, 256), AF.Relu, scale=1.0 / SCALE)
+        add("H0", "s", ["na0"], do_h0)
+
+        def do_pq():
+            ts(("A0T", 0, 32), ("bCA", 0, 32), 0.0, 131072.0, OP.is_gt, OP.mult)
+            tt(("T1", 32, 256), ("bCC", 32, 256), ("PK", 32, 256), OP.min)
+            tt(("KEY", 0, 32), ("PK", 0, 32), ("A0T", 0, 32), OP.add)
+            tt(("PQ", 32, 256), ("bCA", 32, 256), ("T1", 32, 256), OP.min)
+        add("PQ", "v", ["H0"] + counts, do_pq)
+
+        def key(lo, hi):
+            cb = ("bCB", lo, hi) if lo < 192 else ("bM", lo + 128, hi + 128)
+            tt(("bCA", 256 + lo, 256 + hi), cb, ("H0", lo, hi), OP.mult)
+            tt(("KEY", lo, hi), ("PQ", lo, hi), ("bCA", 256 + lo, 256 + hi), OP.min)
+
+        def do_key1():
+            key(32, 192)
+            tt(("TR", 0, 96), ("KEY", 0, 96), ("KEY", 96, 192), OP.max)
+            tt(("TR", 96, 128), ("TR", 0, 32), ("TR", 32, 64), OP.max)
+            tt(("TR", 128, 160), ("TR", 96, 128), ("TR", 64, 96), OP.max)
+        add("KEY1", "v", ["PQ"] + ["nb" + grp[0] for grp in CFG["NB"].split()[:-1]], do_key1)
+
+        def do_tail():
+            key(192, 256)
+            tt(("TR", 160, 192), ("KEY", 192, 224), ("KEY", 224, 256), OP.max)
+            tt((PKS, 0, 32), ("TR", 128, 160), ("TR", 160, 192), OP.max)
+            ts(("TS", 0, 32), (PKS, 0, 32), 12, None, OP.arith_shift_right)
+            ts(("LS", 0, 32), ("TS", 0, 32), -16.0, ("PF", 11, 12), OP.mult, OP.add)
+        add("TAIL", "v", ["KEY1", late], do_tail)
+
+        lists = {"v": CFG["V"].split(), "s": CFG["S"].split(), "t": CFG["T"].split()}
+        assert sorted(lists["v"] + lists["s"] + lists["t"]) == sorted(tasks), set(tasks) ^ set(lists["v"] + lists["s"] + lists["t"])
+        done = set()
+        pos = {"v": 0, "s": 0, "t": 0}
+        while len(done) < len(tasks):
+            moved = False
+            for q in ("v", "s", "t"):
+                while pos[q] < len(lists[q]) and all(p in done for p in tasks[lists[q][pos[q]]][1]):
+                    nm = lists[q][pos[q]]
+                    assert tasks[nm][0] == q
+                    tasks[nm][2]()
+                    done.add(nm)
+                    pos[q] += 1
+                    moved = True
+            assert moved, [lists[q][pos[q]:pos[q] + 1] for q in lists]
+
+        mm(("bCB", 256, 480), [(("IDF", 0, 128), (EQ, 32, 256)), (("NGF", 0, 128), (EQ, 0, 224))])
+
+        dst = T.cores[(rank + 1 + t % (N - 1)) % N]
+        rid, pid = topo.addr(dst)[0], topo.addr(dst)[1]
+        mask = topo.mask(core, dst)
+        ne = len(topo.engines(core, dst))
+
+        def send(out, in_, rsem, lsem):
+            return emit("g", [lambda e: e.remote_dma(ap(out), ap(in_), T.sem[rsem], T.sem[lsem], pid, rid, mask)],
+                        [reg(in_)], [], sem=lsem, val=ne, remote=True)
+
+        def landed(buf, lo, hi, rsem):
+            note("g", buf, lo, hi, True, (rsem, ne, {rsem: ne}))
+        LP, LZ = "LP%d" % t, "LZ%d" % t
+        ends.append(send((LP, 0, 32), (PKS, 0, 32), "an%d" % t, "ln%d" % t))
+        gcopy("v", (XN, 4096, 4352), (XA, 0, 4608), ("LS", 0, 16))
+        gcopy("s", (XN, 4352, 4608), (XA, 0, 4608), ("LS", 16, 32))
+        ends.append(send((LZ, 0, 256), (XN, 4096, 4352), "az%d" % t, "lz%d" % t))
+        ends.append(send((LZ, 256, 512), (XN, 4352, 4608), "ay%d" % t, "ly%d" % t))
+        landed(LP, 0, 32, "an%d" % t)
+        landed(LZ, 0, 256, "az%d" % t)
+        landed(LZ, 256, 512, "ay%d" % t)
+
+        ts(("S0", 0, 32), (PKS, 0, 32), 262144.0, 2097152.0, OP.is_lt, OP.mult)
+        tt(("P2", 0, 32), (PKS, 0, 32), ("S0", 0, 32), OP.add)
+        if not last:
+            mm(("bM", 256, 288), [(("ONS", 0, 128), ("S0", 0, 32))])
+        for k in range(7):
+            ts(("MK", 32 * k, 32 * k + 32), ("P2", 0, 32), float((9 - k) * 131072), None, OP.is_ge)
+        if not last:
+            uz(XN)
+            round_s(("bU", 256, 288), 0)
+        tt(("bCB", 256, 480), ("bCB", 256, 480), ("MK", 0, 224), OP.mult)
+        tt((EN, 0, 224), ("bCB", 256, 480), (EQ, 0, 224), OP.add)
+        if not last:
+            second(EN, 0, 224)
+            value_v(("bU", 256, 288), 0)
+            do_par()
+            products(EN, 0, 7)
+        else:
+            split(EN, 0, 224, 2)
+        J, nq = ("J4", 4) if last else ("J8", 2)
+        ts(("NM", 0, 32), (LP, 0, 32), 4095, None, OP.bitwise_and)
+        ts(("CI", 0, 32), (LP, 0, 32), 7, None, OP.bitwise_and)
+        ts((EN, 224, 256), ("NM", 0, 32), 1184.0, None, OP.add)
+        tt(("CJ", 0, 32), ("CI", 0, 32), (J, 0, 32), OP.add)
+        copy(("LD", 0, 32), ("CJ", 0, 32))
+        if not last:
+            second(EN, 224, 256)
+        WQ, SQ, CQ = 4096 // nq, 512 // nq, 32 // nq
+        parts = [((SQ * q, SQ * q + SQ), (WQ * q, WQ * q + WQ), (CQ * q, CQ * q + CQ)) for q in range(nq)]
+        for q, (R, W, C) in enumerate(parts):
+            gcopy("s", ("DC",) + R, ("D",) + W, ("LD",) + C)
+        if not last:
+            products(EN, 7, 8)
+            names(0, 8, "NI", "LN")
+            packs()
+        else:
+            split(EN, 224, 256, 2)
+        for q, (R, W, C) in enumerate(parts):
+            b = ("bS0", "bS1", "bU0", "bU")[q]
+            extra = [(("ON15", 0, 128), ("K3", 0, SQ))] if q % 2 else []
+            mm((b, 0, SQ), extra + [(("ID", 0, 128), ("DC",) + R), (("ID", 0, 128), (LZ,) + R)])
+            if q % 2:
+                act(("FX", 0, SQ), (b, 0, SQ), AF.Identity, bias=MID, scale=0.5)
+                act(("FB", (q // 2) * SQ, (q // 2) * SQ + SQ), ("FX", 0, SQ), AF.Identity, bias=-MID)
+        for q, (R, W, C) in enumerate(parts):
+            b = ("bS0", "bS1", "bU0", "bU")[q]
+            F = ("FB", (q // 2) * SQ, (q // 2) * SQ + SQ) if q % 2 else ("FL",) + R
+            if q % 2 == 0:
+                ts(F, (b, 0, SQ), 0.5, -0.25, OP.mult, OP.add)
+            emit("v", [lambda e, F=F, W=W, C=C: e.tensor_copy(ap(("D",) + W).indirect(ap(("LD",) + C)), ap(F))],
+                 [F, ("LD",) + C], [("D",) + W])
+            if last:
+                ends.append(dma("y", T.yd[:, W[0]:W[1]], ap(("D",) + W), [("D",) + W], [], "sd%d" % q))
+        if not last:
+            spread_first(EN)
+        else:
+            for h in range(8):
+                b, o = ("bM", "bCB")[h // 4], 64 * (h % 4)
+                mm((b, o, o + 64), [(("R%d" % h, 7 - k, 135 - k), ("EHL", 64 * k, 64 * k + 64)) for k in range(8)])
+            for i, b in enumerate(("bM", "bCB")):
+                act(("PK", 128 * i, 128 * i + 128), (b, 0, 256, 2), AF.Identity, bias=-1184.0)
+                for h in range(4):
+                    tt(("YE", 4 * i + h, 256, 8), ("PK", 128 * i + 32 * h, 128 * i + 32 * h + 32), (b, 64 * h + 1, 64 * h + 64, 2), OP.add)
+            ends.append(dma("s", T.yz[:, :], T[XN][:, 4096:4608], [(XN, 4096, 4608)], [], "sz"))
+            ends.append(dma("s", T.ye[:, :], T.YE[:, :], [("YE", 0, 256)], [], "se"))
+    settle("g", ends)
+    settle("g", [(qsem[q], cnt[q], {}) for q in "vstg"])

@@ -5,44 +5,47 @@ AF = ActivationFunctionType
 RO = 4
 BIG = 1.5 * 2.0 ** 35
 MID = 1.5 * 2.0 ** 23
-SCALE = 4194304.0
-B2, B4, I4, U2 = "bfloat16", "float32", "int32", "uint16"
+SC = 1.25 * 2.0 ** 21
+B2, B4, H2, I4, U2 = "bfloat16", "float32", "float16", "int32", "uint16"
 SCRATCH = {}
 for _n, _w, _d in (("D", 4096, B2), ("XA0", 4608, B2), ("XA1", 4608, B2), ("XB", 4096, B2), ("GA", 4096, B2), ("GB", 4096, B2),
-                   ("GC", 4096, B2), ("DS", 2048, B2), ("DC", 512, B2), ("FL", 512, I4), ("LN", 256, U2), ("LB", 256, U2),
-                   ("LC", 256, U2), ("LS", 32, U2), ("LD", 32, U2), ("EQ0", 256, B4), ("EQ1", 256, B4), ("VF", 256, B4), ("PP", 256, B4), ("SI", 256, I4), ("HI", 256, I4), ("NI", 256, I4),
-                   ("H0", 256, B4), ("T1", 256, B4), ("PQ", 256, B4), ("PK", 256, B4), ("KEY", 256, B4), ("TR", 256, B4),
-                   ("A0T", 32, B4), ("PKS0", 32, I4), ("PKS1", 32, I4), ("TS", 32, I4), ("S0", 32, B2), ("P2", 32, B4),
-                   ("ER", 256, B4), ("MK", 256, B4), ("AR", 8, B4), ("AJ", 32, B4), ("NM", 32, I4),
-                   ("CI", 32, I4), ("CJ", 32, I4), ("BT", 192, B2), ("BN", 192, B2), ("J8", 32, I4), ("JT", 32, I4),
-                   ("ID", 128, B2), ("NG", 128, B2), ("IDF", 128, B4), ("NGF", 128, B4), ("ON15", 128, B2), ("ONS", 128, B2),
-                   ("OL", 144, B2), ("WL", 144, B2), ("XI", 144, B4), ("CTI", 256, B4), ("PI", 8, I4), ("PJ", 16, I4),
-                   ("PF", 32, B4), ("KM", 16, B4), ("WI", 1, I4), ("WF", 1, B4), ("EFI", 256, I4), ("EF", 256, B4),
-                   ("EH", 256, B2), ("EL", 256, B2), ("EHL", 512, B2), ("J4", 32, I4), ("JU", 32, I4), ("K2", 96, B2),
-                   ("K3", 256, B2), ("RX", 256, B4), ("RR", 256, B4), ("HP", 256, B2), ("BI", 128, B2), ("FX", 256, B4),
-                   ("FB", 256, B2), ("YE", 256, B4)):
+                   ("GC", 4096, B2), ("DS", 4096, B2), ("DT", 2048, B2), ("DC", 512, B2), ("FL", 512, I4), ("LN", 256, U2), ("LB", 256, U2),
+                   ("LC", 256, U2), ("LS", 32, U2), ("LD", 32, U2), ("BL", 16, U2), ("EQ0", 256, B4), ("EQ1", 256, B4), ("VF", 256, B4),
+                   ("PP", 256, B4), ("SI", 256, I4), ("HI", 256, I4), ("NI", 256, I4), ("NP", 256, B4), ("NT", 256, B4),
+                   ("WK", 256, B4), ("TR", 256, B4), ("SN", 32, B2), ("PKS0", 32, I4), ("PKS1", 32, I4), ("TS", 32, I4),
+                   ("S0", 32, B2), ("P2", 32, B4), ("ER", 256, B4), ("MK", 256, B4), ("AR", 8, B4), ("AJ", 32, B4), ("NM", 32, I4),
+                   ("CI", 32, I4), ("CJ", 32, I4), ("BT", 960, B2), ("PB", 128, B2), ("J8", 32, I4), ("JT", 32, I4), ("BJ", 16, I4),
+                   ("ID", 128, B2), ("NG", 128, B2), ("IDF", 128, B4), ("NGF", 128, B4), ("ON", 128, B2), ("IC", 128, B2),
+                   ("IB", 128, B2), ("IW", 128, B2), ("OL", 144, B2), ("OH", 144, B2), ("WL", 144, B2), ("XI", 144, B2),
+                   ("CTI", 256, B4), ("THR", 224, B4), ("PI", 8, I4), ("PJ", 16, I4), ("PF", 32, B4), ("KM", 16, B4),
+                   ("WI", 1, I4), ("WF", 1, B4), ("EFI", 256, I4), ("EH", 256, H2), ("J4", 32, I4), ("JU", 32, I4), ("K2", 160, B2),
+                   ("K3", 256, B2), ("RX", 256, B4), ("RR", 256, B2), ("FX", 512, B4), ("FB", 512, B2), ("YE", 256, B4)):
     SCRATCH[_n] = ("sbuf", [128, _w], _d)
-for _n in ("bU0", "bU", "bCA", "bCB", "bCC", "bS0", "bS1", "bM"):
+for _n in ("bK", "bU", "bA", "bB", "bC", "bS0", "bS1", "bM"):
     SCRATCH[_n] = ("psum", [128, 512], B4)
 for _k in range(8):
-    SCRATCH["Q%d" % _k] = ("sbuf", [128, 144], B2)
-    SCRATCH["R%d" % _k] = ("sbuf", [128, 144], B2)
+    SCRATCH["Q%d" % _k] = ("sbuf", [128, 144], H2)
+    SCRATCH["R%d" % _k] = ("sbuf", [128, 144], H2)
 for _t in range(RO):
     SCRATCH["LP%d" % _t] = ("sbuf", [128, 32], I4)
     SCRATCH["LZ%d" % _t] = ("sbuf", [128, 512], B2)
 SEMAPHORES = (["qv", "qs", "qt", "qg"] + ["ldz", "lde", "ldw", "ldd0", "ldd1", "sd0", "sd1", "sd2", "sd3", "se", "sz"]
               + ["%s%d" % (n, t) for t in range(RO) for n in ("an", "az", "ay", "ln", "lz", "ly")])
+TAG = [""]
+REC = []
 
 CFG = {
-    "AS": (7, 1, 5),
-    "CS": (4, 5),
-    "BS": (3, 5),
-    "NA": "01 23 45 67", "NC": "123 45 67", "NB": "123 45 67",
-    "NU": "12 34 56 7",
-    "BM": (1, 6),
-    "V": "gaa0 gaa6 gaa3 gaa2 gaa4 sga2 sga6 sga0 sga3 HC sga4 sgc3 sgc6 sgc2 sgc1 sgc7 HB sgb1 sgb2 sgb4 PQ sgb6 sgb7 KEY1 TAIL",
-    "S": "gaa7 gaa1 abs7 abs0 sga7 gaa5 abs2 RC abs4 abs1 sga1 abs3 abs6 gac4 abs5 H0 RB sgc4 sga5 gac5 gab3 sgc5 gab5 sgb3 sgb5",
-    "T": "sta7 sta1 U7 U0 na6 na2 U1 sta5 na0 U3 stc4 U5 nc1 nc6 na4 stc5 stb3 nc4 stb5 nb1 nb4 nb6",
+    "GS": "a3 a4 a5 a6 a7 c5 c6",
+    "GV": "a0 a1 a2 c1 c2 c3 c4 c7 b123 b45 b67",
+    "SV": "012",
+    "NA": "012 345 67", "NC": "1234 56 7", "NB": "123 45 67",
+    "HB": "123 45,67",
+    "EARLY": 5, "CE": 6,
+    "ORDER": "PT E7 ga0 SP ga3 st3 S7 ga2 abs0 ga1 sa3 abs3 DIFF abs1 abs2 U0 RC U1 H7 sa0 ga5 RB1 ga4 pack ga6 na0 HC st5 sa5 st4 "
+             "sa4 na3 HB1 gc7 ga7 gc2 gc1 abs4 abs5 SN st6 abs6 gb1 st7 abs7 U4 U6 gc4 nb1 gc3 sa6 RB4 sa7 HB4 gc5 na6 gc6 W0 NT "
+             "nc1 stc6 stc5 sc6 gb4 nb4 gb6 sc5 nc5 NC nb6 nc7 Y1 EARLY Y6 LATE LAST TX P2 Z0 Z1 UZ MK SH RZ SE AR HN DC0 DC1 "
+             "UP0 SC0 PA UP1 SC1",
+    "STATE": "vs", "ROUND": "ss", "LROUND": "vsvs", "RRPE": 0,
 }
 
 
@@ -51,7 +54,6 @@ def rank_program(g, core, T, topo):
     if rank is None:
         return
     N = len(T.cores)
-    AS, CS, BS = CFG["AS"], CFG["CS"], CFG["BS"]
     eng = {"v": g.vector, "s": g.scalar, "t": g.tensor, "g": g, "y": g.sync}
     qsem = {"v": "qv", "s": "qs", "t": "qt", "g": "qg"}
     cnt = {"v": 0, "s": 0, "t": 0, "g": 0}
@@ -59,9 +61,11 @@ def rank_program(g, core, T, topo):
     log = {}
     BANKS = [b for b in SCRATCH if SCRATCH[b][0] == "psum"]
 
-    def need(q, buf, lo, hi, wr):
+    def need(q, buf, lo, hi, wr, acc=False):
         out = []
         for e in log.get(buf, []):
+            if acc and e[3] == q:
+                continue
             if e[0] < hi and lo < e[1] and (wr or e[2]):
                 out.append(e[4])
             elif buf in BANKS and e[3] != q:
@@ -92,16 +96,18 @@ def rank_program(g, core, T, topo):
                 known[q][s] = max(known[q].get(s, 0), v)
             known[q][op[0]] = max(known[q].get(op[0], 0), op[1])
 
-    def emit(q, calls, reads, writes, sem=None, val=None, remote=False):
+    def emit(q, calls, reads, writes, sem=None, val=None, remote=False, acc=False):
         ops = []
         for b, lo, hi in reads:
             ops += need(q, b, lo, hi, False)
         for b, lo, hi in writes:
-            ops += need(q, b, lo, hi, True)
+            ops += need(q, b, lo, hi, True, acc)
         settle(q, ops)
         ins = None
+        REC.append((TAG[0], q, reads, writes, acc, remote, []))
         for c in calls:
             ins = c(eng[q])
+            REC[-1][-1].append(ins)
         snap = dict(known[q])
         if sem is None:
             cnt[q] += 1
@@ -140,8 +146,8 @@ def rank_program(g, core, T, topo):
         else:
             emit("v", [lambda e: e.tensor_scalar(ap(out), ap(a), x1, x2, op0, op1)], rd, [reg(out)])
 
-    def fill(out, c):
-        emit("v", [lambda e: e.memset(ap(out), c)], [], [reg(out)])
+    def fill(out, c, p0=0, p1=128):
+        emit("v", [lambda e: e.memset(T[out[0]][p0:p1, out[1]:out[2]], c)], [], [reg(out)], acc=p0 > 0)
 
     def act(out, in_, func, bias=0.0, scale=1.0):
         rd = [reg(x) for x in (in_, bias, scale) if isinstance(x, tuple)]
@@ -159,17 +165,18 @@ def rank_program(g, core, T, topo):
         else:
             emit("s", [lambda e: e.activation(ap(out), ap(win).indirect(ap(off)), AF.Copy)], [reg(win), reg(off)], [reg(out)])
 
-    def mm(out, parts):
+    def mm(out, parts, start=True, stop=True):
         n = len(parts)
         calls = []
         rd = []
-        for i, (l, r) in enumerate(parts):
-            rd += [reg(l), reg(r)]
-            calls.append(lambda e, l=l, r=r, i=i: e.matmul(ap(out), ap(l), ap(r), i == 0, i == n - 1))
-        emit("t", calls, sorted(set(rd)), [reg(out)])
+        for i, p in enumerate(parts):
+            rd += [reg(p[0]), reg(p[1])]
+            o = p[2] if len(p) > 2 else out
+            calls.append(lambda e, p=p, o=o, i=i: e.matmul(ap(o), ap(p[0]), ap(p[1]), start and i == 0, stop and i == n - 1))
+        emit("t", calls, sorted(set(rd)), [reg(out)], acc=not start)
 
-    def wrapped(out, lbuf, rbuf, lo, hi, extra=()):
-        mm(out, [((lbuf, 15 - r, 143 - r), (rbuf, lo + r, hi, 16)) for r in range(16)] + list(extra))
+    def wrap(lbuf, rbuf, lo, hi):
+        return [((lbuf, 15 - r, 143 - r), (rbuf, lo + r, hi, 16)) for r in range(16)]
 
     def dma(q, out_ap, in_ap, reads, writes, sem):
         return emit(q, [lambda e: e.dma_start(out=out_ap, in_=in_ap)], reads, writes, sem=sem, val=16)
@@ -180,83 +187,62 @@ def rank_program(g, core, T, topo):
         else:
             emit("g", [lambda e: e.iota(T[buf][:, lo:hi], pattern, base, cm)], [], [(buf, lo, hi)])
 
-    dma("s", T.EFI[:, :], T.ef[:, :], [], [("EFI", 0, 256)], "lde")
-    dma("y", T.WI[:, :], T.wt[:, :], [], [("WI", 0, 1)], "ldw")
+    def M(b):
+        return (b, 0, 128)
+
+    TAG[0] = "setup"
+    dma("y", T.EFI[:, :], T.ef[:, :], [], [("EFI", 0, 256)], "lde")
+    dma("s", T.WI[:, :], T.wt[:, :], [], [("WI", 0, 1)], "ldw")
     dma("y", T.XA0[:, 4096:4608], T.zv[:, :], [], [("XA0", 4096, 4608)], "ldz")
-    dma("y", T.D[:, 0:2048], T.dv[:, 0:2048], [], [("D", 0, 2048)], "ldd0")
     dma("s", T.D[:, 2048:4096], T.dv[:, 2048:4096], [], [("D", 2048, 4096)], "ldd1")
+    dma("y", T.D[:, 0:2048], T.dv[:, 0:2048], [], [("D", 0, 2048)], "ldd0")
 
     iota("PI", 0, 1, [[1, 1]], 0, 1, False)
     iota("XI", 0, 144, [[1, 144]], 0, 0, True)
+    iota("BJ", 0, 16, [[0, 8], [16, 2]], 0, 0, False)
+    iota("CTI", 32, 256, [[1, 224]], 2592, 0, True)
+    iota("CTI", 0, 32, [[1, 32]], 2832, 0, True)
     iota("JT", 0, 32, [[128, 32]], 0, 0, False)
-    iota("CTI", 32, 256, [[-32, 7], [-1, 32]], 287, 0, True)
-    iota("CTI", 0, 32, [[-1, 32]], 31, 0, True)
+    iota("THR", 0, 224, [[32, 7], [0, 32]], 2592, 0, True)
     I = ("PI", 0, 1)
+    XI, XJ = ("XI", 0, 144), ("XI", 0, 128)
     ts(("PJ", 0, 1), I, 112, None, OP.bitwise_and)
-    ts(("PJ", 1, 2), I, 15, None, OP.bitwise_and)
     ts(("PJ", 2, 3), I, 3, 1, OP.logical_shift_right, OP.bitwise_and)
     ts(("PJ", 3, 4), I, 7, None, OP.bitwise_and)
+    ts(("PJ", 1, 2), I, 15, None, OP.bitwise_and)
     ts(("PJ", 4, 5), I, 1, None, OP.bitwise_and)
     ts(("PJ", 5, 6), I, 1, 7, OP.logical_shift_right, OP.bitwise_and)
-    copy(("PF", 0, 6), ("PJ", 0, 6))
     copy(("PF", 6, 7), I)
-    tt(("PF", 8, 9), ("PF", 0, 1), ("PF", 2, 3), OP.add)
-    ts(("PF", 9, 10), ("PF", 8, 9), 14.0, None, OP.add)
+    copy(("PF", 0, 6), ("PJ", 0, 6))
+    fill(M("ON"), 1.0)
+    ts(("PF", 9, 10), ("PF", 0, 1), ("PF", 2, 3), 14.0, OP.add, OP.add)
+    ts(("KM", 0, 8), ("XI", 0, 8), ("PF", 3, 4), None, OP.is_equal)
+    ts(("PF", 10, 11), ("PF", 0, 1), 15.0, None, OP.add)
+    fill(("K2", 0, 160), 16.0)
     for k in range(8):
-        ts(("KM", k, k + 1), ("PF", 3, 4), float(k), None, OP.is_equal)
-    for k in range(8):
-        ts(("Q%d" % k, 0, 144), ("XI", 0, 144), ("PF", 9, 10), ("KM", k, k + 1), OP.is_equal, OP.mult)
-    copy(("EF", 0, 256), ("EFI", 0, 256))
-
-    def split(E, lo, hi, step):
-        a = ("EH", lo, hi) if step == 1 else ("EHL", 2 * lo, 2 * hi, 2)
-        b = ("EL", lo, hi) if step == 1 else ("EHL", 2 * lo + 1, 2 * hi, 2)
-        copy(a, (E, lo, hi))
-        tt(b, (E, lo, hi), a, OP.subtract)
-    split("EF", 0, 256, 1)
+        ts(("Q%d" % k, 0, 144), XI, ("PF", 9, 10), ("KM", k, k + 1), OP.is_equal, OP.mult)
+    ts(("EH", 0, 256), ("EFI", 0, 256), -2048.0, None, OP.add)
+    copy(("WF", 0, 1), ("WI", 0, 1))
+    ts(("BL", 0, 16), ("BJ", 0, 16), ("PF", 1, 2), None, OP.add)
+    ts(("WL", 0, 144), XI, ("PF", 10, 11), ("WF", 0, 1), OP.is_equal, OP.mult)
 
     def bring(b, k):
-        mm((b, 32 * k, 32 * k + 32), [(("Q%d" % k, 14 - 2 * h, 142 - 2 * h), (e, h, 256, 8)) for h in range(8) for e in ("EH", "EL")])
-    for k in range(4):
-        bring("bCA", k)
-    ts(("PF", 10, 11), ("PF", 0, 1), 15.0, None, OP.add)
-    ts(("OL", 0, 144), ("XI", 0, 144), ("PF", 10, 11), SCALE, OP.is_equal, OP.mult)
-    copy(("WF", 0, 1), ("WI", 0, 1))
-    ts(("WL", 0, 144), ("XI", 0, 144), ("PF", 10, 11), ("WF", 0, 1), OP.is_equal, OP.mult)
-    ts(("ID", 0, 128), ("XI", 0, 128), ("PF", 6, 7), None, OP.is_equal)
-    ts(("NG", 0, 128), ("XI", 0, 128), ("PF", 6, 7), -1.0, OP.is_equal, OP.mult)
-    ts(("IDF", 0, 128), ("XI", 0, 128), ("PF", 6, 7), None, OP.is_equal)
-    ts(("NGF", 0, 128), ("XI", 0, 128), ("PF", 6, 7), -1.0, OP.is_equal, OP.mult)
-    fill(("BT", 0, 96), -7.5)
-    fill(("BT", 96, 192), 1.0)
-    fill(("BN", 0, 96), -1.0)
-    fill(("BN", 96, 192), -2.0)
-    fill(("ON15", 0, 128), SCALE / 128)
-    fill(("K2", 0, 96), 2048 / SCALE)
-    fill(("K3", 0, 256), -0.5 / SCALE)
-    ts(("BI", 0, 128), ("XI", 0, 128), ("PF", 6, 7), 64 * SCALE, OP.is_equal, OP.mult)
-    fill(("ONS", 0, 128), 2.0 ** -21)
-    ts(("PF", 11, 12), ("PF", 1, 2), 4592.0, None, OP.add)
-    ts(("PF", 12, 13), ("PF", 1, 2), 8.0, None, OP.mult)
-    for j, m in (("J8", 2047), ("J4", 1023)):
-        ts(("JU", 0, 32), ("JT", 0, 32), m, None, OP.bitwise_and)
-        ts((j, 0, 32), ("JU", 0, 32), ("PF", 12, 13), None, OP.add)
-    ts(("PF", 13, 14), ("PF", 4, 5), 8.0, 7.0, OP.mult, OP.add)
-    tt(("PF", 14, 15), ("PF", 13, 14), ("PF", 0, 1), OP.add)
-    for h in range(8):
-        ts(("KM", 8 + h, 9 + h), ("PF", 5, 6), float(h), None, OP.is_equal)
-        ts(("R%d" % h, 0, 144), ("XI", 0, 144), ("PF", 14, 15), ("KM", 8 + h, 9 + h), OP.is_equal, OP.mult)
+        mm((b, 32 * k, 32 * k + 32), [(("Q%d" % k, 14 - 2 * h, 142 - 2 * h), ("EH", h, 256, 8)) for h in range(8)])
 
-    def second(EQ, lo, hi):
-        act(("bU0", lo, hi), (EQ, lo, hi), AF.Identity, bias=-6722560.0, scale=2080.0)
+    def usum(out, XA, lo):
+        mm(out, [(M("ON"), ("K2", 0, 32))] + wrap("WL", XA, lo, lo + 512))
+    for k in range(8):
+        if k == 2:
+            usum(("bU", 256, 288), "XA0", 4096)
+        bring("bA" if k < 4 else "bB", k)
+
+    def second(out, E):
+        act(out, E, AF.Identity, bias=-6722560.0, scale=2080.0)
 
     def spread_first(EQ):
-        act(("ER", 0, 32), (EQ, 0, 32), AF.Copy)
-        act(("ER", 32, 64), (EQ, 0, 32), AF.Copy)
-        act(("ER", 64, 128), ("ER", 0, 64), AF.Copy)
-        act(("ER", 128, 224), ("ER", 0, 96), AF.Copy)
-        act(("bU0", 256, 480), ("ER", 0, 224), AF.Copy)
-        act(("bU", 288, 512), ("ER", 0, 224), AF.Identity, bias=-6722560.0, scale=2080.0)
+        n = 32 * max(len(p.replace(",", "")) for p in CFG["HB"].split())
+        gcopy("s", ("ER", 0, n), (EQ, 0, 32), ("BL", 0, n // 16))
+        second(("bK", 256, 256 + n), ("ER", 0, n))
 
     def round_s(src, lo):
         n = src[2] - src[1]
@@ -267,46 +253,59 @@ def rank_program(g, core, T, topo):
         n = src[2] - src[1]
         tt(("VF", lo, lo + n), src, ("RR", lo, lo + n), OP.subtract)
 
-    def finish(lo, hi, ni, lst):
+    def products(EQ, lo, hi):
+        vgather(("PP", lo, hi), ("VF", 0, 32), ("BL", 0, (hi - lo) // 16), (EQ, lo, hi), OP.mult)
+
+    def names(lo, hi, sec, ni, lst):
+        tt(("SI", lo, hi), ("PP", lo, hi), ("bK", sec, sec + hi - lo), OP.add)
         ts((ni, lo, hi), ("SI", lo, hi), 5, 4095, OP.arith_shift_right, OP.bitwise_and)
         copy((lst, lo, hi), (ni, lo, hi))
 
-    def hash_many(EQ, k0, k1, ni, lst):
-        products(EQ, k0, k1)
-        names(k0, k1, ni, lst)
+    ts(M("ID"), XJ, ("PF", 6, 7), None, OP.is_equal)
+    ts(("OL", 0, 144), XI, ("PF", 10, 11), -SC, OP.is_equal, OP.mult)
+    for b, c in (("NG", -1.0), ("IDF", 1.0), ("NGF", -1.0), ("IC", -4.5 * SC), ("IB", 4.5 * SC), ("IW", 65536.0)):
+        act(M(b), M("ID"), AF.Copy, scale=c)
+    act(("OH", 0, 144), ("OL", 0, 144), AF.Copy, scale=0.5)
+    act(("bC", 256, 512), ("CTI", 0, 256), AF.Copy, scale=4096.0)
 
-    def products(EQ, k0, k1):
-        for k in range(k0, k1):
-            tt(("PP", 32 * k, 32 * k + 32), (EQ, 32 * k, 32 * k + 32), ("VF", 0, 32), OP.mult)
+    SIDE = {c: c in CFG["GS"].split() for c in CFG["GS"].split() + CFG["GV"].split()}
+    byS = {c[0] + k: s for c, s in SIDE.items() for k in c[1:]}
+    BIAS = {}
+    for w, c, base in (("a", "NA", 4.5), ("c", "NC", 0.0), ("b", "NB", 0.0)):
+        for grp in CFG[c].split():
+            assert len({byS[w + k] for k in grp}) == 1
+            BIAS[w + grp] = base + (-0.5 if byS[w + grp[0]] else 7.5)
+    BCOL = {v: 160 * i for i, v in enumerate(sorted(set(BIAS.values())))}
+    for v, o in BCOL.items():
+        fill(("BT", o, o + 160), v * SC / 64, 0, 64)
+    fill(("BT", 0, 160 * len(BCOL)), SC / 64, 64, 128)
+    fill(M("PB"), 1.0, 0, 64)
+    fill(M("PB"), 0.0, 64, 128)
 
-    def names(k0, k1, ni, lst):
-        tt(("SI", 32 * k0, 32 * k1), ("PP", 32 * k0, 32 * k1), ("bU0", 32 * k0, 32 * k1), OP.add)
-        finish(32 * k0, 32 * k1, ni, lst)
+    def later_constants():
+        fill(("K3", 0, 256), -0.5 / 128)
+        ts(("PF", 11, 12), ("PF", 1, 2), -41472.0, None, OP.add)
+        ts(("PF", 12, 13), ("PF", 1, 2), 8.0, None, OP.mult)
+        ts(("PF", 13, 14), ("PF", 4, 5), 8.0, 7.0, OP.mult, OP.add)
+        ts(("KM", 8, 16), ("XI", 0, 8), ("PF", 5, 6), None, OP.is_equal)
+        for j, m in (("J8", 2047), ("J4", 1023)):
+            ts(("JU", 0, 32), ("JT", 0, 32), m, None, OP.bitwise_and)
+            ts((j, 0, 32), ("JU", 0, 32), ("PF", 12, 13), None, OP.add)
+        tt(("PF", 14, 15), ("PF", 13, 14), ("PF", 0, 1), OP.add)
 
-    def hash_first():
-        tt(("PP", 32, 256), ("bU0", 256, 480), ("VF", 32, 256), OP.mult)
-        tt(("SI", 32, 256), ("PP", 32, 256), ("bU", 288, 512), OP.add)
-        finish(32, 256, "HI", "LB")
-
-    def uz(XA):
-        wrapped(("bU", 256, 288), "WL", XA, 4096, 4608, [(("ON15", 0, 128), ("K2", 0, 32))])
-
-    uz("XA0")
-    for k in range(4, 8):
-        bring("bCB", k)
-    act(("bCC", 256, 512), ("CTI", 0, 256), AF.Copy, scale=4096.0)
-    for h, b in ((0, "bCA"), (1, "bCB")):
-        act(("EQ0", 128 * h, 128 * h + 128), (b, 128 * h, 128 * h + 128), AF.Identity, bias=1184.0)
-        second("EQ0", 128 * h, 128 * h + 128)
-        if h == 0:
-            round_s(("bU", 256, 288), 0)
-            value_v(("bU", 256, 288), 0)
-        hash_many("EQ0", 4 * h, 4 * h + 4, "NI", "LN")
-    spread_first("EQ0")
-
-    def packs():
-        tt(("PK", 0, 256), ("NI", 0, 256), ("bCC", 256, 512), OP.add)
-    packs()
+    def turn(h):
+        ts(("R%d" % h, 0, 144), XI, ("PF", 14, 15), ("KM", 8 + h, 9 + h), OP.is_equal, OP.mult)
+    later_constants()
+    round_s(("bU", 256, 288), 0)
+    act(("EQ0", 0, 128), ("bA", 0, 128), AF.Identity, bias=3232.0)
+    second(("bK", 0, 128), ("EQ0", 0, 128))
+    value_v(("bU", 256, 288), 0)
+    products("EQ0", 0, 128)
+    act(("EQ0", 128, 256), ("bB", 128, 256), AF.Identity, bias=3232.0)
+    names(0, 128, 0, "NI", "LN")
+    REC.append(None)
+    for h in range(8):
+        turn(h)
 
     ends = []
     for t in range(RO):
@@ -316,162 +315,183 @@ def rank_program(g, core, T, topo):
         PKS = "PKS%d" % (t % 2)
         ZB = (XA, 4096, 4608)
         DW = ("D", 0, 4096)
+        SN = ("SN", 0, 32)
+        ORDER = CFG["ORDER"].split()
         tasks = {}
-        order = ["a%d" % k for k in AS] + ["c%d" % k for k in CS] + ["b%d" % k for k in BS]
 
-        def add(name, q, pre, fn):
-            tasks[name] = (q, pre, fn)
+        def add(name, pre, fn):
+            tasks[name] = (pre, fn)
 
-        def xa(k):
+        def xa(k, n=1):
             b = (k - 1) % 8
-            return (XA, 512 * b, 512 * b + 512)
+            return (XA, 512 * b, 512 * (b + n))
 
-        def lst(name, k):
-            return (name, 32 * k, 32 * k + 32)
+        def cols(name, k, n=1):
+            return (name, 32 * k, 32 * (k + n))
 
-        def blk(name, k):
-            return (name, 512 * k, 512 * k + 512)
-
-        def bank(name):
-            return ("bS%d" % (order.index(name) % 2), 0, 512)
-
-        def ds(name):
-            i = order.index(name) % 4
-            return ("DS", 512 * i, 512 * i + 512)
-
-        def by_scalar(n, pre, L, k, y, G, extra):
-            i = order.index(n)
-            add("ga" + n, "s", pre, lambda: gcopy("s", ds(n), DW, lst(L, k)))
-            add("st" + n, "t", ["ga" + n] + (["sg" + order[i - 2]] if i >= 2 else []),
-                lambda: mm(bank(n), [(("ID", 0, 128), ds(n)), (("NG", 0, 128), y)]))
-            add("sg" + n, "s", ["st" + n] + extra, lambda: act(blk(G, k), bank(n), AF.Sign, bias=-0.5))
-        for k in range(8):
-            if k in AS:
-                n = "a%d" % k
-                add("abs%d" % k, "s", ["st" + n], lambda n=n, k=k: act(xa(k), bank(n), AF.Abs))
-                by_scalar(n, [], "LN", k, ZB, "GA", ["abs%d" % k])
-            else:
-                add("gaa%d" % k, "v", [], lambda k=k: vgather(blk("XB", k), DW, lst("LN", k), ZB, OP.subtract))
-                add("abs%d" % k, "s", ["gaa%d" % k], lambda k=k: act(xa(k), blk("XB", k), AF.Abs))
-                add("sga%d" % k, "v", ["gaa%d" % k], lambda k=k: ts(blk("GA", k), blk("XB", k), 0.0, None, OP.is_gt))
-            for w, S_, G, L, pre in (("c", CS, "GC", "LC", "HC"), ("b", BS, "GB", "LB", "HB")):
-                if k == 0:
-                    continue
-                n = w + str(k)
-                y = xa(0) if w == "c" else xa(k)
-                if k in S_:
-                    by_scalar(n, [pre], L, k, y, G, [])
-                elif w == "b" and k in CFG["BM"]:
-                    add("sg" + n, "v", [pre], lambda k=k: vgather(("GB", 512 * k, 512 * k + 1024), DW, ("LB", 32 * k, 32 * k + 64),
-                                                                  (XA, 512 * k - 512, 512 * k + 512), OP.is_gt))
-                elif w == "b" and k - 1 in CFG["BM"]:
-                    add("sg" + n, "v", ["sgb%d" % (k - 1)], lambda: None)
-                else:
-                    add("sg" + n, "v", [pre], lambda k=k, G=G, L=L, y=y: vgather(blk(G, k), DW, lst(L, k), y, OP.is_gt))
-
-        def count(w, ks):
-            G, B, S_ = {"a": ("GA", "bCA", AS), "b": ("GB", "bCB", BS), "c": ("GC", "bCC", CS)}[w]
-            kinds = [k in S_ for k in ks]
+        def blk(name, k, n=1):
+            return (name, 512 * k, 512 * (k + n))
+        HG = [[[int(x) for x in s] for s in p.split(",")] for p in CFG["HB"].split()]
+        hb = {k: "HB%d" % p[0][0] for p in HG for s in p for k in s}
+        subs = ["st" + (k if c[0] == "a" else c[0] + k) for c in CFG["GS"].split() for k in c[1:]]
+        sign = {}
+        spare = [0]
+        gets = {}
+        for call, s in SIDE.items():
+            w, ks = call[0], [int(x) for x in call[1:]]
             k0, n = ks[0], len(ks)
-            if kinds == sorted(kinds):
-                b0 = 96 - 32 * kinds.count(False)
-                o = 32 * k0
-                if w == "b" and k0 >= 6:
-                    B, o = "bM", 32 * k0 + 128
-                extra = [(("ON15", 0, 128), ("BT", b0, b0 + 32 * n))]
-                if w == "c":
-                    extra.append((("BI", 0, 128), ("HP", 32 * k0, 32 * (k0 + n))))
-                wrapped((B, o, o + 32 * n), "OL", G, 512 * k0, 512 * (k0 + n), extra)
-            else:
+            G, L = {"a": ("GA", "LN"), "b": ("GB", "LB"), "c": ("GC", "LC")}[w]
+            pre = {"a": [], "c": ["HC"], "b": sorted({hb.get(k) for k in ks})}[w]
+            gn = "g%s%d" % (w, k0)
+            gets[gn] = [w + str(k) for k in ks]
+            if s:
+                if w == "a":
+                    DS, o = "DS", k0
+                else:
+                    DS, o = "DT", spare[0]
+                    spare[0] += n
+                add(gn, pre, lambda DS=DS, o=o, n=n, L=L, k0=k0: gcopy("s", blk(DS, o, n), DW, cols(L, k0, n)))
                 for k in ks:
-                    count(w, [k])
+                    nm = str(k) if w == "a" else w + str(k)
+                    bank = ("bS%d" % (subs.index("st" + nm) % 2), 0, 512)
+                    y = {"a": ZB, "c": xa(0), "b": xa(k)}[w]
+                    add("st" + nm, [gn], lambda bank=bank, d=blk(DS, o + k - k0), y=y: mm(bank, [(M("ID"), d), (M("NG"), y)]))
+                    if w == "a":
+                        add("abs%d" % k, ["st" + nm], lambda k=k, bank=bank: act(xa(k), bank, AF.Abs))
+                    sign[w + str(k)] = "s%s%d" % (w, k)
+                    add("s%s%d" % (w, k), ["st" + nm], lambda k=k, bank=bank, G=G: act(blk(G, k), bank, AF.Sign, bias=-0.5))
+            elif w == "a":
+                add(gn, pre, lambda k0=k0: vgather(blk("XB", k0), DW, cols("LN", k0), ZB, OP.subtract))
+                add("abs%d" % k0, [gn], lambda k0=k0: act(xa(k0), blk("XB", k0), AF.Abs))
+                grp = [x for x in CFG["SV"].split() if str(k0) in x][0]
+                sign[call] = "sa" + grp[0]
+                if int(grp[0]) == k0:
+                    add("sa%d" % k0, ["ga" + x for x in grp],
+                        lambda k0=k0, n=len(grp): ts(blk("GA", k0, n), blk("XB", k0, n), 0.0, None, OP.is_gt))
+            else:
+                y = xa(0) if w == "c" else xa(k0, n)
+                add(gn, pre, lambda G=G, L=L, k0=k0, n=n, y=y: vgather(blk(G, k0, n), DW, cols(L, k0, n), y, OP.is_gt))
+                for k in ks:
+                    sign[w + str(k)] = gn
+        for i, o in enumerate(subs[2:]):
+            p = subs[i][2:]
+            tasks[o][0].extend(["abs" + p, "sa" + p] if p.isdigit() else ["s" + p])
+        E = CFG["EARLY"]
+
+        def cb(k, n):
+            return cols("bB" if k <= E else "bM", k, n)
+
+        def count(w, grp):
+            G, B = {"a": ("GA", "bA"), "b": ("GB", None), "c": ("GC", "bC")}[w]
+            k0, n = int(grp[0]), len(grp)
+            out = cols(B, k0, n) if B else cb(k0, n)
+            o = BCOL[BIAS[w + grp]]
+            parts = [(M("PB"), ("BT", o, o + 32 * n))]
+            if w != "a":
+                parts += [(M("I" + w.upper()), SN, cols(out[0], k0 + i)) for i in range(n)]
+            mm(out, parts + wrap("OH" if byS[w + grp[0]] else "OL", G, 512 * k0, 512 * (k0 + n)))
         for w, c in (("a", "NA"), ("c", "NC"), ("b", "NB")):
             for grp in CFG[c].split():
-                ks = [int(x) for x in grp]
-                add("n%s%d" % (w, ks[0]), "t", ["sg%s%d" % (w, k) for k in ks] + (["H0"] if w == "c" else []), lambda w=w, ks=ks: count(w, ks))
-        counts = ["n%s%s" % (w, grp[0]) for w, c in (("a", "NA"), ("c", "NC")) for grp in CFG[c].split()]
-        late = "nb" + CFG["NB"].split()[-1][0]
-        add("U0", "t", ["abs0"], lambda: wrapped(("bM", 288, 320), "WL", XA, 3584, 4096, [(("ON15", 0, 128), ("K2", 0, 32))]))
-        add("RC", "s", ["U0"], lambda: round_s(("bM", 288, 320), 0))
-        UG = [[int(x) for x in grp] for grp in CFG["NU"].split()]
-        for ks in UG:
-            add("U%d" % ks[0], "t", ["abs%d" % k for k in ks], lambda ks=ks: wrapped(
-                ("bU", 32 * ks[0], 32 * ks[-1] + 32), "WL", XA, 512 * (ks[0] - 1), 512 * ks[-1],
-                [(("ON15", 0, 128), ("K2", 0, 32 * len(ks)))]))
+                add("n" + w + grp[0], [sign[w + k] for k in grp] + ([] if w == "a" else ["SN"]), lambda w=w, grp=grp: count(w, grp))
 
-        def do_par():
-            emit("s", [lambda e: e.activation(T.AJ[:, 0:32], T.bM[:, 256:288], AF.Copy, accum_out=T.AR[:, 0:1])],
-                 [("bM", 256, 288)], [("AJ", 0, 32), ("AR", 0, 1)])
-            act(("AR", 1, 2), ("AR", 0, 1), AF.Identity, bias=MID, scale=0.5)
-            act(("AR", 2, 3), ("AR", 1, 2), AF.Identity, bias=2 * MID, scale=-2.0)
-            act(("AR", 3, 4), ("AR", 2, 3), AF.Abs, bias=("AR", 0, 1))
-            for lo, b in ((0, -7.5), (96, 1.0)):
-                act(("BT", lo, lo + 96), ("BN", lo, lo + 96), AF.Identity, bias=b, scale=("AR", 3, 4))
+        def groups(c, w, lo, hi):
+            return ["n" + w + grp[0] for grp in CFG[c].split() if lo <= int(grp[0]) <= hi]
+        add("SN", ["na0"], lambda: act(SN, cols("bA", 0), AF.Sign, bias=-4.5 * SC))
+        add("U0", ["abs0"], lambda: usum(("bM", 288, 320), XA, 3584))
+        add("RC", ["U0"], lambda: round_s(("bM", 288, 320), 0))
 
         def do_hc():
             value_v(("bM", 288, 320), 0)
-            hash_many(EQ, 1, 8, "HI", "LC")
-        add("HC", "v", ["RC"], do_hc)
+            products(EQ, 32, 256)
+            names(32, 256, 32, "HI", "LC")
+        add("HC", ["RC", "H7"], do_hc)
+        k7 = 7 if t else 4
 
-        def do_rb():
-            round_s(("bU", 32, 256), 32)
-        add("RB", "s", ["U%d" % ks[0] for ks in UG], do_rb)
+        def do_e7():
+            if t:
+                ts(cols("NM", 0), cols("LP%d" % (t - 1), 0), 4095, None, OP.bitwise_and)
+                ts(cols(EQ, 7), cols("NM", 0), 1184.0, None, OP.add)
+        add("E7", [], do_e7)
+        add("S7", ["E7"], lambda: second(cols("bK", k7, 8 - k7), cols(EQ, k7, 8 - k7)))
 
-        def do_hb():
-            value_v(("bU", 32, 256), 32)
-            hash_first()
-        add("HB", "v", ["RB", "HC"], do_hb)
+        def do_h7():
+            if t:
+                tt(cols("PP", 7), cols(EQ, 7), cols("VF", 0), OP.mult)
+            else:
+                products(EQ, 128, 256)
+            names(32 * k7, 256, 32 * k7, "NI", "LN")
+        add("H7", ["S7"], do_h7)
+        for k in range(4, 8):
+            tasks[[n for n in gets if "a%d" % k in gets[n]][0]][0].append("H7")
+        for i, p in enumerate(HG):
+            B, k0, n = ("bU", "bM")[i], p[0][0], sum(len(s) for s in p)
+            for j, s in enumerate(p):
+                def do_u(B=B, k0=k0, n=n, s=s, j=j, end=j == len(p) - 1):
+                    o = cols(B, s[0], len(s))
+                    parts = [x + (o,) for x in wrap("WL", XA, 512 * (s[0] - 1), 512 * s[-1])]
+                    if j == 0:
+                        parts = [(M("ON"), ("K2", 0, 32 * n))] + parts
+                    mm(cols(B, k0, n) if j == 0 else o, parts, j == 0, end)
+                add("U%d" % s[0], ["abs%d" % k for k in s] + (["U%d" % p[j - 1][0]] if j else ["HC"] if i else []), do_u)
 
-        def do_h0():
-            for k in range(1, 8):
-                act(("H0", 32 * k, 32 * k + 32), ("bCA", 0, 32), AF.Copy, scale=-1.0)
-            act(("HP", 32, 256), ("H0", 32, 256), AF.Relu, scale=1.0 / SCALE)
-        add("H0", "s", ["na0"], do_h0)
+            def do_rb(B=B, k0=k0, n=n):
+                round_s(cols(B, k0, n), 32 * k0)
+                if CFG["RRPE"]:
+                    mm(cols(B, k0, n), [(M("NG"), cols("RR", k0, n))], False, True)
+            add("RB%d" % k0, ["U%d" % p[-1][0], "RC"], do_rb)
 
-        def do_pq():
-            ts(("A0T", 0, 32), ("bCA", 0, 32), 0.0, 131072.0, OP.is_gt, OP.mult)
-            tt(("T1", 32, 256), ("bCC", 32, 256), ("PK", 32, 256), OP.min)
-            tt(("KEY", 0, 32), ("PK", 0, 32), ("A0T", 0, 32), OP.add)
-            tt(("PQ", 32, 256), ("bCA", 32, 256), ("T1", 32, 256), OP.min)
-        add("PQ", "v", ["H0"] + counts, do_pq)
+            def do_hb(B=B, k0=k0, n=n):
+                if CFG["RRPE"]:
+                    tt(cols("PP", k0, n), ("ER", 0, 32 * n), cols(B, k0, n), OP.mult)
+                else:
+                    tt(cols(B, k0, n), cols(B, k0, n), cols("RR", k0, n), OP.subtract)
+                    tt(cols("PP", k0, n), ("ER", 0, 32 * n), cols(B, k0, n), OP.mult)
+                names(32 * k0, 32 * (k0 + n), 256, "HI", "LB")
+            add("HB%d" % k0, ["RB%d" % k0, "HC"], do_hb)
+        add("pack", ["H7"], lambda: tt(("NP", 0, 256), ("NI", 0, 256), ("bC", 256, 512), OP.add))
+        add("W0", ["pack", "SN"], lambda: mm(("bA", 256, 288), [(M("IDF"), cols("NP", 0)), (M("IW"), SN)]))
+        add("DIFF", ["E7"], lambda: mm(("bA", 288, 512), [(M("IDF"), (EQ, 32, 256)), (M("NGF"), (EQ, 0, 224))]))
 
-        def key(lo, hi):
-            cb = ("bCB", lo, hi) if lo < 192 else ("bM", lo + 128, hi + 128)
-            tt(("bCA", 256 + lo, 256 + hi), cb, ("H0", lo, hi), OP.mult)
-            tt(("KEY", lo, hi), ("PQ", lo, hi), ("bCA", 256 + lo, 256 + hi), OP.min)
+        CE = CFG["CE"]
+        W0 = ("bA", 256, 288)
+        add("NT", ["pack"] + groups("NA", "a", 0, 7), lambda: tt(cols("NT", 1, 7), cols("bA", 1, 7), cols("NP", 1, 7), OP.max))
+        add("NC", ["NT"] + groups("NC", "c", 1, CE), lambda: tt(cols("NT", 1, CE), cols("bC", 1, CE), cols("NT", 1, CE), OP.max))
+        add("Y1", groups("NB", "b", 1, E), lambda: act(cb(1, E), cb(1, E), AF.Abs))
+        add("Y%d" % (E + 1), groups("NB", "b", E + 1, 7), lambda: act(cb(E + 1, 7 - E), cb(E + 1, 7 - E), AF.Abs))
 
-        def do_key1():
-            key(32, 192)
-            tt(("TR", 0, 96), ("KEY", 0, 96), ("KEY", 96, 192), OP.max)
-            tt(("TR", 96, 128), ("TR", 0, 32), ("TR", 32, 64), OP.max)
-            tt(("TR", 128, 160), ("TR", 96, 128), ("TR", 64, 96), OP.max)
-        add("KEY1", "v", ["PQ"] + ["nb" + grp[0] for grp in CFG["NB"].split()[:-1]], do_key1)
+        def do_early():
+            tt(cols("WK", 1, E), cols("NT", 1, E), cb(1, E), OP.max)
+            h = E // 2
+            tt(cols("TR", 0, h), cols("WK", 1, h), cols("WK", 1 + h, h), OP.min)
+            if E > 4:
+                tt(cols("TR", 3), cols("WK", 5) if E == 5 else cols("TR", 2), W0, OP.min)
+            tt(cols("TR", 5), cols("TR", 0), cols("TR", 1), OP.min)
+            tt(cols("TR", 4), cols("TR", 5), cols("TR", 3) if E > 4 else W0, OP.min)
+        add("EARLY", ["NC", "Y1", "W0"], do_early)
+        best = [cols("TR", 4)]
 
-        def do_tail():
-            key(192, 256)
-            tt(("TR", 160, 192), ("KEY", 192, 224), ("KEY", 224, 256), OP.max)
-            tt((PKS, 0, 32), ("TR", 128, 160), ("TR", 160, 192), OP.max)
-            ts(("TS", 0, 32), (PKS, 0, 32), 12, None, OP.arith_shift_right)
-            ts(("LS", 0, 32), ("TS", 0, 32), -16.0, ("PF", 11, 12), OP.mult, OP.add)
-        add("TAIL", "v", ["KEY1", late], do_tail)
+        def fold(ks, end):
+            items = [cols("WK", k) for k in ks] + best
+            i = 0
+            while len(items) > 1:
+                out = end if len(items) == 2 and end else cols("TR", (5, 6, 7)[i])
+                tt(out, items[0], items[1], OP.min)
+                items = items[2:] + [out]
+                i += 1
+            best[0] = items[0]
 
-        lists = {"v": CFG["V"].split(), "s": CFG["S"].split(), "t": CFG["T"].split()}
-        assert sorted(lists["v"] + lists["s"] + lists["t"]) == sorted(tasks), set(tasks) ^ set(lists["v"] + lists["s"] + lists["t"])
-        done = set()
-        pos = {"v": 0, "s": 0, "t": 0}
-        while len(done) < len(tasks):
-            moved = False
-            for q in ("v", "s", "t"):
-                while pos[q] < len(lists[q]) and all(p in done for p in tasks[lists[q][pos[q]]][1]):
-                    nm = lists[q][pos[q]]
-                    assert tasks[nm][0] == q
-                    tasks[nm][2]()
-                    done.add(nm)
-                    pos[q] += 1
-                    moved = True
-            assert moved, [lists[q][pos[q]:pos[q] + 1] for q in lists]
+        def do_late():
+            tt(cols("WK", E + 1, 7 - E), cols("NT", E + 1, 7 - E), cb(E + 1, 7 - E), OP.max)
+            fold(range(E + 1, CE + 1), cols(PKS, 0) if CE == 7 else cols("TR", 0))
+        add("LATE", ["EARLY", "Y%d" % (E + 1)], do_late)
 
-        mm(("bCB", 256, 480), [(("IDF", 0, 128), (EQ, 32, 256)), (("NGF", 0, 128), (EQ, 0, 224))])
+        def do_last():
+            if CE < 7:
+                tt(cols("WK", CE + 1, 7 - CE), cols("WK", CE + 1, 7 - CE), cols("bC", CE + 1, 7 - CE), OP.max)
+                fold(range(CE + 1, 8), cols(PKS, 0))
+            ts(cols("TS", 0), cols(PKS, 0), 12, None, OP.arith_shift_right)
+            ts(cols("LS", 0), cols("TS", 0), 16.0, ("PF", 11, 12), OP.mult, OP.add)
+        add("LAST", ["LATE"] + groups("NC", "c", CE + 1, 7), do_last)
 
         dst = T.cores[(rank + 1 + t % (N - 1)) % N]
         rid, pid = topo.addr(dst)[0], topo.addr(dst)[1]
@@ -479,84 +499,113 @@ def rank_program(g, core, T, topo):
         ne = len(topo.engines(core, dst))
 
         def send(out, in_, rsem, lsem):
-            return emit("g", [lambda e: e.remote_dma(ap(out), ap(in_), T.sem[rsem], T.sem[lsem], pid, rid, mask)],
-                        [reg(in_)], [], sem=lsem, val=ne, remote=True)
-
-        def landed(buf, lo, hi, rsem):
-            note("g", buf, lo, hi, True, (rsem, ne, {rsem: ne}))
+            ends.append(emit("g", [lambda e: e.remote_dma(ap(out), ap(in_), T.sem[rsem], T.sem[lsem], pid, rid, mask)],
+                             [reg(in_)], [], sem=lsem, val=ne, remote=out))
+            note("g", out[0], out[1], out[2], True, (rsem, ne, {rsem: ne}))
         LP, LZ = "LP%d" % t, "LZ%d" % t
-        ends.append(send((LP, 0, 32), (PKS, 0, 32), "an%d" % t, "ln%d" % t))
-        gcopy("v", (XN, 4096, 4352), (XA, 0, 4608), ("LS", 0, 16))
-        gcopy("s", (XN, 4352, 4608), (XA, 0, 4608), ("LS", 16, 32))
-        ends.append(send((LZ, 0, 256), (XN, 4096, 4352), "az%d" % t, "lz%d" % t))
-        ends.append(send((LZ, 256, 512), (XN, 4352, 4608), "ay%d" % t, "ly%d" % t))
-        landed(LP, 0, 32, "an%d" % t)
-        landed(LZ, 0, 256, "az%d" % t)
-        landed(LZ, 256, 512, "ay%d" % t)
 
-        ts(("S0", 0, 32), (PKS, 0, 32), 262144.0, 2097152.0, OP.is_lt, OP.mult)
-        tt(("P2", 0, 32), (PKS, 0, 32), ("S0", 0, 32), OP.add)
-        if not last:
-            mm(("bM", 256, 288), [(("ONS", 0, 128), ("S0", 0, 32))])
-        for k in range(7):
-            ts(("MK", 32 * k, 32 * k + 32), ("P2", 0, 32), float((9 - k) * 131072), None, OP.is_ge)
-        if not last:
-            uz(XN)
-            round_s(("bU", 256, 288), 0)
-        tt(("bCB", 256, 480), ("bCB", 256, 480), ("MK", 0, 224), OP.mult)
-        tt((EN, 0, 224), ("bCB", 256, 480), (EQ, 0, 224), OP.add)
-        if not last:
-            second(EN, 0, 224)
-            value_v(("bU", 256, 288), 0)
-            do_par()
-            products(EN, 0, 7)
-        else:
-            split(EN, 0, 224, 2)
-        J, nq = ("J4", 4) if last else ("J8", 2)
-        ts(("NM", 0, 32), (LP, 0, 32), 4095, None, OP.bitwise_and)
-        ts(("CI", 0, 32), (LP, 0, 32), 7, None, OP.bitwise_and)
-        ts((EN, 224, 256), ("NM", 0, 32), 1184.0, None, OP.add)
-        tt(("CJ", 0, 32), ("CI", 0, 32), (J, 0, 32), OP.add)
-        copy(("LD", 0, 32), ("CJ", 0, 32))
-        if not last:
-            second(EN, 224, 256)
-        WQ, SQ, CQ = 4096 // nq, 512 // nq, 32 // nq
-        parts = [((SQ * q, SQ * q + SQ), (WQ * q, WQ * q + WQ), (CQ * q, CQ * q + CQ)) for q in range(nq)]
-        for q, (R, W, C) in enumerate(parts):
-            gcopy("s", ("DC",) + R, ("D",) + W, ("LD",) + C)
-        if not last:
-            products(EN, 7, 8)
-            names(0, 8, "NI", "LN")
-            packs()
-        else:
-            split(EN, 224, 256, 2)
-        for q, (R, W, C) in enumerate(parts):
-            b = ("bS0", "bS1", "bU0", "bU")[q]
-            extra = [(("ON15", 0, 128), ("K3", 0, SQ))] if q % 2 else []
-            mm((b, 0, SQ), extra + [(("ID", 0, 128), ("DC",) + R), (("ID", 0, 128), (LZ,) + R)])
-            if q % 2:
-                act(("FX", 0, SQ), (b, 0, SQ), AF.Identity, bias=MID, scale=0.5)
-                act(("FB", (q // 2) * SQ, (q // 2) * SQ + SQ), ("FX", 0, SQ), AF.Identity, bias=-MID)
-        for q, (R, W, C) in enumerate(parts):
-            b = ("bS0", "bS1", "bU0", "bU")[q]
-            F = ("FB", (q // 2) * SQ, (q // 2) * SQ + SQ) if q % 2 else ("FL",) + R
-            if q % 2 == 0:
-                ts(F, (b, 0, SQ), 0.5, -0.25, OP.mult, OP.add)
-            emit("v", [lambda e, F=F, W=W, C=C: e.tensor_copy(ap(("D",) + W).indirect(ap(("LD",) + C)), ap(F))],
-                 [F, ("LD",) + C], [("D",) + W])
+        def later(fn):
+            return (lambda: None) if last else fn
+        add("TX", ["LAST"], lambda: send(cols(LP, 0), cols(PKS, 0), "an%d" % t, "ln%d" % t))
+        for h, (a, l) in enumerate((("az", "lz"), ("ay", "ly"))):
+            def do_z(h=h, a=a, l=l):
+                Z = (XN, 4096 + 256 * h, 4352 + 256 * h)
+                gcopy(CFG["STATE"][h], Z, (XA, 0, 4608), ("LS", 16 * h, 16 * h + 16))
+                send((LZ, 256 * h, 256 * h + 256), Z, "%s%d" % (a, t), "%s%d" % (l, t))
+            add("Z%d" % h, ["TX"] + ["Z0"] * h, do_z)
+
+        def do_p2():
+            ts(cols("S0", 0), cols("TS", 0), 2816.0, 512.0, OP.is_ge, OP.mult)
+            tt(cols("P2", 0), cols("TS", 0), cols("S0", 0), OP.subtract)
+        add("P2", ["LAST"], do_p2)
+        add("UZ", ["Z1"], later(lambda: usum(("bU", 256, 288), XN, 4096)))
+        add("PA", ["P2"], later(lambda: mm(("bM", 256, 288), [(M("ON"), cols("S0", 0))])))
+        add("MK", ["P2"], lambda: vgather(("MK", 0, 224), cols("P2", 0), ("BL", 0, 14), ("THR", 0, 224), OP.is_lt))
+        add("RZ", ["UZ"], later(lambda: round_s(("bU", 256, 288), 0)))
+
+        def do_sh():
+            tt(("bA", 288, 512), ("bA", 288, 512), ("MK", 0, 224), OP.mult)
+            tt((EN, 0, 224), ("bA", 288, 512), (EQ, 0, 224), OP.add)
+        add("SH", ["MK", "DIFF"], do_sh)
+        add("SE", ["SH"], later(lambda: second(("bK", 0, 224), (EN, 0, 224))))
+
+        def do_hn():
             if last:
-                ends.append(dma("y", T.yd[:, W[0]:W[1]], ap(("D",) + W), [("D",) + W], [], "sd%d" % q))
-        if not last:
-            spread_first(EN)
-        else:
-            for h in range(8):
-                b, o = ("bM", "bCB")[h // 4], 64 * (h % 4)
-                mm((b, o, o + 64), [(("R%d" % h, 7 - k, 135 - k), ("EHL", 64 * k, 64 * k + 64)) for k in range(8)])
-            for i, b in enumerate(("bM", "bCB")):
-                act(("PK", 128 * i, 128 * i + 128), (b, 0, 256, 2), AF.Identity, bias=-1184.0)
-                for h in range(4):
-                    tt(("YE", 4 * i + h, 256, 8), ("PK", 128 * i + 32 * h, 128 * i + 32 * h + 32), (b, 64 * h + 1, 64 * h + 64, 2), OP.add)
+                ts(("EH", 0, 224), (EN, 0, 224), -3232.0, None, OP.add)
+                ts(cols("NM", 0), cols(LP, 0), 4095, None, OP.bitwise_and)
+                ts(cols("EH", 7), cols("NM", 0), -2048.0, None, OP.add)
+            else:
+                value_v(("bU", 256, 288), 0)
+                products(EN, 0, 224)
+                names(0, 224, 0, "NI", "LN")
+        add("HN", ["SE", "RZ"], do_hn)
+        J, nq = ("J4", 4) if last else ("J8", 2)
+
+        def do_ar():
+            ts(cols("CI", 0), cols(LP, 0), 7, None, OP.bitwise_and)
+            tt(cols("CJ", 0), cols("CI", 0), cols(J, 0), OP.add)
+            copy(cols("LD", 0), cols("CJ", 0))
+        add("AR", ["TX"], do_ar)
+        WQ, SQ, CQ = 4096 // nq, 512 // nq, 32 // nq
+        RND = CFG["LROUND"] if last else CFG["ROUND"]
+        for h in range(2):
+            parts = [(q, (SQ * q, SQ * q + SQ), (WQ * q, WQ * q + WQ), (CQ * q, CQ * q + CQ), ("bS0", "bS1", "bK", "bU")[q])
+                     for q in range(h * nq // 2, (h + 1) * nq // 2)]
+
+            def do_dc(parts=parts):
+                for q, R, W, C, b in parts:
+                    gcopy("s", ("DC",) + R, ("D",) + W, ("LD",) + C)
+
+            def do_up(parts=parts):
+                for q, R, W, C, b in parts:
+                    extra = [(M("ON"), ("K3", 0, SQ))] if RND[q] == "s" else []
+                    mm((b, 0, SQ), extra + [(M("ID"), ("DC",) + R), (M("ID"), (LZ,) + R)])
+                    if RND[q] == "s":
+                        act(("FX",) + R, (b, 0, SQ), AF.Identity, bias=MID, scale=0.5)
+                        act(("FB",) + R, ("FX",) + R, AF.Identity, bias=-MID)
+
+            def do_sc(parts=parts):
+                for q, R, W, C, b in parts:
+                    F = ("FB",) + R if RND[q] == "s" else ("FL",) + R
+                    if RND[q] == "v":
+                        ts(F, (b, 0, SQ), 0.5, -0.25, OP.mult, OP.add)
+                    emit("v", [lambda e, F=F, W=W, C=C: e.tensor_copy(ap(("D",) + W).indirect(ap(("LD",) + C)), ap(F))],
+                         [F, ("LD",) + C], [("D",) + W])
+                    if last:
+                        ends.append(dma("y", T.yd[:, W[0]:W[1]], ap(("D",) + W), [("D",) + W], [], "sd%d" % q))
+            add("DC%d" % h, ["AR"], do_dc)
+            add("UP%d" % h, ["DC%d" % h, "Z%d" % h], do_up)
+            add("SC%d" % h, ["UP%d" % h], do_sc)
+
+        def do_pt():
+            emit("s", [lambda e: e.activation(T.AJ[:, 0:32], T.bM[:, 256:288], AF.Copy, scale=1.0 / 512, accum_out=T.AR[:, 0:1])],
+                 [("bM", 256, 288)], [("AJ", 0, 32), ("AR", 0, 1)])
+            act(("AR", 1, 2), ("AR", 0, 1), AF.Identity, bias=MID, scale=0.5)
+            act(("AR", 2, 3), ("AR", 1, 2), AF.Identity, bias=2 * MID, scale=-2.0)
+            emit("s", [lambda e: e.activation(T.PB[64:128, :], T.ON[64:128, :], AF.Abs, bias=T.AR[64:128, 0:1], scale=T.AR[64:128, 2:3])],
+                 [M("ON"), ("AR", 0, 3)], [M("PB")])
+        add("PT", [], do_pt if t else lambda: None)
+        add("SP", [], lambda: spread_first(EQ))
+        for n in tasks:
+            tasks[n][0].extend({"na": ["PT"], "HB": ["SP"]}.get(n[:2], []))
+
+        assert sorted(ORDER) == sorted(tasks), set(tasks) ^ set(ORDER)
+        done = []
+        while len(done) < len(ORDER):
+            nm = [x for x in ORDER if x not in done and all(p in done for p in tasks[x][0])][0]
+            TAG[0] = nm
+            tasks[nm][1]()
+            done.append(nm)
+        TAG[1:] = [" ".join(done), {n: tasks[n][0] for n in tasks}]
+        TAG[0] = "end"
+        REC.append(None)
+        if last:
             ends.append(dma("s", T.yz[:, :], T[XN][:, 4096:4608], [(XN, 4096, 4608)], [], "sz"))
+            for h in range(8):
+                b = ("bM", "bB")[h // 4]
+                mm(cols(b, h), [(("R%d" % h, 7 - k, 135 - k), cols("EH", k)) for k in range(8)])
+            for h in range(8):
+                act(("YE", h, 256, 8), cols(("bM", "bB")[h // 4], h), AF.Identity, bias=2048.0)
             ends.append(dma("s", T.ye[:, :], T.YE[:, :], [("YE", 0, 256)], [], "se"))
     settle("g", ends)
     settle("g", [(qsem[q], cnt[q], {}) for q in "vstg"])

@@ -9,43 +9,49 @@ SC = 1.25 * 2.0 ** 21
 B2, B4, H2, I4, U2 = "bfloat16", "float32", "float16", "int32", "uint16"
 SCRATCH = {}
 for _n, _w, _d in (("D", 4096, B2), ("XA0", 4608, B2), ("XA1", 4608, B2), ("XB", 4096, B2), ("GA", 4096, B2), ("GB", 4096, B2),
-                   ("GC", 4096, B2), ("DS", 4096, B2), ("DT", 2048, B2), ("DC", 512, B2), ("FL", 512, I4), ("LN", 256, U2), ("LB", 256, U2),
-                   ("LC", 256, U2), ("LS", 32, U2), ("LD", 32, U2), ("BL", 16, U2), ("EQ0", 256, B4), ("EQ1", 256, B4), ("VF", 256, B4),
-                   ("PP", 256, B4), ("SI", 256, I4), ("HI", 256, I4), ("NI", 256, I4), ("NP", 256, B4), ("NT", 256, B4),
-                   ("WK", 256, B4), ("TR", 256, B4), ("SN", 32, B2), ("PKS0", 32, I4), ("PKS1", 32, I4), ("TS", 32, I4),
+                   ("GC", 4096, B2), ("DS", 4096, B2), ("DT", 2048, B2), ("DC", 512, B2), ("FL", 512, I4),
+                   ("LS", 32, U2), ("LD", 32, U2), ("BL", 16, U2), ("EQ0", 256, B4), ("EQ1", 256, B4), ("Va", 32, I4), ("Vc", 32, I4), ("Vb", 256, I4), ("K4", 224, B2),
+                   ("NP", 256, B4), ("NT", 256, B4), ("FA", 256, B2), ("FC", 256, B2), ("FY", 256, B2), ("WK", 256, B4), ("TR", 256, B4), ("SN", 32, B2), ("PKS0", 32, I4), ("PKS1", 32, I4), ("TS", 32, I4),
                    ("S0", 32, B2), ("P2", 32, B4), ("ER", 256, B4), ("MK", 256, B4), ("AR", 8, B4), ("AJ", 32, B4), ("NM", 32, I4),
-                   ("CI", 32, I4), ("CJ", 32, I4), ("BT", 960, B2), ("PB", 128, B2), ("J8", 32, I4), ("JT", 32, I4), ("BJ", 16, I4),
+                   ("CI", 32, I4), ("CJ", 32, I4), ("BT", 960, B2), ("PB", 128, B2), ("JM", 32, I4), ("JL", 32, I4), ("BJ", 16, I4),
                    ("ID", 128, B2), ("NG", 128, B2), ("IDF", 128, B4), ("NGF", 128, B4), ("ON", 128, B2), ("IC", 128, B2),
                    ("IB", 128, B2), ("IW", 128, B2), ("OL", 144, B2), ("OH", 144, B2), ("WL", 144, B2), ("XI", 144, B2),
                    ("CTI", 256, B4), ("THR", 224, B4), ("PI", 8, I4), ("PJ", 16, I4), ("PF", 32, B4), ("KM", 16, B4),
-                   ("WI", 1, I4), ("WF", 1, B4), ("EFI", 256, I4), ("EH", 256, H2), ("J4", 32, I4), ("JU", 32, I4), ("K2", 160, B2),
-                   ("K3", 256, B2), ("RX", 256, B4), ("RR", 256, B2), ("FX", 512, B4), ("FB", 512, B2), ("YE", 256, B4)):
+                   ("WI", 1, I4), ("WF", 1, B4), ("EFI", 256, I4), ("EH", 256, H2), ("O16", 144, H2), ("K2", 256, B2),
+                   ("K3", 256, B2), ("RX", 288, B4), ("RR", 288, B4), ("RH", 256, B2), ("FX", 512, B4), ("FB", 512, B2), ("YE", 256, B4)):
     SCRATCH[_n] = ("sbuf", [128, _w], _d)
-for _n in ("bK", "bU", "bA", "bB", "bC", "bS0", "bS1", "bM"):
+for _n in "abc":
+    for _w, _d in (("P", B4), ("S", I4), ("I", I4), ("L", U2)):
+        SCRATCH[_w + _n] = ("sbuf", [128, 256], _d)
+for _n in ("bK", "bU", "bA", "bB", "bC", "bM"):
     SCRATCH[_n] = ("psum", [128, 512], B4)
+SCRATCH["bS"] = ("psum", [128, 1024], B4)
 for _k in range(8):
     SCRATCH["Q%d" % _k] = ("sbuf", [128, 144], H2)
     SCRATCH["R%d" % _k] = ("sbuf", [128, 144], H2)
 for _t in range(RO):
     SCRATCH["LP%d" % _t] = ("sbuf", [128, 32], I4)
     SCRATCH["LZ%d" % _t] = ("sbuf", [128, 512], B2)
-SEMAPHORES = (["qv", "qs", "qt", "qg"] + ["ldz", "lde", "ldw", "ldd0", "ldd1", "sd0", "sd1", "sd2", "sd3", "se", "sz"]
-              + ["%s%d" % (n, t) for t in range(RO) for n in ("an", "az", "ay", "ln", "lz", "ly")])
-TAG = [""]
+SEMAPHORES = (["qv", "qs", "qt", "qg"] + ["ldz", "lde", "ldw", "ldd0", "se", "sz"] + ["sd%d" % _k for _k in range(8)]
+              + ["%s%d" % (n, t) for t in range(RO) for n in ("an", "ln")]
+              + ["%s%d_%d" % (n, t, h) for t in range(RO) for n in ("az", "lz") for h in range(5)])
+TAG = ["", "", ""]
 REC = []
 
 CFG = {
-    "GS": "a3 a4 a5 a6 a7 c5 c6",
-    "GV": "a0 a1 a2 c1 c2 c3 c4 c7 b123 b45 b67",
-    "SV": "012",
-    "NA": "012 345 67", "NC": "1234 56 7", "NB": "123 45 67",
-    "HB": "123 45,67",
+    "GS": "a34 a56 c45 c6",
+    "GV": "a0 a1 a2 a7 c1 c2 c3 c7 b123 b45 b67",
+    "SV": "012 7",
+    "NA": "012 3456 7", "NC": "123 456 7", "NB": "123 45 67",
+    "HB": "12,34 567",
     "EARLY": 5, "CE": 6,
-    "ORDER": "PT E7 ga0 SP ga3 st3 S7 ga2 abs0 ga1 sa3 abs3 DIFF abs1 abs2 U0 RC U1 H7 sa0 ga5 RB1 ga4 pack ga6 na0 HC st5 sa5 st4 "
-             "sa4 na3 HB1 gc7 ga7 gc2 gc1 abs4 abs5 SN st6 abs6 gb1 st7 abs7 U4 U6 gc4 nb1 gc3 sa6 RB4 sa7 HB4 gc5 na6 gc6 W0 NT "
-             "nc1 stc6 stc5 sc6 gb4 nb4 gb6 sc5 nc5 NC nb6 nc7 Y1 EARLY Y6 LATE LAST TX P2 Z0 Z1 UZ MK SH RZ SE AR HN DC0 DC1 "
-             "UP0 SC0 PA UP1 SC1",
-    "STATE": "vs", "ROUND": "ss", "LROUND": "vsvs", "RRPE": 0,
+    "ORDER": "H7 SP0 pack DIFF ga3 ga0 ga2 abs0 ga1 st3. ga5 ga7 st3 U0 sa0 abs3 abs4 sa7 RC na7 sa3 HC. HC. na0 HC. abs1 abs2 st5. "
+             "HC. st5 abs7 HC U1 abs5 abs6 gc1 U3 gc7 SN sa5 RB1 U5 gc2 nc7 HB1. gc4 RB5 gc3 na3 HB1. HB5. gc6 W0 HB1. stc4. HB5. "
+             "HB1. stc4 HB5. HB1 nc1 HB5. sc4 gb1 stc6 HB5 NT sc6 nb1 gb4 nc4 gb6 nb4 Y1 NC nb6 EARLY. EARLY. Y6 EARLY LATE LAST "
+             "TX P2. Z0. P2 PA PT. Z0 Z1. MK PT. E7. AR. Z1 UZ SH. PT. E7 AR. PT SH RZ. S7 AR RZ SE HN. DC0 HN. DC1 UP0 SP. HN. "
+             "UP1. SC0. HN. UP1. SC0 UP1 SP HN SC1 PN",
+    "CUT": "16v 16s", "LCUT": "4v 12v 16v", "SENDS": "16v 16s", "LSENDS": "16v 16s", "SS": "", "AGAIN": 0, "MIX": 0, "U16": 0, "PACK": 0, "CHOICE": "v", "MERGE": 1, "MOD": "svv", "AV": "0 12 7",
+    "END": "TX Z0 Z1 P2. AR. P2 AR. MK AR DC0 DC1 SH. UP0 DC2 UP1 SH SC0. SC1. YH SC0 HN. SC1 UP2 YZ HN SC2 YE0 YE1",
 }
 
 
@@ -68,7 +74,7 @@ def rank_program(g, core, T, topo):
                 continue
             if e[0] < hi and lo < e[1] and (wr or e[2]):
                 out.append(e[4])
-            elif buf in BANKS and e[3] != q:
+            elif buf in BANKS and e[3] != q and e[0] // 512 <= (hi - 1) // 512 and lo // 512 <= (e[1] - 1) // 512:
                 out.append(e[4])
         return out
 
@@ -96,7 +102,17 @@ def rank_program(g, core, T, topo):
                 known[q][s] = max(known[q].get(s, 0), v)
             known[q][op[0]] = max(known[q].get(op[0], 0), op[1])
 
+    held = [None]
+
     def emit(q, calls, reads, writes, sem=None, val=None, remote=False, acc=False):
+        if held[0] is None:
+            issue(q, calls, reads, writes, sem, val, remote, acc)
+        else:
+            held[0].append(lambda: issue(q, calls, reads, writes, sem, val, remote, acc))
+
+    ends = []
+
+    def issue(q, calls, reads, writes, sem, val, remote, acc):
         ops = []
         for b, lo, hi in reads:
             ops += need(q, b, lo, hi, False)
@@ -121,7 +137,10 @@ def rank_program(g, core, T, topo):
             note(q, b, lo, hi, False, op)
         for b, lo, hi in writes:
             note(q, b, lo, hi, True, op)
-        return op
+        if sem not in qsem.values():
+            ends.append(op)
+        if remote:
+            note("g", remote[0], remote[1], remote[2], True, (remote[3], val, {remote[3]: val}))
 
     def ap(r):
         if len(r) > 3:
@@ -190,37 +209,48 @@ def rank_program(g, core, T, topo):
     def M(b):
         return (b, 0, 128)
 
+    def pieces(cut):
+        out = []
+        for p in cut.split():
+            c0 = out[-1][1] if out else 0
+            out.append((c0, c0 + int(p[:-1]), p[-1]))
+        return out
+
     TAG[0] = "setup"
     dma("y", T.EFI[:, :], T.ef[:, :], [], [("EFI", 0, 256)], "lde")
     dma("s", T.WI[:, :], T.wt[:, :], [], [("WI", 0, 1)], "ldw")
     dma("y", T.XA0[:, 4096:4608], T.zv[:, :], [], [("XA0", 4096, 4608)], "ldz")
-    dma("s", T.D[:, 2048:4096], T.dv[:, 2048:4096], [], [("D", 2048, 4096)], "ldd1")
-    dma("y", T.D[:, 0:2048], T.dv[:, 0:2048], [], [("D", 0, 2048)], "ldd0")
+    dma("y", T.D[:, :], T.dv[:, :], [], [("D", 0, 4096)], "ldd0")
 
     iota("PI", 0, 1, [[1, 1]], 0, 1, False)
     iota("XI", 0, 144, [[1, 144]], 0, 0, True)
     iota("BJ", 0, 16, [[0, 8], [16, 2]], 0, 0, False)
+    fill(("K4", 0, 224), 32.0, 0, 64)
+    fill(M("ON"), 1.0)
+    fill(("K2", 0, 256), 16.0)
     iota("CTI", 32, 256, [[1, 224]], 2592, 0, True)
     iota("CTI", 0, 32, [[1, 32]], 2832, 0, True)
-    iota("JT", 0, 32, [[128, 32]], 0, 0, False)
-    iota("THR", 0, 224, [[32, 7], [0, 32]], 2592, 0, True)
     I = ("PI", 0, 1)
     XI, XJ = ("XI", 0, 144), ("XI", 0, 128)
     ts(("PJ", 0, 1), I, 112, None, OP.bitwise_and)
     ts(("PJ", 2, 3), I, 3, 1, OP.logical_shift_right, OP.bitwise_and)
     ts(("PJ", 3, 4), I, 7, None, OP.bitwise_and)
     ts(("PJ", 1, 2), I, 15, None, OP.bitwise_and)
-    ts(("PJ", 4, 5), I, 1, None, OP.bitwise_and)
-    ts(("PJ", 5, 6), I, 1, 7, OP.logical_shift_right, OP.bitwise_and)
     copy(("PF", 6, 7), I)
-    copy(("PF", 0, 6), ("PJ", 0, 6))
-    fill(M("ON"), 1.0)
+    copy(("PF", 0, 4), ("PJ", 0, 4))
     ts(("PF", 9, 10), ("PF", 0, 1), ("PF", 2, 3), 14.0, OP.add, OP.add)
     ts(("KM", 0, 8), ("XI", 0, 8), ("PF", 3, 4), None, OP.is_equal)
     ts(("PF", 10, 11), ("PF", 0, 1), 15.0, None, OP.add)
-    fill(("K2", 0, 160), 16.0)
+    MOD = dict(zip("acb", CFG["MOD"]))
+    KM = {w: "K4" if MOD[w] == "v" else "K2" for w in MOD}
     for k in range(8):
         ts(("Q%d" % k, 0, 144), XI, ("PF", 9, 10), ("KM", k, k + 1), OP.is_equal, OP.mult)
+    fill(("K4", 0, 224), 1.0 / 512, 64, 128)
+    ts(M("ID"), XJ, ("PF", 6, 7), None, OP.is_equal)
+    ts(("OL", 0, 144), XI, ("PF", 10, 11), -SC, OP.is_equal, OP.mult)
+    act(("bC", 256, 512), ("CTI", 0, 256), AF.Copy, scale=4096.0)
+    for b, c in (("NG", -1.0), ("IDF", 1.0), ("NGF", -1.0), ("IC", -4.5 * SC), ("IW", 65536.0), ("IB", 4.5 * SC)):
+        act(M(b), M("ID"), AF.Copy, scale=c)
     ts(("EH", 0, 256), ("EFI", 0, 256), -2048.0, None, OP.add)
     copy(("WF", 0, 1), ("WI", 0, 1))
     ts(("BL", 0, 16), ("BJ", 0, 16), ("PF", 1, 2), None, OP.add)
@@ -230,7 +260,7 @@ def rank_program(g, core, T, topo):
         mm((b, 32 * k, 32 * k + 32), [(("Q%d" % k, 14 - 2 * h, 142 - 2 * h), ("EH", h, 256, 8)) for h in range(8)])
 
     def usum(out, XA, lo):
-        mm(out, [(M("ON"), ("K2", 0, 32))] + wrap("WL", XA, lo, lo + 512))
+        mm(out, [(M("ON"), (KM["c" if lo < 4096 else "a"], 0, 32))] + wrap("WL", XA, lo, lo + 512))
     for k in range(8):
         if k == 2:
             usum(("bU", 256, 288), "XA0", 4096)
@@ -246,68 +276,77 @@ def rank_program(g, core, T, topo):
 
     def round_s(src, lo):
         n = src[2] - src[1]
+        w = {0: "a", 256: "c"}.get(lo, "b")
+        RR = ("RH" if w == "b" and CFG["AGAIN"] else "RR", lo, lo + n)
+        if MOD[w] == "v":
+            return ts(RR, src, BIG, -BIG, OP.add, OP.add)
         act(("RX", lo, lo + n), src, AF.Identity, bias=BIG, scale=1.0 + 2.0 ** -22)
-        act(("RR", lo, lo + n), ("RX", lo, lo + n), AF.Identity, bias=-BIG)
+        act(RR, ("RX", lo, lo + n), AF.Identity, bias=-BIG)
 
-    def value_v(src, lo):
-        n = src[2] - src[1]
-        tt(("VF", lo, lo + n), src, ("RR", lo, lo + n), OP.subtract)
+    def value_v(w, src, lo):
+        tt(("V" + w, 0, 32), src, ("RR", lo, lo + 32), OP.subtract)
 
-    def products(EQ, lo, hi):
-        vgather(("PP", lo, hi), ("VF", 0, 32), ("BL", 0, (hi - lo) // 16), (EQ, lo, hi), OP.mult)
+    def products(w, EQ, lo, hi):
+        vgather(("P" + w, lo, hi), ("V" + w, 0, 32), ("BL", 0, (hi - lo) // 16), (EQ, lo, hi), OP.mult)
 
-    def names(lo, hi, sec, ni, lst):
-        tt(("SI", lo, hi), ("PP", lo, hi), ("bK", sec, sec + hi - lo), OP.add)
-        ts((ni, lo, hi), ("SI", lo, hi), 5, 4095, OP.arith_shift_right, OP.bitwise_and)
-        copy((lst, lo, hi), (ni, lo, hi))
+    def names(w, lo, hi, sec):
+        tt(("S" + w, lo, hi), ("P" + w, lo, hi), ("bK", sec, sec + hi - lo), OP.add)
+        if w != "a" and CFG["U16"]:
+            return ts(("L" + w, lo, hi), ("S" + w, lo, hi), 5, 4095, OP.arith_shift_right, OP.bitwise_and)
+        ts(("I" + w, lo, hi), ("S" + w, lo, hi), 5, 4095, OP.arith_shift_right, OP.bitwise_and)
+        copy(("L" + w, lo, hi), ("I" + w, lo, hi))
 
-    ts(M("ID"), XJ, ("PF", 6, 7), None, OP.is_equal)
-    ts(("OL", 0, 144), XI, ("PF", 10, 11), -SC, OP.is_equal, OP.mult)
-    for b, c in (("NG", -1.0), ("IDF", 1.0), ("NGF", -1.0), ("IC", -4.5 * SC), ("IB", 4.5 * SC), ("IW", 65536.0)):
-        act(M(b), M("ID"), AF.Copy, scale=c)
-    act(("OH", 0, 144), ("OL", 0, 144), AF.Copy, scale=0.5)
-    act(("bC", 256, 512), ("CTI", 0, 256), AF.Copy, scale=4096.0)
 
     SIDE = {c: c in CFG["GS"].split() for c in CFG["GS"].split() + CFG["GV"].split()}
     byS = {c[0] + k: s for c, s in SIDE.items() for k in c[1:]}
+    byS.update({"a" + k: True for k in CFG["SS"].replace(" ", "")})
     BIAS = {}
-    for w, c, base in (("a", "NA", 4.5), ("c", "NC", 0.0), ("b", "NB", 0.0)):
+    CE = CFG["CE"]
+    for w, c in (("a", "NA"), ("c", "NC"), ("b", "NB")):
         for grp in CFG[c].split():
             assert len({byS[w + k] for k in grp}) == 1
-            BIAS[w + grp] = base + (-0.5 if byS[w + grp[0]] else 7.5)
+            BIAS[w + grp] = (-4.5 if w == "c" and int(grp[0]) <= CE else 0.0) + (-0.5 if byS[w + grp[0]] else 7.5)
+            if CFG["CHOICE"] == "v":
+                BIAS[w + grp] = (4.5 if w == "a" else 0.0) + (-0.5 if byS[w + grp[0]] else 7.5)
     BCOL = {v: 160 * i for i, v in enumerate(sorted(set(BIAS.values())))}
-    for v, o in BCOL.items():
-        fill(("BT", o, o + 160), v * SC / 64, 0, 64)
-    fill(("BT", 0, 160 * len(BCOL)), SC / 64, 64, 128)
-    fill(M("PB"), 1.0, 0, 64)
-    fill(M("PB"), 0.0, 64, 128)
 
-    def later_constants():
-        fill(("K3", 0, 256), -0.5 / 128)
-        ts(("PF", 11, 12), ("PF", 1, 2), -41472.0, None, OP.add)
-        ts(("PF", 12, 13), ("PF", 1, 2), 8.0, None, OP.mult)
-        ts(("PF", 13, 14), ("PF", 4, 5), 8.0, 7.0, OP.mult, OP.add)
-        ts(("KM", 8, 16), ("XI", 0, 8), ("PF", 5, 6), None, OP.is_equal)
-        for j, m in (("J8", 2047), ("J4", 1023)):
-            ts(("JU", 0, 32), ("JT", 0, 32), m, None, OP.bitwise_and)
-            ts((j, 0, 32), ("JU", 0, 32), ("PF", 12, 13), None, OP.add)
-        tt(("PF", 14, 15), ("PF", 13, 14), ("PF", 0, 1), OP.add)
+    def biases():
+        for v, o in BCOL.items():
+            fill(("BT", o, o + 160), v * SC / 64, 0, 64)
+        fill(("BT", 0, 160 * len(BCOL)), SC / 64, 64, 128)
+        fill(M("PB"), 1.0, 0, 64)
+        fill(M("PB"), 0.0, 64, 128)
+    biases()
+    for j, cut in (("JM", "CUT"), ("JL", "LCUT")):
+        for c0, c1, how in pieces(CFG[cut]):
+            iota(j, c0, c1, [[128, c1 - c0]], 0, 0, False)
+    iota("THR", 0, 224, [[32, 7], [0, 32]], 2592, 0, True)
+    ts(("OH", 0, 144), XI, ("PF", 10, 11), -SC / 2, OP.is_equal, OP.mult)
+    fill(("K3", 0, 256), -0.5 / 128)
+    ts(("PF", 11, 12), ("PF", 1, 2), -41472.0, None, OP.add)
+    ts(("PF", 12, 13), ("PF", 1, 2), 8.0, None, OP.mult)
+    ts(("O16", 0, 144), XI, 0.0, 1.0, OP.mult, OP.add)
 
-    def turn(h):
-        ts(("R%d" % h, 0, 144), XI, ("PF", 14, 15), ("KM", 8 + h, 9 + h), OP.is_equal, OP.mult)
-    later_constants()
+    def slots():
+        for j in ("JM", "JL"):
+            ts((j, 0, 32), (j, 0, 32), ("PF", 12, 13), None, OP.add)
+    for h in range(8):
+        emit("g", [lambda e, h=h: e.affine_select(T["R%d" % h][:, :], T.O16[:, :], [[-16, 9], [-1, 2], [1000, 8]], OP.is_equal, 0.0,
+                                                  -2 * h - 7000, 1)], [("O16", 0, 144)], [("R%d" % h, 0, 144)])
     round_s(("bU", 256, 288), 0)
     act(("EQ0", 0, 128), ("bA", 0, 128), AF.Identity, bias=3232.0)
     second(("bK", 0, 128), ("EQ0", 0, 128))
-    value_v(("bU", 256, 288), 0)
-    products("EQ0", 0, 128)
+    value_v("a", ("bU", 256, 288), 0)
+    products("a", "EQ0", 0, 128)
     act(("EQ0", 128, 256), ("bB", 128, 256), AF.Identity, bias=3232.0)
-    names(0, 128, 0, "NI", "LN")
+    names("a", 0, 128, 0)
+    second(("bK", 128, 256), ("EQ0", 128, 256))
+    products("a", "EQ0", 128, 256)
+    names("a", 128, 256, 128)
+    if not CFG["PACK"]:
+        tt(("NP", 0, 256), ("Ia", 0, 256), ("bC", 256, 512), OP.add)
     REC.append(None)
-    for h in range(8):
-        turn(h)
 
-    ends = []
     for t in range(RO):
         last = t == RO - 1
         XA, XN = "XA%d" % (t % 2), "XA%d" % ((t + 1) % 2)
@@ -333,14 +372,14 @@ def rank_program(g, core, T, topo):
             return (name, 512 * k, 512 * (k + n))
         HG = [[[int(x) for x in s] for s in p.split(",")] for p in CFG["HB"].split()]
         hb = {k: "HB%d" % p[0][0] for p in HG for s in p for k in s}
-        subs = ["st" + (k if c[0] == "a" else c[0] + k) for c in CFG["GS"].split() for k in c[1:]]
+        used, reader = [0], [[], []]
         sign = {}
         spare = [0]
         gets = {}
         for call, s in SIDE.items():
             w, ks = call[0], [int(x) for x in call[1:]]
             k0, n = ks[0], len(ks)
-            G, L = {"a": ("GA", "LN"), "b": ("GB", "LB"), "c": ("GC", "LC")}[w]
+            G, L = "G" + w.upper(), "L" + w
             pre = {"a": [], "c": ["HC"], "b": sorted({hb.get(k) for k in ks})}[w]
             gn = "g%s%d" % (w, k0)
             gets[gn] = [w + str(k) for k in ks]
@@ -351,21 +390,37 @@ def rank_program(g, core, T, topo):
                     DS, o = "DT", spare[0]
                     spare[0] += n
                 add(gn, pre, lambda DS=DS, o=o, n=n, L=L, k0=k0: gcopy("s", blk(DS, o, n), DW, cols(L, k0, n)))
-                for k in ks:
-                    nm = str(k) if w == "a" else w + str(k)
-                    bank = ("bS%d" % (subs.index("st" + nm) % 2), 0, 512)
-                    y = {"a": ZB, "c": xa(0), "b": xa(k)}[w]
-                    add("st" + nm, [gn], lambda bank=bank, d=blk(DS, o + k - k0), y=y: mm(bank, [(M("ID"), d), (M("NG"), y)]))
-                    if w == "a":
-                        add("abs%d" % k, ["st" + nm], lambda k=k, bank=bank: act(xa(k), bank, AF.Abs))
-                    sign[w + str(k)] = "s%s%d" % (w, k)
-                    add("s%s%d" % (w, k), ["st" + nm], lambda k=k, bank=bank, G=G: act(blk(G, k), bank, AF.Sign, bias=-0.5))
+                nm = str(k0) if w == "a" else w + str(k0)
+                b0 = used[0] % 2 if n == 1 else 0
+                used[0] = b0 + n
+                bank = blk("bS", b0, n)
+
+                def do_st(ks=ks, w=w, b0=b0, DS=DS, o=o):
+                    for i, k in enumerate(ks):
+                        mm(blk("bS", b0 + i), [(M("ID"), blk(DS, o + i)), (M("NG"), {"a": ZB, "c": xa(0), "b": xa(k)}[w])])
+                add("st" + nm, [gn] + sorted({x for i in range(n) for x in reader[b0 + i]}), do_st)
+                sg = "s%s%d" % (w, k0)
+                add(sg, ["st" + nm], lambda k0=k0, n=n, bank=bank, G=G: act(blk(G, k0, n), bank, AF.Sign, bias=-0.5))
+                if w == "a":
+                    add("abs%d" % k0, ["st" + nm], lambda k0=k0, n=n, bank=bank: act(xa(k0, n), bank, AF.Abs))
+                for i, k in enumerate(ks):
+                    sign[w + str(k)] = sg
+                    reader[b0 + i] = [sg] + ["abs%d" % k0] * (w == "a")
+                    if w == "a" and i:
+                        add("abs%d" % k, ["abs%d" % k0], lambda: None)
             elif w == "a":
-                add(gn, pre, lambda k0=k0: vgather(blk("XB", k0), DW, cols("LN", k0), ZB, OP.subtract))
-                add("abs%d" % k0, [gn], lambda k0=k0: act(xa(k0), blk("XB", k0), AF.Abs))
+                add(gn, pre, lambda k0=k0: vgather(blk("XB", k0), DW, cols("La", k0), ZB, OP.subtract))
+                grp = [x for x in CFG["AV"].split() if str(k0) in x][0]
+                if int(grp[0]) == k0:
+                    add("abs%d" % k0, ["ga" + x for x in grp], lambda k0=k0, n=len(grp): act(xa(k0, n), blk("XB", k0, n), AF.Abs))
+                else:
+                    add("abs%d" % k0, ["abs" + grp[0]], lambda: None)
                 grp = [x for x in CFG["SV"].split() if str(k0) in x][0]
                 sign[call] = "sa" + grp[0]
-                if int(grp[0]) == k0:
+                if int(grp[0]) == k0 and grp in CFG["SS"].split():
+                    add("sa%d" % k0, ["ga" + x for x in grp],
+                        lambda k0=k0, n=len(grp): act(blk("GA", k0, n), blk("XB", k0, n), AF.Sign, bias=-0.5))
+                elif int(grp[0]) == k0:
                     add("sa%d" % k0, ["ga" + x for x in grp],
                         lambda k0=k0, n=len(grp): ts(blk("GA", k0, n), blk("XB", k0, n), 0.0, None, OP.is_gt))
             else:
@@ -373,9 +428,6 @@ def rank_program(g, core, T, topo):
                 add(gn, pre, lambda G=G, L=L, k0=k0, n=n, y=y: vgather(blk(G, k0, n), DW, cols(L, k0, n), y, OP.is_gt))
                 for k in ks:
                     sign[w + str(k)] = gn
-        for i, o in enumerate(subs[2:]):
-            p = subs[i][2:]
-            tasks[o][0].extend(["abs" + p, "sa" + p] if p.isdigit() else ["s" + p])
         E = CFG["EARLY"]
 
         def cb(k, n):
@@ -396,31 +448,31 @@ def rank_program(g, core, T, topo):
 
         def groups(c, w, lo, hi):
             return ["n" + w + grp[0] for grp in CFG[c].split() if lo <= int(grp[0]) <= hi]
-        add("SN", ["na0"], lambda: act(SN, cols("bA", 0), AF.Sign, bias=-4.5 * SC))
+        add("SN", ["na0"], lambda: act(SN, cols("bA", 0), AF.Sign, bias=-4.5 * SC if CFG["CHOICE"] == "v" else 0.0))
+        add("SP0", [], lambda: None if t else spread_first(EQ))
         add("U0", ["abs0"], lambda: usum(("bM", 288, 320), XA, 3584))
-        add("RC", ["U0"], lambda: round_s(("bM", 288, 320), 0))
+        add("RC", ["U0"], lambda: round_s(("bM", 288, 320), 256))
 
         def do_hc():
-            value_v(("bM", 288, 320), 0)
-            products(EQ, 32, 256)
-            names(32, 256, 32, "HI", "LC")
-        add("HC", ["RC", "H7"], do_hc)
-        k7 = 7 if t else 4
+            value_v("c", ("bM", 288, 320), 256)
+            products("c", EQ, 32, 256)
+            names("c", 32, 256, 32)
+        MG = min(CFG["MERGE"], 1)
+        add("HC", ["RC"] + ([] if MG else ["S7"]), do_hc)
 
         def do_e7():
-            if t:
-                ts(cols("NM", 0), cols("LP%d" % (t - 1), 0), 4095, None, OP.bitwise_and)
-                ts(cols(EQ, 7), cols("NM", 0), 1184.0, None, OP.add)
-        add("E7", [], do_e7)
-        add("S7", ["E7"], lambda: second(cols("bK", k7, 8 - k7), cols(EQ, k7, 8 - k7)))
+            tp, E7 = (t, EN) if MG else (t - 1, EQ)
+            if (not last) if MG else t:
+                ts(cols("NM", 0), cols("LP%d" % tp, 0), 4095, None, OP.bitwise_and)
+                ts(cols(E7, 7), cols("NM", 0), 1184.0, None, OP.add)
+        add("E7", ["TX"] if MG else [], do_e7)
+        add("S7", ["E7"], lambda: second(cols("bK", 7), cols(EN if MG else EQ, 7)) if ((not last) if MG else t) else None)
 
         def do_h7():
-            if t:
-                tt(cols("PP", 7), cols(EQ, 7), cols("VF", 0), OP.mult)
-            else:
-                products(EQ, 128, 256)
-            names(32 * k7, 256, 32 * k7, "NI", "LN")
-        add("H7", ["S7"], do_h7)
+            if t and not MG:
+                tt(cols("Pa", 7), cols(EQ, 7), cols("Va", 0), OP.mult)
+                names("a", 224, 256, 224)
+        add("H7", [] if MG else ["S7"], do_h7)
         for k in range(4, 8):
             tasks[[n for n in gets if "a%d" % k in gets[n]][0]][0].append("H7")
         for i, p in enumerate(HG):
@@ -430,68 +482,124 @@ def rank_program(g, core, T, topo):
                     o = cols(B, s[0], len(s))
                     parts = [x + (o,) for x in wrap("WL", XA, 512 * (s[0] - 1), 512 * s[-1])]
                     if j == 0:
-                        parts = [(M("ON"), ("K2", 0, 32 * n))] + parts
+                        parts = [(M("ON"), (KM["b"], 0, 32 * n))] + parts
                     mm(cols(B, k0, n) if j == 0 else o, parts, j == 0, end)
                 add("U%d" % s[0], ["abs%d" % k for k in s] + (["U%d" % p[j - 1][0]] if j else ["HC"] if i else []), do_u)
 
-            def do_rb(B=B, k0=k0, n=n):
-                round_s(cols(B, k0, n), 32 * k0)
-                if CFG["RRPE"]:
-                    mm(cols(B, k0, n), [(M("NG"), cols("RR", k0, n))], False, True)
-            add("RB%d" % k0, ["U%d" % p[-1][0], "RC"], do_rb)
+            add("RB%d" % k0, ["U%d" % p[-1][0]], lambda B=B, k0=k0, n=n: round_s(cols(B, k0, n), 32 * k0))
 
-            def do_hb(B=B, k0=k0, n=n):
-                if CFG["RRPE"]:
-                    tt(cols("PP", k0, n), ("ER", 0, 32 * n), cols(B, k0, n), OP.mult)
+            def do_hb(B=B, k0=k0, n=n, i=i):
+                if CFG["AGAIN"]:
+                    V = cols(B, 9 + i, n)
+                    mm(V, [(M("ON"), ("K2", 0, 32 * n))] + wrap("WL", XA, 512 * (k0 - 1), 512 * (k0 + n - 1)) + [(M("NG"), cols("RH", k0, n))])
+                    tt(cols("Pb", k0, n), ("ER", 0, 32 * n), V, OP.mult)
+                elif MOD["b"] == "v":
+                    tt(cols("Vb", k0, n), cols(B, k0, n), cols("RR", k0, n), OP.subtract)
+                    vgather(cols("Pb", k0, n), cols(EQ, 0), ("BL", 0, 2 * n), cols("Vb", k0, n), OP.mult)
                 else:
                     tt(cols(B, k0, n), cols(B, k0, n), cols("RR", k0, n), OP.subtract)
-                    tt(cols("PP", k0, n), ("ER", 0, 32 * n), cols(B, k0, n), OP.mult)
-                names(32 * k0, 32 * (k0 + n), 256, "HI", "LB")
-            add("HB%d" % k0, ["RB%d" % k0, "HC"], do_hb)
-        add("pack", ["H7"], lambda: tt(("NP", 0, 256), ("NI", 0, 256), ("bC", 256, 512), OP.add))
-        add("W0", ["pack", "SN"], lambda: mm(("bA", 256, 288), [(M("IDF"), cols("NP", 0)), (M("IW"), SN)]))
-        add("DIFF", ["E7"], lambda: mm(("bA", 288, 512), [(M("IDF"), (EQ, 32, 256)), (M("NGF"), (EQ, 0, 224))]))
+                    tt(cols("Pb", k0, n), ("ER", 0, 32 * n), cols(B, k0, n), OP.mult)
+                names("b", 32 * k0, 32 * (k0 + n), 256)
+            add("HB%d" % k0, ["RB%d" % k0, "SP0"], do_hb)
+        def pack():
+            tt(("NP", 0, 256), ("Ia", 0, 256), ("bC", 256, 512), OP.add)
+        add("pack", ["H7"], lambda: pack() if CFG["PACK"] else None)
+        add("PN", ["HN"], lambda: pack() if not CFG["PACK"] and not last else None)
+        add("DIFF", [] if MG else ["E7"], lambda: mm(("bA", 288, 512), [(M("IDF"), (EQ, 32, 256)), (M("NGF"), (EQ, 0, 224))]))
 
-        CE = CFG["CE"]
-        W0 = ("bA", 256, 288)
-        add("NT", ["pack"] + groups("NA", "a", 0, 7), lambda: tt(cols("NT", 1, 7), cols("bA", 1, 7), cols("NP", 1, 7), OP.max))
-        add("NC", ["NT"] + groups("NC", "c", 1, CE), lambda: tt(cols("NT", 1, CE), cols("bC", 1, CE), cols("NT", 1, CE), OP.max))
-        add("Y1", groups("NB", "b", 1, E), lambda: act(cb(1, E), cb(1, E), AF.Abs))
-        add("Y%d" % (E + 1), groups("NB", "b", E + 1, 7), lambda: act(cb(E + 1, 7 - E), cb(E + 1, 7 - E), AF.Abs))
+        add("FA", groups("NA", "a", 0, 7), lambda: act(cols("FA", 1, 7), cols("bA", 1, 7), AF.Relu))
+        add("FC", groups("NC", "c", 1, CE), lambda: act(cols("FC", 1, CE), cols("bC", 1, CE), AF.Relu))
+        for k0, n in ((1, E), (E + 1, 7 - E)):
+            def do_y(k0=k0, n=n):
+                act(cb(k0, n), cb(k0, n), AF.Abs)
+                act(cols("FY", k0, n), cb(k0, n), AF.Relu, bias=-4.5 * SC)
+            add("Y%d" % k0, groups("NB", "b", k0, k0 + n - 1), do_y)
+
+        def more(b, k0, n):
+            return (M("ID"), cols(b, k0, n), cols("bU", k0, n))
+        add("W0", ["pack", "SN", "HB1"], lambda: mm(cols("bU", 0, 8), [(M("IDF"), cols("NP", 0, 8)), (M("IW"), SN, cols("bU", 0))], True, False))
+        add("W1", ["W0", "FA", "FC", "Y1"], lambda: mm(cols("bU", 1, 7), [more("FA", 1, 7), more("FC", 1, CE), more("FY", 1, E)], False, False))
+        add("W2", ["W1", "Y%d" % (E + 1)], lambda: mm(cols("bU", E + 1, 7 - E), [more("FY", E + 1, 7 - E)], False, True))
+        add("WS", ["W2"], lambda: act(cols("WK", 4, 4), cols("bU", 4, 4), AF.Copy))
 
         def do_early():
-            tt(cols("WK", 1, E), cols("NT", 1, E), cb(1, E), OP.max)
-            h = E // 2
-            tt(cols("TR", 0, h), cols("WK", 1, h), cols("WK", 1 + h, h), OP.min)
-            if E > 4:
-                tt(cols("TR", 3), cols("WK", 5) if E == 5 else cols("TR", 2), W0, OP.min)
-            tt(cols("TR", 5), cols("TR", 0), cols("TR", 1), OP.min)
-            tt(cols("TR", 4), cols("TR", 5), cols("TR", 3) if E > 4 else W0, OP.min)
-        add("EARLY", ["NC", "Y1", "W0"], do_early)
-        best = [cols("TR", 4)]
-
-        def fold(ks, end):
-            items = [cols("WK", k) for k in ks] + best
-            i = 0
-            while len(items) > 1:
-                out = end if len(items) == 2 and end else cols("TR", (5, 6, 7)[i])
-                tt(out, items[0], items[1], OP.min)
-                items = items[2:] + [out]
-                i += 1
-            best[0] = items[0]
-
-        def do_late():
-            tt(cols("WK", E + 1, 7 - E), cols("NT", E + 1, 7 - E), cb(E + 1, 7 - E), OP.max)
-            fold(range(E + 1, CE + 1), cols(PKS, 0) if CE == 7 else cols("TR", 0))
-        add("LATE", ["EARLY", "Y%d" % (E + 1)], do_late)
+            if CE == 5:
+                tt(cols("TR", 0, 2), cols("bU", 0, 2), cols("WK", 4, 2), OP.min)
+                tt(cols("TR", 2, 2), cols("bU", 2, 2), cols("TR", 0, 2), OP.min)
+            elif CE == 6:
+                tt(cols("TR", 0, 3), cols("bU", 1, 3), cols("WK", 4, 3), OP.min)
+                tt(cols("TR", 3), cols("bU", 0), cols("TR", 0), OP.min)
+                tt(cols("TR", 4), cols("TR", 1), cols("TR", 2), OP.min)
+                tt(cols("TR", 5), cols("TR", 3), cols("TR", 4), OP.min)
+            else:
+                tt(cols("TR", 0, 4), cols("bU", 0, 4), cols("WK", 4, 4), OP.min)
+        add("EARLY", ["WS"], do_early)
 
         def do_last():
             if CE < 7:
                 tt(cols("WK", CE + 1, 7 - CE), cols("WK", CE + 1, 7 - CE), cols("bC", CE + 1, 7 - CE), OP.max)
-                fold(range(CE + 1, 8), cols(PKS, 0))
+            if CE == 6:
+                tt(cols(PKS, 0), cols("WK", 7), cols("TR", 5), OP.min)
+            else:
+                tt(cols("TR", 4, 2), cols("TR", 2, 2), cols("WK", 6, 2) if CE == 5 else cols("TR", 0, 2), OP.min)
+                tt(cols(PKS, 0), cols("TR", 4), cols("TR", 5), OP.min)
             ts(cols("TS", 0), cols(PKS, 0), 12, None, OP.arith_shift_right)
             ts(cols("LS", 0), cols("TS", 0), 16.0, ("PF", 11, 12), OP.mult, OP.add)
-        add("LAST", ["LATE"] + groups("NC", "c", CE + 1, 7), do_last)
+        add("LAST", ["EARLY"] + groups("NC", "c", CE + 1, 7), do_last)
+        if CFG["CHOICE"] == "v":
+            for n in ("FA", "FC", "W1", "W2", "WS", "EARLY", "LAST"):
+                del tasks[n]
+            W0 = ("bA", 256, 288)
+            cw = [cb]
+            add("W0", ["pack", "SN"], lambda: mm(W0, [(M("IDF"), cols("NP", 0)), (M("IW"), SN)]))
+            add("NT", ["pack"] + groups("NA", "a", 0, 7), lambda: tt(cols("NT", 1, 7), cols("bA", 1, 7), cols("NP", 1, 7), OP.max))
+            add("NC", ["NT"] + groups("NC", "c", 1, CE), lambda: tt(cols("NT", 1, CE), cols("bC", 1, CE), cols("NT", 1, CE), OP.max))
+            add("Y1", groups("NB", "b", 1, E), lambda: act(cb(1, E), cb(1, E), AF.Abs))
+            add("Y%d" % (E + 1), groups("NB", "b", E + 1, 7), lambda: act(cb(E + 1, 7 - E), cb(E + 1, 7 - E), AF.Abs))
+
+            def v_early():
+                tt(cols("WK", 1, E), cols("NT", 1, E), cw[0](1, E), OP.max)
+                h = E // 2
+                tt(cols("TR", 0, h), cols("WK", 1, h), cols("WK", 1 + h, h), OP.min)
+                if E > 4:
+                    tt(cols("TR", 3), cols("WK", 5) if E == 5 else cols("TR", 2), W0, OP.min)
+                tt(cols("TR", 5), cols("TR", 0), cols("TR", 1), OP.min)
+                tt(cols("TR", 4), cols("TR", 5), cols("TR", 3) if E > 4 else W0, OP.min)
+            add("EARLY", ["NC", "Y1", "W0"], v_early)
+            best = [cols("TR", 4)]
+
+            def fold(ks, end):
+                items = [cols("WK", k) for k in ks] + best
+                i = 0
+                while len(items) > 1:
+                    out = end if len(items) == 2 and end else cols("TR", (5, 6, 7)[i])
+                    tt(out, items[0], items[1], OP.min)
+                    items = items[2:] + [out]
+                    i += 1
+                best[0] = items[0]
+
+            def v_late():
+                tt(cols("WK", E + 1, 7 - E), cols("NT", E + 1, 7 - E), cw[0](E + 1, 7 - E), OP.max)
+                fold(range(E + 1, CE + 1), cols(PKS, 0) if CE == 7 else cols("TR", 0))
+            add("LATE", ["EARLY", "Y%d" % (E + 1)], v_late)
+
+            def v_last():
+                if CE < 7:
+                    tt(cols("WK", CE + 1, 7 - CE), cols("WK", CE + 1, 7 - CE), cols("bC", CE + 1, 7 - CE), OP.max)
+                    fold(range(CE + 1, 8), cols(PKS, 0))
+                ts(cols("TS", 0), cols(PKS, 0), 12, None, OP.arith_shift_right)
+                ts(cols("LS", 0), cols("TS", 0), 16.0, ("PF", 11, 12), OP.mult, OP.add)
+            add("LAST", ["LATE"] + groups("NC", "c", CE + 1, 7), v_last)
+            if CFG["MIX"]:
+                W0 = cols("bU", 0)
+                add("NT", groups("NA", "a", 0, 7), lambda: act(cols("FA", 1, 7), cols("bA", 1, 7), AF.Relu, bias=-4.5 * SC))
+                add("NC", groups("NC", "c", 1, CE), lambda: act(cols("FC", 1, CE), cols("bC", 1, CE), AF.Relu, bias=-4.5 * SC))
+                add("W0", ["pack", "SN", "HB1"], lambda: mm(cols("bU", 0, 8), [(M("IDF"), cols("NP", 0, 8)), (M("IW"), SN, cols("bU", 0))], True, False))
+                add("W1", ["W0", "NT", "NC"], lambda: mm(cols("bU", 1, 7), [more("FA", 1, 7), more("FC", 1, CE)], False, True))
+                for k0, n in ((1, E), (E + 1, 7 - E)):
+                    add("Y%d" % k0, groups("NB", "b", k0, k0 + n - 1), lambda k0=k0, n=n: act(cols("NT", k0, n), cb(k0, n), AF.Abs))
+                tasks["EARLY"][0].append("W1")
+                cw = [lambda k, n: cols("bU", k, n)]
 
         dst = T.cores[(rank + 1 + t % (N - 1)) % N]
         rid, pid = topo.addr(dst)[0], topo.addr(dst)[1]
@@ -499,26 +607,30 @@ def rank_program(g, core, T, topo):
         ne = len(topo.engines(core, dst))
 
         def send(out, in_, rsem, lsem):
-            ends.append(emit("g", [lambda e: e.remote_dma(ap(out), ap(in_), T.sem[rsem], T.sem[lsem], pid, rid, mask)],
-                             [reg(in_)], [], sem=lsem, val=ne, remote=out))
-            note("g", out[0], out[1], out[2], True, (rsem, ne, {rsem: ne}))
+            emit("g", [lambda e: e.remote_dma(ap(out), ap(in_), T.sem[rsem], T.sem[lsem], pid, rid, mask)],
+                 [reg(in_)], [], sem=lsem, val=ne, remote=out + (rsem,))
         LP, LZ = "LP%d" % t, "LZ%d" % t
 
         def later(fn):
             return (lambda: None) if last else fn
         add("TX", ["LAST"], lambda: send(cols(LP, 0), cols(PKS, 0), "an%d" % t, "ln%d" % t))
-        for h, (a, l) in enumerate((("az", "lz"), ("ay", "ly"))):
-            def do_z(h=h, a=a, l=l):
-                Z = (XN, 4096 + 256 * h, 4352 + 256 * h)
-                gcopy(CFG["STATE"][h], Z, (XA, 0, 4608), ("LS", 16 * h, 16 * h + 16))
-                send((LZ, 256 * h, 256 * h + 256), Z, "%s%d" % (a, t), "%s%d" % (l, t))
-            add("Z%d" % h, ["TX"] + ["Z0"] * h, do_z)
+        SENT = pieces(CFG["LSENDS" if last else "SENDS"])
+        for h, (c0, c1, how) in enumerate(SENT):
+            def do_z(h=h, c0=c0, c1=c1, how=how):
+                Z = (XN, 4096 + 16 * c0, 4096 + 16 * c1)
+                gcopy(how, Z, (XA, 0, 4608), ("LS", c0, c1))
+                if not CFG.get("ONE"):
+                    send((LZ, 16 * c0, 16 * c1), Z, "az%d_%d" % (t, h), "lz%d_%d" % (t, h))
+                elif h:
+                    send((LZ, 0, 512), (XN, 4096, 4608), "az%d_%d" % (t, h), "lz%d_%d" % (t, h))
+            add("Z%d" % h, ["TX"] + ["Z%d" % (h - 1)] * (h > 0), do_z)
+        ZL = "Z%d" % (len(SENT) - 1)
 
         def do_p2():
             ts(cols("S0", 0), cols("TS", 0), 2816.0, 512.0, OP.is_ge, OP.mult)
             tt(cols("P2", 0), cols("TS", 0), cols("S0", 0), OP.subtract)
         add("P2", ["LAST"], do_p2)
-        add("UZ", ["Z1"], later(lambda: usum(("bU", 256, 288), XN, 4096)))
+        add("UZ", [ZL], later(lambda: usum(("bU", 256, 288), XN, 4096)))
         add("PA", ["P2"], later(lambda: mm(("bM", 256, 288), [(M("ON"), cols("S0", 0))])))
         add("MK", ["P2"], lambda: vgather(("MK", 0, 224), cols("P2", 0), ("BL", 0, 14), ("THR", 0, 224), OP.is_lt))
         add("RZ", ["UZ"], later(lambda: round_s(("bU", 256, 288), 0)))
@@ -527,55 +639,97 @@ def rank_program(g, core, T, topo):
             tt(("bA", 288, 512), ("bA", 288, 512), ("MK", 0, 224), OP.mult)
             tt((EN, 0, 224), ("bA", 288, 512), (EQ, 0, 224), OP.add)
         add("SH", ["MK", "DIFF"], do_sh)
-        add("SE", ["SH"], later(lambda: second(("bK", 0, 224), (EN, 0, 224))))
+        if CFG["MERGE"] == 2:
+            add("SE", ["SH", "E7"], later(lambda: second(("bK", 0, 256), (EN, 0, 256))))
+            add("S7", ["SE"], lambda: None)
+        else:
+            add("SE", ["SH"], later(lambda: second(("bK", 0, 224), (EN, 0, 224))))
 
         def do_hn():
             if last:
-                ts(("EH", 0, 224), (EN, 0, 224), -3232.0, None, OP.add)
                 ts(cols("NM", 0), cols(LP, 0), 4095, None, OP.bitwise_and)
                 ts(cols("EH", 7), cols("NM", 0), -2048.0, None, OP.add)
             else:
-                value_v(("bU", 256, 288), 0)
-                products(EN, 0, 224)
-                names(0, 224, 0, "NI", "LN")
-        add("HN", ["SE", "RZ"], do_hn)
-        J, nq = ("J4", 4) if last else ("J8", 2)
+                value_v("a", ("bU", 256, 288), 0)
+                n = 256 if CFG["MERGE"] in (1, 2) else 224
+                products("a", EN, 0, n)
+                if CFG["MERGE"] == 4:
+                    tt(("Sa", 0, n), ("Pa", 0, n), ("bK", 0, n), OP.add)
+                else:
+                    names("a", 0, n, 0)
+        add("HN", ["SE", "RZ"] + ["S7"] * (CFG["MERGE"] in (1, 2)), do_hn)
 
+        def do_h8():
+            tt(cols("Pa", 7), cols(EN, 7), cols("Va", 0), OP.mult)
+            if CFG["MERGE"] == 3:
+                names("a", 224, 256, 224)
+            else:
+                tt(cols("Sa", 7), cols("Pa", 7), cols("bK", 7), OP.add)
+                ts(("Ia", 0, 256), ("Sa", 0, 256), 5, 4095, OP.arith_shift_right, OP.bitwise_and)
+                copy(("La", 0, 256), ("Ia", 0, 256))
+        if CFG["MERGE"] > 2:
+            add("H8", ["HN", "S7"], later(do_h8))
+            tasks["PN"][0].append("H8")
+            if MOD["a"] == "v":
+                add("S7", ["E7"], later(lambda: ts(cols("bK", 7), cols(EN, 7), 2080.0, -6722560.0, OP.mult, OP.add)))
         def do_ar():
+            if not t:
+                slots()
             ts(cols("CI", 0), cols(LP, 0), 7, None, OP.bitwise_and)
-            tt(cols("CJ", 0), cols("CI", 0), cols(J, 0), OP.add)
+            tt(cols("CJ", 0), cols("CI", 0), cols("JL" if last else "JM", 0), OP.add)
             copy(cols("LD", 0), cols("CJ", 0))
         add("AR", ["TX"], do_ar)
-        WQ, SQ, CQ = 4096 // nq, 512 // nq, 32 // nq
-        RND = CFG["LROUND"] if last else CFG["ROUND"]
-        for h in range(2):
-            parts = [(q, (SQ * q, SQ * q + SQ), (WQ * q, WQ * q + WQ), (CQ * q, CQ * q + CQ), ("bS0", "bS1", "bK", "bU")[q])
-                     for q in range(h * nq // 2, (h + 1) * nq // 2)]
+        for q, (c0, c1, how) in enumerate(pieces(CFG["LCUT" if last else "CUT"])):
+            R, W, C = (16 * c0, 16 * c1), ("D", 128 * c0, 128 * c1), ("LD", c0, c1)
+            b, o = (("bS", 0), ("bS", 512), ("bB", 0))[q % 3]
+            b = (b, o, o + 16 * (c1 - c0))
 
-            def do_dc(parts=parts):
-                for q, R, W, C, b in parts:
-                    gcopy("s", ("DC",) + R, ("D",) + W, ("LD",) + C)
+            def do_up(R=R, b=b, how=how):
+                extra = [(M("ON"), ("K3", 0, b[2] - b[1]))] if how == "s" else []
+                mm(b, extra + [(M("ID"), ("DC",) + R), (M("ID"), (LZ,) + R)])
+                if how == "s":
+                    act(("FX",) + R, b, AF.Identity, bias=MID, scale=0.5)
+                    act(("FB",) + R, ("FX",) + R, AF.Identity, bias=-MID)
 
-            def do_up(parts=parts):
-                for q, R, W, C, b in parts:
-                    extra = [(M("ON"), ("K3", 0, SQ))] if RND[q] == "s" else []
-                    mm((b, 0, SQ), extra + [(M("ID"), ("DC",) + R), (M("ID"), (LZ,) + R)])
-                    if RND[q] == "s":
-                        act(("FX",) + R, (b, 0, SQ), AF.Identity, bias=MID, scale=0.5)
-                        act(("FB",) + R, ("FX",) + R, AF.Identity, bias=-MID)
+            def do_sc(q=q, R=R, W=W, C=C, b=b, how=how):
+                F = ("FB",) + R if how == "s" else ("FL",) + R
+                if how == "v":
+                    ts(F, b, 0.5, -0.25, OP.mult, OP.add)
+                emit("v", [lambda e: e.tensor_copy(ap(W).indirect(ap(C)), ap(F))], [F, C], [W])
+                if last:
+                    dma("y", T.yd[:, W[1]:W[2]], ap(W), [W], [], "sd%d" % q)
+            add("DC%d" % q, ["AR"], lambda R=R, W=W, C=C: gcopy("s", ("DC",) + R, W, C))
+            add("UP%d" % q, ["DC%d" % q, ZL if CFG.get("ONE") else "Z%d" % min(h for h, p in enumerate(SENT) if c1 <= p[1])], do_up)
+            add("SC%d" % q, ["UP%d" % q], do_sc)
+        if last:
+            add("YZ", [ZL], lambda: dma("s", T.yz[:, :], T[XN][:, 4096:4608], [(XN, 4096, 4608)], [], "sz"))
 
-            def do_sc(parts=parts):
-                for q, R, W, C, b in parts:
-                    F = ("FB",) + R if RND[q] == "s" else ("FL",) + R
-                    if RND[q] == "v":
-                        ts(F, (b, 0, SQ), 0.5, -0.25, OP.mult, OP.add)
-                    emit("v", [lambda e, F=F, W=W, C=C: e.tensor_copy(ap(("D",) + W).indirect(ap(("LD",) + C)), ap(F))],
-                         [F, ("LD",) + C], [("D",) + W])
-                    if last:
-                        ends.append(dma("y", T.yd[:, W[0]:W[1]], ap(("D",) + W), [("D",) + W], [], "sd%d" % q))
-            add("DC%d" % h, ["AR"], do_dc)
-            add("UP%d" % h, ["DC%d" % h, "Z%d" % h], do_up)
-            add("SC%d" % h, ["UP%d" % h], do_sc)
+            def back(ks):
+                return [(("R%d" % h, 7 - k, 135 - k), cols("EH", k), ("bU", h, 256, 8)) for k in ks for h in range(8)]
+
+            def do_ye0():
+                ts(("EH", 0, 224), (EN, 0, 224), -3232.0, None, OP.add)
+                for k in range(7):
+                    mm(cols("bU", 0, 8), [(M("ON"), ("K2", 0, 256))] * (k == 0) + back([k]), k == 0, False)
+
+            def do_ye1():
+                mm(cols("bU", 0, 8), back([7]), False, True)
+                act(("YE", 0, 256), cols("bU", 0, 8), AF.Copy)
+                dma("s", T.ye[:, :], T.YE[:, :], [("YE", 0, 256)], [], "se")
+            def do_ye(h0):
+                b = ("bM", "bU")[h0 // 4]
+                for h in range(h0, h0 + 4):
+                    mm(cols(b, h), [(("R%d" % h, 7 - k, 135 - k), cols("EH", k)) for k in range(8)])
+                for h in range(h0, h0 + 4):
+                    act(("YE", h, 256, 8), cols(b, h), AF.Identity, bias=2048.0)
+                if h0:
+                    dma("s", T.ye[:, :], T.YE[:, :], [("YE", 0, 256)], [], "se")
+            add("YH", ["SH"], lambda: ts(("EH", 0, 224), (EN, 0, 224), -3232.0, None, OP.add))
+            add("YE0", ["HN", "YH"], lambda: do_ye(0))
+            add("YE1", ["YE0"], lambda: do_ye(4))
+            ORDER = ORDER[:ORDER.index("LAST") + 1] + CFG["END"].split()
+            for n in set(tasks) - set(ORDER) - {o.strip(".") for o in ORDER}:
+                del tasks[n]
 
         def do_pt():
             emit("s", [lambda e: e.activation(T.AJ[:, 0:32], T.bM[:, 256:288], AF.Copy, scale=1.0 / 512, accum_out=T.AR[:, 0:1])],
@@ -584,28 +738,35 @@ def rank_program(g, core, T, topo):
             act(("AR", 2, 3), ("AR", 1, 2), AF.Identity, bias=2 * MID, scale=-2.0)
             emit("s", [lambda e: e.activation(T.PB[64:128, :], T.ON[64:128, :], AF.Abs, bias=T.AR[64:128, 0:1], scale=T.AR[64:128, 2:3])],
                  [M("ON"), ("AR", 0, 3)], [M("PB")])
-        add("PT", [], do_pt if t else lambda: None)
-        add("SP", [], lambda: spread_first(EQ))
-        for n in tasks:
-            tasks[n][0].extend({"na": ["PT"], "HB": ["SP"]}.get(n[:2], []))
+        if not last:
+            add("PT", ["PA"], do_pt)
+            add("SP", ["SH"], lambda: spread_first(EN))
 
-        assert sorted(ORDER) == sorted(tasks), set(tasks) ^ set(ORDER)
-        done = []
-        while len(done) < len(ORDER):
-            nm = [x for x in ORDER if x not in done and all(p in done for p in tasks[x][0])][0]
-            TAG[0] = nm
+        whole = [o for o in ORDER if o[-1] != "."]
+        assert sorted(whole) == sorted(tasks), set(tasks) ^ set(whole)
+        steps = {}
+        for nm in tasks:
+            held[0] = steps[nm] = []
             tasks[nm][1]()
-            done.append(nm)
-        TAG[1:] = [" ".join(done), {n: tasks[n][0] for n in tasks}]
+        held[0] = None
+        done = []
+        if t == 1:
+            TAG[2:] = [{n: list(tasks[n][0]) for n in tasks}]
+        for n in tasks:
+            tasks[n][0][:] = [p for p in tasks[n][0] if p in tasks]
+        todo = list(ORDER)
+        while todo:
+            o = [x for x in todo if all(p in done for p in tasks[x.strip(".")][0])][0]
+            todo.remove(o)
+            tasks[o.strip(".")][0][:] = []
+            nm = o.strip(".")
+            TAG[0] = nm
+            for _ in range(min(len(steps[nm]), 1) if o != nm else len(steps[nm])):
+                steps[nm].pop(0)()
+            done.append(o)
+        if t == 1:
+            TAG[1:2] = [" ".join(done)]
         TAG[0] = "end"
         REC.append(None)
-        if last:
-            ends.append(dma("s", T.yz[:, :], T[XN][:, 4096:4608], [(XN, 4096, 4608)], [], "sz"))
-            for h in range(8):
-                b = ("bM", "bB")[h // 4]
-                mm(cols(b, h), [(("R%d" % h, 7 - k, 135 - k), cols("EH", k)) for k in range(8)])
-            for h in range(8):
-                act(("YE", h, 256, 8), cols(("bM", "bB")[h // 4], h), AF.Identity, bias=2048.0)
-            ends.append(dma("s", T.ye[:, :], T.YE[:, :], [("YE", 0, 256)], [], "se"))
     settle("g", ends)
     settle("g", [(qsem[q], cnt[q], {}) for q in "vstg"])

from concourse.mybir import dt, AluOpType, AxisListType, ActivationFunctionType

OP = AluOpType
AF = ActivationFunctionType
RO = 4
BIG = 1.5 * 2.0 ** 35
MID = 1.5 * 2.0 ** 23
SC = 1.25 * 2.0 ** 21
B2, B4, H2, I4, U2 = "bfloat16", "float32", "float16", "int32", "uint16"
SCRATCH = {}
for _n, _w, _d in (("D", 4096, B2), ("XA0", 4608, B2), ("XA1", 4608, B2), ("XB", 4096, B2), ("GA", 4096, B2), ("GB", 4096, B2),
                   ("GC", 4096, B2), ("DS", 4096, B2), ("DT", 2048, B2), ("DC", 512, B2), ("FL", 512, I4),
                   ("LS", 32, U2), ("LD", 32, U2), ("BL", 16, U2), ("EQ0", 256, B4), ("EQ1", 256, B4), ("Va", 32, I4), ("Vc", 32, I4), ("Vb", 256, I4), ("K4", 224, B2),
                   ("NP", 256, B4), ("NT", 256, B4), ("FA", 256, B2), ("FC", 256, B2), ("FY", 256, B2), ("WK", 256, B4), ("TR", 256, B4), ("SN", 32, B2), ("PKS0", 32, I4), ("PKS1", 32, I4), ("TS", 32, I4),
                   ("S0", 32, B2), ("P2", 32, B4), ("ER", 256, B4), ("MK", 256, B4), ("AR", 8, B4), ("AJ", 32, B4), ("NM", 32, I4),
                   ("CI", 32, I4), ("CJ", 32, I4), ("BT", 960, B2), ("PB", 128, B2), ("JM", 32, I4), ("JL", 32, I4), ("BJ", 16, I4),
                   ("ID", 128, B2), ("NG", 128, B2), ("IDF", 128, B4), ("NGF", 128, B4), ("ON", 128, B2), ("IC", 128, B2),
                   ("IB", 128, B2), ("IW", 128, B2), ("OL", 144, B2), ("OH", 144, B2), ("WL", 144, B2), ("XI", 144, B2),
                   ("CTI", 256, B4), ("THR", 224, B4), ("PI", 8, I4), ("PJ", 16, I4), ("PF", 32, B4), ("KM", 16, B4),
                   ("WI", 1, I4), ("WF", 1, B4), ("EFI", 256, I4), ("EH", 256, H2), ("O16", 144, H2), ("K2", 256, B2),
                   ("K3", 256, B2), ("RX", 288, B4), ("RR", 288, B4), ("RH", 256, B2), ("FX", 512, B4), ("FB", 512, B2), ("YE", 256, B4)):
    SCRATCH[_n] = ("sbuf", [128, _w], _d)
for _n in "abc":
    for _w, _d in (("P", B4), ("S", I4), ("I", I4), ("L", U2)):
        SCRATCH[_w + _n] = ("sbuf", [128, 256], _d)
for _n in ("bK", "bU", "bA", "bB", "bC", "bM"):
    SCRATCH[_n] = ("psum", [128, 512], B4)
SCRATCH["bS"] = ("psum", [128, 1024], B4)
for _k in range(8):
    SCRATCH["Q%d" % _k] = ("sbuf", [128, 144], H2)
    SCRATCH["R%d" % _k] = ("sbuf", [128, 144], H2)
for _t in range(RO):
    SCRATCH["LP%d" % _t] = ("sbuf", [128, 32], I4)
    SCRATCH["LZ%d" % _t] = ("sbuf", [128, 512], B2)
SEMAPHORES = (["qv", "qs", "qt", "qg"] + ["ldz", "lde", "ldw", "ldd0", "se", "sz"] + ["sd%d" % _k for _k in range(8)]
              + ["%s%d" % (n, t) for t in range(RO) for n in ("an", "ln")]
              + ["%s%d_%d" % (n, t, h) for t in range(RO) for n in ("az", "lz") for h in range(5)])
TAG = ["", "", ""]
REC = []

CFG = {
    "GS": "a34 a56 c45 c6",
    "GV": "a0 a1 a2 a7 c1 c2 c3 c7 b123 b45 b67",
    "SV": "012 7",
    "NA": "012 3456 7", "NC": "123 456 7", "NB": "123 45 67",
    "HB": "12,34 567",
    "EARLY": 5, "CE": 6,
    "ORDER": "H7 SP0 pack DIFF ga3 ga0 ga2 abs0 ga1 st3. ga5 ga7 st3 U0 sa0 abs3 abs4 sa7 RC na7 sa3 HC. HC. na0 HC. abs1 abs2 st5. "
             "HC. st5 abs7 HC U1 abs5 abs6 gc1 U3 gc7 SN sa5 RB1 U5 gc2 nc7 HB1. gc4 RB5 gc3 na3 HB1. HB5. gc6 W0 HB1. stc4. HB5. "
             "HB1. stc4 HB5. HB1 nc1 HB5. sc4 gb1 stc6 HB5 NT sc6 nb1 gb4 nc4 gb6 nb4 Y1 NC nb6 EARLY. EARLY. Y6 EARLY LATE LAST "
             "TX P2. Z0. P2 PA PT. Z0 Z1. MK PT. E7. AR. Z1 UZ SH. PT. E7 AR. PT SH RZ. S7 AR RZ SE HN. DC0 HN. DC1 UP0 SP. HN. "
             "UP1. SC0. HN. UP1. SC0 UP1 SP HN SC1 PN",
    "CUT": "16v 16s", "LCUT": "4v 12v 16v", "SENDS": "16v 16s", "LSENDS": "16v 16s", "SS": "", "AGAIN": 0, "MIX": 0, "U16": 0, "PACK": 0, "CHOICE": "v", "MERGE": 1, "MOD": "svv", "AV": "0 12 7",
    "END": "TX Z0 Z1 P2. AR. P2 AR. MK AR DC0 DC1 SH. UP0 DC2 UP1 SH SC0. SC1. YH SC0 HN. SC1 UP2 YZ HN SC2 YE0 YE1",
}


def rank_program(g, core, T, topo):
    rank = T.rank_of(core)
    if rank is None:
        return
    N = len(T.cores)
    eng = {"v": g.vector, "s": g.scalar, "t": g.tensor, "g": g, "y": g.sync}
    qsem = {"v": "qv", "s": "qs", "t": "qt", "g": "qg"}
    cnt = {"v": 0, "s": 0, "t": 0, "g": 0}
    known = {q: {} for q in eng}
    log = {}
    BANKS = [b for b in SCRATCH if SCRATCH[b][0] == "psum"]

    def need(q, buf, lo, hi, wr, acc=False):
        out = []
        for e in log.get(buf, []):
            if acc and e[3] == q:
                continue
            if e[0] < hi and lo < e[1] and (wr or e[2]):
                out.append(e[4])
            elif buf in BANKS and e[3] != q and e[0] // 512 <= (hi - 1) // 512 and lo // 512 <= (e[1] - 1) // 512:
                out.append(e[4])
        return out

    def note(q, buf, lo, hi, wr, op):
        keep = []
        for e in log.get(buf, []):
            covered = lo <= e[0] and e[1] <= hi
            if covered and (wr or (not e[2] and e[3] == q)):
                continue
            keep.append(e)
        keep.append([lo, hi, wr, q, op])
        log[buf] = keep

    def settle(q, ops):
        best = {}
        for op in ops:
            if known[q].get(op[0], 0) < op[1]:
                if op[0] not in best or best[op[0]][1] < op[1]:
                    best[op[0]] = op
        for op in sorted(best.values(), key=lambda o: -len(o[2])):
            if known[q].get(op[0], 0) >= op[1]:
                continue
            eng[q].wait_ge(T.sem[op[0]], op[1])
            for s, v in op[2].items():
                known[q][s] = max(known[q].get(s, 0), v)
            known[q][op[0]] = max(known[q].get(op[0], 0), op[1])

    held = [None]

    def emit(q, calls, reads, writes, sem=None, val=None, remote=False, acc=False):
        if held[0] is None:
            issue(q, calls, reads, writes, sem, val, remote, acc)
        else:
            held[0].append(lambda: issue(q, calls, reads, writes, sem, val, remote, acc))

    ends = []

    def issue(q, calls, reads, writes, sem, val, remote, acc):
        ops = []
        for b, lo, hi in reads:
            ops += need(q, b, lo, hi, False)
        for b, lo, hi in writes:
            ops += need(q, b, lo, hi, True, acc)
        settle(q, ops)
        ins = None
        REC.append((TAG[0], q, reads, writes, acc, remote, []))
        for c in calls:
            ins = c(eng[q])
            REC[-1][-1].append(ins)
        snap = dict(known[q])
        if sem is None:
            cnt[q] += 1
            sem, val = qsem[q], cnt[q]
            ins.then_inc(T.sem[sem], 1)
        elif not remote:
            ins.then_inc(T.sem[sem], val)
        snap[sem] = max(snap.get(sem, 0), val)
        op = (sem, val, snap)
        for b, lo, hi in reads:
            note(q, b, lo, hi, False, op)
        for b, lo, hi in writes:
            note(q, b, lo, hi, True, op)
        if sem not in qsem.values():
            ends.append(op)
        if remote:
            note("g", remote[0], remote[1], remote[2], True, (remote[3], val, {remote[3]: val}))

    def ap(r):
        if len(r) > 3:
            return T[r[0]][:, r[1]:r[2]:r[3]]
        return T[r[0]][:, r[1]:r[2]]

    def reg(r):
        return (r[0], r[1], r[2])

    def copy(out, in_):
        emit("v", [lambda e: e.tensor_copy(ap(out), ap(in_))], [reg(in_)], [reg(out)])

    def tt(out, a, b, op):
        emit("v", [lambda e: e.tensor_tensor(ap(out), ap(a), ap(b), op)], [reg(a), reg(b)], [reg(out)])

    def ts(out, a, s1, s2, op0, op1=None):
        rd = [reg(a)] + [reg(s) for s in (s1, s2) if isinstance(s, tuple)]
        x1 = ap(s1) if isinstance(s1, tuple) else s1
        x2 = ap(s2) if isinstance(s2, tuple) else s2
        if op1 is None:
            emit("v", [lambda e: e.tensor_scalar(ap(out), ap(a), x1, None, op0)], rd, [reg(out)])
        else:
            emit("v", [lambda e: e.tensor_scalar(ap(out), ap(a), x1, x2, op0, op1)], rd, [reg(out)])

    def fill(out, c, p0=0, p1=128):
        emit("v", [lambda e: e.memset(T[out[0]][p0:p1, out[1]:out[2]], c)], [], [reg(out)], acc=p0 > 0)

    def act(out, in_, func, bias=0.0, scale=1.0):
        rd = [reg(x) for x in (in_, bias, scale) if isinstance(x, tuple)]
        b = ap(bias) if isinstance(bias, tuple) else bias
        k = ap(scale) if isinstance(scale, tuple) else scale
        emit("s", [lambda e: e.activation(ap(out), ap(in_), func, bias=b, scale=k)], rd, [reg(out)])

    def vgather(out, win, off, in1, op):
        emit("v", [lambda e: e.tensor_tensor(ap(out), ap(win).indirect(ap(off)), ap(in1), op)],
             [reg(win), reg(off), reg(in1)], [reg(out)])

    def gcopy(q, out, win, off):
        if q == "v":
            emit("v", [lambda e: e.tensor_copy(ap(out), ap(win).indirect(ap(off)))], [reg(win), reg(off)], [reg(out)])
        else:
            emit("s", [lambda e: e.activation(ap(out), ap(win).indirect(ap(off)), AF.Copy)], [reg(win), reg(off)], [reg(out)])

    def mm(out, parts, start=True, stop=True):
        n = len(parts)
        calls = []
        rd = []
        for i, p in enumerate(parts):
            rd += [reg(p[0]), reg(p[1])]
            o = p[2] if len(p) > 2 else out
            calls.append(lambda e, p=p, o=o, i=i: e.matmul(ap(o), ap(p[0]), ap(p[1]), start and i == 0, stop and i == n - 1))
        emit("t", calls, sorted(set(rd)), [reg(out)], acc=not start)

    def wrap(lbuf, rbuf, lo, hi):
        return [((lbuf, 15 - r, 143 - r), (rbuf, lo + r, hi, 16)) for r in range(16)]

    def dma(q, out_ap, in_ap, reads, writes, sem):
        return emit(q, [lambda e: e.dma_start(out=out_ap, in_=in_ap)], reads, writes, sem=sem, val=16)

    def iota(buf, lo, hi, pattern, base, cm, flag):
        if flag:
            emit("g", [lambda e: e.iota(T[buf][:, lo:hi], pattern, base, cm, allow_small_or_imprecise_dtypes=True)], [], [(buf, lo, hi)])
        else:
            emit("g", [lambda e: e.iota(T[buf][:, lo:hi], pattern, base, cm)], [], [(buf, lo, hi)])

    def M(b):
        return (b, 0, 128)

    def pieces(cut):
        out = []
        for p in cut.split():
            c0 = out[-1][1] if out else 0
            out.append((c0, c0 + int(p[:-1]), p[-1]))
        return out

    TAG[0] = "setup"
    dma("y", T.EFI[:, :], T.ef[:, :], [], [("EFI", 0, 256)], "lde")
    dma("s", T.WI[:, :], T.wt[:, :], [], [("WI", 0, 1)], "ldw")
    dma("y", T.XA0[:, 4096:4608], T.zv[:, :], [], [("XA0", 4096, 4608)], "ldz")
    dma("y", T.D[:, :], T.dv[:, :], [], [("D", 0, 4096)], "ldd0")

    iota("PI", 0, 1, [[1, 1]], 0, 1, False)
    iota("XI", 0, 144, [[1, 144]], 0, 0, True)
    iota("BJ", 0, 16, [[0, 8], [16, 2]], 0, 0, False)
    fill(("K4", 0, 224), 32.0, 0, 64)
    fill(M("ON"), 1.0)
    fill(("K2", 0, 256), 16.0)
    iota("CTI", 32, 256, [[1, 224]], 2592, 0, True)
    iota("CTI", 0, 32, [[1, 32]], 2832, 0, True)
    I = ("PI", 0, 1)
    XI, XJ = ("XI", 0, 144), ("XI", 0, 128)
    ts(("PJ", 0, 1), I, 112, None, OP.bitwise_and)
    ts(("PJ", 2, 3), I, 3, 1, OP.logical_shift_right, OP.bitwise_and)
    ts(("PJ", 3, 4), I, 7, None, OP.bitwise_and)
    ts(("PJ", 1, 2), I, 15, None, OP.bitwise_and)
    copy(("PF", 6, 7), I)
    copy(("PF", 0, 4), ("PJ", 0, 4))
    ts(("PF", 9, 10), ("PF", 0, 1), ("PF", 2, 3), 14.0, OP.add, OP.add)
    ts(("KM", 0, 8), ("XI", 0, 8), ("PF", 3, 4), None, OP.is_equal)
    ts(("PF", 10, 11), ("PF", 0, 1), 15.0, None, OP.add)
    MOD = dict(zip("acb", CFG["MOD"]))
    KM = {w: "K4" if MOD[w] == "v" else "K2" for w in MOD}
    for k in range(8):
        ts(("Q%d" % k, 0, 144), XI, ("PF", 9, 10), ("KM", k, k + 1), OP.is_equal, OP.mult)
    fill(("K4", 0, 224), 1.0 / 512, 64, 128)
    ts(M("ID"), XJ, ("PF", 6, 7), None, OP.is_equal)
    ts(("OL", 0, 144), XI, ("PF", 10, 11), -SC, OP.is_equal, OP.mult)
    act(("bC", 256, 512), ("CTI", 0, 256), AF.Copy, scale=4096.0)
    for b, c in (("NG", -1.0), ("IDF", 1.0), ("NGF", -1.0), ("IC", -4.5 * SC), ("IW", 65536.0), ("IB", 4.5 * SC)):
        act(M(b), M("ID"), AF.Copy, scale=c)
    ts(("EH", 0, 256), ("EFI", 0, 256), -2048.0, None, OP.add)
    copy(("WF", 0, 1), ("WI", 0, 1))
    ts(("BL", 0, 16), ("BJ", 0, 16), ("PF", 1, 2), None, OP.add)
    ts(("WL", 0, 144), XI, ("PF", 10, 11), ("WF", 0, 1), OP.is_equal, OP.mult)

    def bring(b, k):
        mm((b, 32 * k, 32 * k + 32), [(("Q%d" % k, 14 - 2 * h, 142 - 2 * h), ("EH", h, 256, 8)) for h in range(8)])

    def usum(out, XA, lo):
        mm(out, [(M("ON"), (KM["c" if lo < 4096 else "a"], 0, 32))] + wrap("WL", XA, lo, lo + 512))
    for k in range(8):
        if k == 2:
            usum(("bU", 256, 288), "XA0", 4096)
        bring("bA" if k < 4 else "bB", k)

    def second(out, E):
        act(out, E, AF.Identity, bias=-6722560.0, scale=2080.0)

    def spread_first(EQ):
        n = 32 * max(len(p.replace(",", "")) for p in CFG["HB"].split())
        gcopy("s", ("ER", 0, n), (EQ, 0, 32), ("BL", 0, n // 16))
        second(("bK", 256, 256 + n), ("ER", 0, n))

    def round_s(src, lo):
        n = src[2] - src[1]
        w = {0: "a", 256: "c"}.get(lo, "b")
        RR = ("RH" if w == "b" and CFG["AGAIN"] else "RR", lo, lo + n)
        if MOD[w] == "v":
            return ts(RR, src, BIG, -BIG, OP.add, OP.add)
        act(("RX", lo, lo + n), src, AF.Identity, bias=BIG, scale=1.0 + 2.0 ** -22)
        act(RR, ("RX", lo, lo + n), AF.Identity, bias=-BIG)

    def value_v(w, src, lo):
        tt(("V" + w, 0, 32), src, ("RR", lo, lo + 32), OP.subtract)

    def products(w, EQ, lo, hi):
        vgather(("P" + w, lo, hi), ("V" + w, 0, 32), ("BL", 0, (hi - lo) // 16), (EQ, lo, hi), OP.mult)

    def names(w, lo, hi, sec):
        tt(("S" + w, lo, hi), ("P" + w, lo, hi), ("bK", sec, sec + hi - lo), OP.add)
        if w != "a" and CFG["U16"]:
            return ts(("L" + w, lo, hi), ("S" + w, lo, hi), 5, 4095, OP.arith_shift_right, OP.bitwise_and)
        ts(("I" + w, lo, hi), ("S" + w, lo, hi), 5, 4095, OP.arith_shift_right, OP.bitwise_and)
        copy(("L" + w, lo, hi), ("I" + w, lo, hi))


    SIDE = {c: c in CFG["GS"].split() for c in CFG["GS"].split() + CFG["GV"].split()}
    byS = {c[0] + k: s for c, s in SIDE.items() for k in c[1:]}
    byS.update({"a" + k: True for k in CFG["SS"].replace(" ", "")})
    BIAS = {}
    CE = CFG["CE"]
    for w, c in (("a", "NA"), ("c", "NC"), ("b", "NB")):
        for grp in CFG[c].split():
            assert len({byS[w + k] for k in grp}) == 1
            BIAS[w + grp] = (-4.5 if w == "c" and int(grp[0]) <= CE else 0.0) + (-0.5 if byS[w + grp[0]] else 7.5)
            if CFG["CHOICE"] == "v":
                BIAS[w + grp] = (4.5 if w == "a" else 0.0) + (-0.5 if byS[w + grp[0]] else 7.5)
    BCOL = {v: 160 * i for i, v in enumerate(sorted(set(BIAS.values())))}

    def biases():
        for v, o in BCOL.items():
            fill(("BT", o, o + 160), v * SC / 64, 0, 64)
        fill(("BT", 0, 160 * len(BCOL)), SC / 64, 64, 128)
        fill(M("PB"), 1.0, 0, 64)
        fill(M("PB"), 0.0, 64, 128)
    biases()
    for j, cut in (("JM", "CUT"), ("JL", "LCUT")):
        for c0, c1, how in pieces(CFG[cut]):
            iota(j, c0, c1, [[128, c1 - c0]], 0, 0, False)
    iota("THR", 0, 224, [[32, 7], [0, 32]], 2592, 0, True)
    ts(("OH", 0, 144), XI, ("PF", 10, 11), -SC / 2, OP.is_equal, OP.mult)
    fill(("K3", 0, 256), -0.5 / 128)
    ts(("PF", 11, 12), ("PF", 1, 2), -41472.0, None, OP.add)
    ts(("PF", 12, 13), ("PF", 1, 2), 8.0, None, OP.mult)
    ts(("O16", 0, 144), XI, 0.0, 1.0, OP.mult, OP.add)

    def slots():
        for j in ("JM", "JL"):
            ts((j, 0, 32), (j, 0, 32), ("PF", 12, 13), None, OP.add)
    for h in range(8):
        emit("g", [lambda e, h=h: e.affine_select(T["R%d" % h][:, :], T.O16[:, :], [[-16, 9], [-1, 2], [1000, 8]], OP.is_equal, 0.0,
                                                  -2 * h - 7000, 1)], [("O16", 0, 144)], [("R%d" % h, 0, 144)])
    round_s(("bU", 256, 288), 0)
    act(("EQ0", 0, 128), ("bA", 0, 128), AF.Identity, bias=3232.0)
    second(("bK", 0, 128), ("EQ0", 0, 128))
    value_v("a", ("bU", 256, 288), 0)
    products("a", "EQ0", 0, 128)
    act(("EQ0", 128, 256), ("bB", 128, 256), AF.Identity, bias=3232.0)
    names("a", 0, 128, 0)
    second(("bK", 128, 256), ("EQ0", 128, 256))
    products("a", "EQ0", 128, 256)
    names("a", 128, 256, 128)
    if not CFG["PACK"]:
        tt(("NP", 0, 256), ("Ia", 0, 256), ("bC", 256, 512), OP.add)
    REC.append(None)

    for t in range(RO):
        last = t == RO - 1
        XA, XN = "XA%d" % (t % 2), "XA%d" % ((t + 1) % 2)
        EQ, EN = "EQ%d" % (t % 2), "EQ%d" % ((t + 1) % 2)
        PKS = "PKS%d" % (t % 2)
        ZB = (XA, 4096, 4608)
        DW = ("D", 0, 4096)
        SN = ("SN", 0, 32)
        ORDER = CFG["ORDER"].split()
        tasks = {}

        def add(name, pre, fn):
            tasks[name] = (pre, fn)

        def xa(k, n=1):
            b = (k - 1) % 8
            return (XA, 512 * b, 512 * (b + n))

        def cols(name, k, n=1):
            return (name, 32 * k, 32 * (k + n))

        def blk(name, k, n=1):
            return (name, 512 * k, 512 * (k + n))
        HG = [[[int(x) for x in s] for s in p.split(",")] for p in CFG["HB"].split()]
        hb = {k: "HB%d" % p[0][0] for p in HG for s in p for k in s}
        used, reader = [0], [[], []]
        sign = {}
        spare = [0]
        gets = {}
        for call, s in SIDE.items():
            w, ks = call[0], [int(x) for x in call[1:]]
            k0, n = ks[0], len(ks)
            G, L = "G" + w.upper(), "L" + w
            pre = {"a": [], "c": ["HC"], "b": sorted({hb.get(k) for k in ks})}[w]
            gn = "g%s%d" % (w, k0)
            gets[gn] = [w + str(k) for k in ks]
            if s:
                if w == "a":
                    DS, o = "DS", k0
                else:
                    DS, o = "DT", spare[0]
                    spare[0] += n
                add(gn, pre, lambda DS=DS, o=o, n=n, L=L, k0=k0: gcopy("s", blk(DS, o, n), DW, cols(L, k0, n)))
                nm = str(k0) if w == "a" else w + str(k0)
                b0 = used[0] % 2 if n == 1 else 0
                used[0] = b0 + n
                bank = blk("bS", b0, n)

                def do_st(ks=ks, w=w, b0=b0, DS=DS, o=o):
                    for i, k in enumerate(ks):
                        mm(blk("bS", b0 + i), [(M("ID"), blk(DS, o + i)), (M("NG"), {"a": ZB, "c": xa(0), "b": xa(k)}[w])])
                add("st" + nm, [gn] + sorted({x for i in range(n) for x in reader[b0 + i]}), do_st)
                sg = "s%s%d" % (w, k0)
                add(sg, ["st" + nm], lambda k0=k0, n=n, bank=bank, G=G: act(blk(G, k0, n), bank, AF.Sign, bias=-0.5))
                if w == "a":
                    add("abs%d" % k0, ["st" + nm], lambda k0=k0, n=n, bank=bank: act(xa(k0, n), bank, AF.Abs))
                for i, k in enumerate(ks):
                    sign[w + str(k)] = sg
                    reader[b0 + i] = [sg] + ["abs%d" % k0] * (w == "a")
                    if w == "a" and i:
                        add("abs%d" % k, ["abs%d" % k0], lambda: None)
            elif w == "a":
                add(gn, pre, lambda k0=k0: vgather(blk("XB", k0), DW, cols("La", k0), ZB, OP.subtract))
                grp = [x for x in CFG["AV"].split() if str(k0) in x][0]
                if int(grp[0]) == k0:
                    add("abs%d" % k0, ["ga" + x for x in grp], lambda k0=k0, n=len(grp): act(xa(k0, n), blk("XB", k0, n), AF.Abs))
                else:
                    add("abs%d" % k0, ["abs" + grp[0]], lambda: None)
                grp = [x for x in CFG["SV"].split() if str(k0) in x][0]
                sign[call] = "sa" + grp[0]
                if int(grp[0]) == k0 and grp in CFG["SS"].split():
                    add("sa%d" % k0, ["ga" + x for x in grp],
                        lambda k0=k0, n=len(grp): act(blk("GA", k0, n), blk("XB", k0, n), AF.Sign, bias=-0.5))
                elif int(grp[0]) == k0:
                    add("sa%d" % k0, ["ga" + x for x in grp],
                        lambda k0=k0, n=len(grp): ts(blk("GA", k0, n), blk("XB", k0, n), 0.0, None, OP.is_gt))
            else:
                y = xa(0) if w == "c" else xa(k0, n)
                add(gn, pre, lambda G=G, L=L, k0=k0, n=n, y=y: vgather(blk(G, k0, n), DW, cols(L, k0, n), y, OP.is_gt))
                for k in ks:
                    sign[w + str(k)] = gn
        E = CFG["EARLY"]

        def cb(k, n):
            return cols("bB" if k <= E else "bM", k, n)

        def count(w, grp):
            G, B = {"a": ("GA", "bA"), "b": ("GB", None), "c": ("GC", "bC")}[w]
            k0, n = int(grp[0]), len(grp)
            out = cols(B, k0, n) if B else cb(k0, n)
            o = BCOL[BIAS[w + grp]]
            parts = [(M("PB"), ("BT", o, o + 32 * n))]
            if w != "a":
                parts += [(M("I" + w.upper()), SN, cols(out[0], k0 + i)) for i in range(n)]
            mm(out, parts + wrap("OH" if byS[w + grp[0]] else "OL", G, 512 * k0, 512 * (k0 + n)))
        for w, c in (("a", "NA"), ("c", "NC"), ("b", "NB")):
            for grp in CFG[c].split():
                add("n" + w + grp[0], [sign[w + k] for k in grp] + ([] if w == "a" else ["SN"]), lambda w=w, grp=grp: count(w, grp))

        def groups(c, w, lo, hi):
            return ["n" + w + grp[0] for grp in CFG[c].split() if lo <= int(grp[0]) <= hi]
        add("SN", ["na0"], lambda: act(SN, cols("bA", 0), AF.Sign, bias=-4.5 * SC if CFG["CHOICE"] == "v" else 0.0))
        add("SP0", [], lambda: None if t else spread_first(EQ))
        add("U0", ["abs0"], lambda: usum(("bM", 288, 320), XA, 3584))
        add("RC", ["U0"], lambda: round_s(("bM", 288, 320), 256))

        def do_hc():
            value_v("c", ("bM", 288, 320), 256)
            products("c", EQ, 32, 256)
            names("c", 32, 256, 32)
        MG = min(CFG["MERGE"], 1)
        add("HC", ["RC"] + ([] if MG else ["S7"]), do_hc)

        def do_e7():
            tp, E7 = (t, EN) if MG else (t - 1, EQ)
            if (not last) if MG else t:
                ts(cols("NM", 0), cols("LP%d" % tp, 0), 4095, None, OP.bitwise_and)
                ts(cols(E7, 7), cols("NM", 0), 1184.0, None, OP.add)
        add("E7", ["TX"] if MG else [], do_e7)
        add("S7", ["E7"], lambda: second(cols("bK", 7), cols(EN if MG else EQ, 7)) if ((not last) if MG else t) else None)

        def do_h7():
            if t and not MG:
                tt(cols("Pa", 7), cols(EQ, 7), cols("Va", 0), OP.mult)
                names("a", 224, 256, 224)
        add("H7", [] if MG else ["S7"], do_h7)
        for k in range(4, 8):
            tasks[[n for n in gets if "a%d" % k in gets[n]][0]][0].append("H7")
        for i, p in enumerate(HG):
            B, k0, n = ("bU", "bM")[i], p[0][0], sum(len(s) for s in p)
            for j, s in enumerate(p):
                def do_u(B=B, k0=k0, n=n, s=s, j=j, end=j == len(p) - 1):
                    o = cols(B, s[0], len(s))
                    parts = [x + (o,) for x in wrap("WL", XA, 512 * (s[0] - 1), 512 * s[-1])]
                    if j == 0:
                        parts = [(M("ON"), (KM["b"], 0, 32 * n))] + parts
                    mm(cols(B, k0, n) if j == 0 else o, parts, j == 0, end)
                add("U%d" % s[0], ["abs%d" % k for k in s] + (["U%d" % p[j - 1][0]] if j else ["HC"] if i else []), do_u)

            add("RB%d" % k0, ["U%d" % p[-1][0]], lambda B=B, k0=k0, n=n: round_s(cols(B, k0, n), 32 * k0))

            def do_hb(B=B, k0=k0, n=n, i=i):
                if CFG["AGAIN"]:
                    V = cols(B, 9 + i, n)
                    mm(V, [(M("ON"), ("K2", 0, 32 * n))] + wrap("WL", XA, 512 * (k0 - 1), 512 * (k0 + n - 1)) + [(M("NG"), cols("RH", k0, n))])
                    tt(cols("Pb", k0, n), ("ER", 0, 32 * n), V, OP.mult)
                elif MOD["b"] == "v":
                    tt(cols("Vb", k0, n), cols(B, k0, n), cols("RR", k0, n), OP.subtract)
                    vgather(cols("Pb", k0, n), cols(EQ, 0), ("BL", 0, 2 * n), cols("Vb", k0, n), OP.mult)
                else:
                    tt(cols(B, k0, n), cols(B, k0, n), cols("RR", k0, n), OP.subtract)
                    tt(cols("Pb", k0, n), ("ER", 0, 32 * n), cols(B, k0, n), OP.mult)
                names("b", 32 * k0, 32 * (k0 + n), 256)
            add("HB%d" % k0, ["RB%d" % k0, "SP0"], do_hb)
        def pack():
            tt(("NP", 0, 256), ("Ia", 0, 256), ("bC", 256, 512), OP.add)
        add("pack", ["H7"], lambda: pack() if CFG["PACK"] else None)
        add("PN", ["HN"], lambda: pack() if not CFG["PACK"] and not last else None)
        add("DIFF", [] if MG else ["E7"], lambda: mm(("bA", 288, 512), [(M("IDF"), (EQ, 32, 256)), (M("NGF"), (EQ, 0, 224))]))

        add("FA", groups("NA", "a", 0, 7), lambda: act(cols("FA", 1, 7), cols("bA", 1, 7), AF.Relu))
        add("FC", groups("NC", "c", 1, CE), lambda: act(cols("FC", 1, CE), cols("bC", 1, CE), AF.Relu))
        for k0, n in ((1, E), (E + 1, 7 - E)):
            def do_y(k0=k0, n=n):
                act(cb(k0, n), cb(k0, n), AF.Abs)
                act(cols("FY", k0, n), cb(k0, n), AF.Relu, bias=-4.5 * SC)
            add("Y%d" % k0, groups("NB", "b", k0, k0 + n - 1), do_y)

        def more(b, k0, n):
            return (M("ID"), cols(b, k0, n), cols("bU", k0, n))
        add("W0", ["pack", "SN", "HB1"], lambda: mm(cols("bU", 0, 8), [(M("IDF"), cols("NP", 0, 8)), (M("IW"), SN, cols("bU", 0))], True, False))
        add("W1", ["W0", "FA", "FC", "Y1"], lambda: mm(cols("bU", 1, 7), [more("FA", 1, 7), more("FC", 1, CE), more("FY", 1, E)], False, False))
        add("W2", ["W1", "Y%d" % (E + 1)], lambda: mm(cols("bU", E + 1, 7 - E), [more("FY", E + 1, 7 - E)], False, True))
        add("WS", ["W2"], lambda: act(cols("WK", 4, 4), cols("bU", 4, 4), AF.Copy))

        def do_early():
            if CE == 5:
                tt(cols("TR", 0, 2), cols("bU", 0, 2), cols("WK", 4, 2), OP.min)
                tt(cols("TR", 2, 2), cols("bU", 2, 2), cols("TR", 0, 2), OP.min)
            elif CE == 6:
                tt(cols("TR", 0, 3), cols("bU", 1, 3), cols("WK", 4, 3), OP.min)
                tt(cols("TR", 3), cols("bU", 0), cols("TR", 0), OP.min)
                tt(cols("TR", 4), cols("TR", 1), cols("TR", 2), OP.min)
                tt(cols("TR", 5), cols("TR", 3), cols("TR", 4), OP.min)
            else:
                tt(cols("TR", 0, 4), cols("bU", 0, 4), cols("WK", 4, 4), OP.min)
        add("EARLY", ["WS"], do_early)

        def do_last():
            if CE < 7:
                tt(cols("WK", CE + 1, 7 - CE), cols("WK", CE + 1, 7 - CE), cols("bC", CE + 1, 7 - CE), OP.max)
            if CE == 6:
                tt(cols(PKS, 0), cols("WK", 7), cols("TR", 5), OP.min)
            else:
                tt(cols("TR", 4, 2), cols("TR", 2, 2), cols("WK", 6, 2) if CE == 5 else cols("TR", 0, 2), OP.min)
                tt(cols(PKS, 0), cols("TR", 4), cols("TR", 5), OP.min)
            ts(cols("TS", 0), cols(PKS, 0), 12, None, OP.arith_shift_right)
            ts(cols("LS", 0), cols("TS", 0), 16.0, ("PF", 11, 12), OP.mult, OP.add)
        add("LAST", ["EARLY"] + groups("NC", "c", CE + 1, 7), do_last)
        if CFG["CHOICE"] == "v":
            for n in ("FA", "FC", "W1", "W2", "WS", "EARLY", "LAST"):
                del tasks[n]
            W0 = ("bA", 256, 288)
            cw = [cb]
            add("W0", ["pack", "SN"], lambda: mm(W0, [(M("IDF"), cols("NP", 0)), (M("IW"), SN)]))
            add("NT", ["pack"] + groups("NA", "a", 0, 7), lambda: tt(cols("NT", 1, 7), cols("bA", 1, 7), cols("NP", 1, 7), OP.max))
            add("NC", ["NT"] + groups("NC", "c", 1, CE), lambda: tt(cols("NT", 1, CE), cols("bC", 1, CE), cols("NT", 1, CE), OP.max))
            add("Y1", groups("NB", "b", 1, E), lambda: act(cb(1, E), cb(1, E), AF.Abs))
            add("Y%d" % (E + 1), groups("NB", "b", E + 1, 7), lambda: act(cb(E + 1, 7 - E), cb(E + 1, 7 - E), AF.Abs))

            def v_early():
                tt(cols("WK", 1, E), cols("NT", 1, E), cw[0](1, E), OP.max)
                h = E // 2
                tt(cols("TR", 0, h), cols("WK", 1, h), cols("WK", 1 + h, h), OP.min)
                if E > 4:
                    tt(cols("TR", 3), cols("WK", 5) if E == 5 else cols("TR", 2), W0, OP.min)
                tt(cols("TR", 5), cols("TR", 0), cols("TR", 1), OP.min)
                tt(cols("TR", 4), cols("TR", 5), cols("TR", 3) if E > 4 else W0, OP.min)
            add("EARLY", ["NC", "Y1", "W0"], v_early)
            best = [cols("TR", 4)]

            def fold(ks, end):
                items = [cols("WK", k) for k in ks] + best
                i = 0
                while len(items) > 1:
                    out = end if len(items) == 2 and end else cols("TR", (5, 6, 7)[i])
                    tt(out, items[0], items[1], OP.min)
                    items = items[2:] + [out]
                    i += 1
                best[0] = items[0]

            def v_late():
                tt(cols("WK", E + 1, 7 - E), cols("NT", E + 1, 7 - E), cw[0](E + 1, 7 - E), OP.max)
                fold(range(E + 1, CE + 1), cols(PKS, 0) if CE == 7 else cols("TR", 0))
            add("LATE", ["EARLY", "Y%d" % (E + 1)], v_late)

            def v_last():
                if CE < 7:
                    tt(cols("WK", CE + 1, 7 - CE), cols("WK", CE + 1, 7 - CE), cols("bC", CE + 1, 7 - CE), OP.max)
                    fold(range(CE + 1, 8), cols(PKS, 0))
                ts(cols("TS", 0), cols(PKS, 0), 12, None, OP.arith_shift_right)
                ts(cols("LS", 0), cols("TS", 0), 16.0, ("PF", 11, 12), OP.mult, OP.add)
            add("LAST", ["LATE"] + groups("NC", "c", CE + 1, 7), v_last)
            if CFG["MIX"]:
                W0 = cols("bU", 0)
                add("NT", groups("NA", "a", 0, 7), lambda: act(cols("FA", 1, 7), cols("bA", 1, 7), AF.Relu, bias=-4.5 * SC))
                add("NC", groups("NC", "c", 1, CE), lambda: act(cols("FC", 1, CE), cols("bC", 1, CE), AF.Relu, bias=-4.5 * SC))
                add("W0", ["pack", "SN", "HB1"], lambda: mm(cols("bU", 0, 8), [(M("IDF"), cols("NP", 0, 8)), (M("IW"), SN, cols("bU", 0))], True, False))
                add("W1", ["W0", "NT", "NC"], lambda: mm(cols("bU", 1, 7), [more("FA", 1, 7), more("FC", 1, CE)], False, True))
                for k0, n in ((1, E), (E + 1, 7 - E)):
                    add("Y%d" % k0, groups("NB", "b", k0, k0 + n - 1), lambda k0=k0, n=n: act(cols("NT", k0, n), cb(k0, n), AF.Abs))
                tasks["EARLY"][0].append("W1")
                cw = [lambda k, n: cols("bU", k, n)]

        dst = T.cores[(rank + 1 + t % (N - 1)) % N]
        rid, pid = topo.addr(dst)[0], topo.addr(dst)[1]
        mask = topo.mask(core, dst)
        ne = len(topo.engines(core, dst))

        def send(out, in_, rsem, lsem):
            emit("g", [lambda e: e.remote_dma(ap(out), ap(in_), T.sem[rsem], T.sem[lsem], pid, rid, mask)],
                 [reg(in_)], [], sem=lsem, val=ne, remote=out + (rsem,))
        LP, LZ = "LP%d" % t, "LZ%d" % t

        def later(fn):
            return (lambda: None) if last else fn
        add("TX", ["LAST"], lambda: send(cols(LP, 0), cols(PKS, 0), "an%d" % t, "ln%d" % t))
        SENT = pieces(CFG["LSENDS" if last else "SENDS"])
        for h, (c0, c1, how) in enumerate(SENT):
            def do_z(h=h, c0=c0, c1=c1, how=how):
                Z = (XN, 4096 + 16 * c0, 4096 + 16 * c1)
                gcopy(how, Z, (XA, 0, 4608), ("LS", c0, c1))
                if not CFG.get("ONE"):
                    send((LZ, 16 * c0, 16 * c1), Z, "az%d_%d" % (t, h), "lz%d_%d" % (t, h))
                elif h:
                    send((LZ, 0, 512), (XN, 4096, 4608), "az%d_%d" % (t, h), "lz%d_%d" % (t, h))
            add("Z%d" % h, ["TX"] + ["Z%d" % (h - 1)] * (h > 0), do_z)
        ZL = "Z%d" % (len(SENT) - 1)

        def do_p2():
            ts(cols("S0", 0), cols("TS", 0), 2816.0, 512.0, OP.is_ge, OP.mult)
            tt(cols("P2", 0), cols("TS", 0), cols("S0", 0), OP.subtract)
        add("P2", ["LAST"], do_p2)
        add("UZ", [ZL], later(lambda: usum(("bU", 256, 288), XN, 4096)))
        add("PA", ["P2"], later(lambda: mm(("bM", 256, 288), [(M("ON"), cols("S0", 0))])))
        add("MK", ["P2"], lambda: vgather(("MK", 0, 224), cols("P2", 0), ("BL", 0, 14), ("THR", 0, 224), OP.is_lt))
        add("RZ", ["UZ"], later(lambda: round_s(("bU", 256, 288), 0)))

        def do_sh():
            tt(("bA", 288, 512), ("bA", 288, 512), ("MK", 0, 224), OP.mult)
            tt((EN, 0, 224), ("bA", 288, 512), (EQ, 0, 224), OP.add)
        add("SH", ["MK", "DIFF"], do_sh)
        if CFG["MERGE"] == 2:
            add("SE", ["SH", "E7"], later(lambda: second(("bK", 0, 256), (EN, 0, 256))))
            add("S7", ["SE"], lambda: None)
        else:
            add("SE", ["SH"], later(lambda: second(("bK", 0, 224), (EN, 0, 224))))

        def do_hn():
            if last:
                ts(cols("NM", 0), cols(LP, 0), 4095, None, OP.bitwise_and)
                ts(cols("EH", 7), cols("NM", 0), -2048.0, None, OP.add)
            else:
                value_v("a", ("bU", 256, 288), 0)
                n = 256 if CFG["MERGE"] in (1, 2) else 224
                products("a", EN, 0, n)
                if CFG["MERGE"] == 4:
                    tt(("Sa", 0, n), ("Pa", 0, n), ("bK", 0, n), OP.add)
                else:
                    names("a", 0, n, 0)
        add("HN", ["SE", "RZ"] + ["S7"] * (CFG["MERGE"] in (1, 2)), do_hn)

        def do_h8():
            tt(cols("Pa", 7), cols(EN, 7), cols("Va", 0), OP.mult)
            if CFG["MERGE"] == 3:
                names("a", 224, 256, 224)
            else:
                tt(cols("Sa", 7), cols("Pa", 7), cols("bK", 7), OP.add)
                ts(("Ia", 0, 256), ("Sa", 0, 256), 5, 4095, OP.arith_shift_right, OP.bitwise_and)
                copy(("La", 0, 256), ("Ia", 0, 256))
        if CFG["MERGE"] > 2:
            add("H8", ["HN", "S7"], later(do_h8))
            tasks["PN"][0].append("H8")
            if MOD["a"] == "v":
                add("S7", ["E7"], later(lambda: ts(cols("bK", 7), cols(EN, 7), 2080.0, -6722560.0, OP.mult, OP.add)))
        def do_ar():
            if not t:
                slots()
            ts(cols("CI", 0), cols(LP, 0), 7, None, OP.bitwise_and)
            tt(cols("CJ", 0), cols("CI", 0), cols("JL" if last else "JM", 0), OP.add)
            copy(cols("LD", 0), cols("CJ", 0))
        add("AR", ["TX"], do_ar)
        for q, (c0, c1, how) in enumerate(pieces(CFG["LCUT" if last else "CUT"])):
            R, W, C = (16 * c0, 16 * c1), ("D", 128 * c0, 128 * c1), ("LD", c0, c1)
            b, o = (("bS", 0), ("bS", 512), ("bB", 0))[q % 3]
            b = (b, o, o + 16 * (c1 - c0))

            def do_up(R=R, b=b, how=how):
                extra = [(M("ON"), ("K3", 0, b[2] - b[1]))] if how == "s" else []
                mm(b, extra + [(M("ID"), ("DC",) + R), (M("ID"), (LZ,) + R)])
                if how == "s":
                    act(("FX",) + R, b, AF.Identity, bias=MID, scale=0.5)
                    act(("FB",) + R, ("FX",) + R, AF.Identity, bias=-MID)

            def do_sc(q=q, R=R, W=W, C=C, b=b, how=how):
                F = ("FB",) + R if how == "s" else ("FL",) + R
                if how == "v":
                    ts(F, b, 0.5, -0.25, OP.mult, OP.add)
                emit("v", [lambda e: e.tensor_copy(ap(W).indirect(ap(C)), ap(F))], [F, C], [W])
                if last:
                    dma("y", T.yd[:, W[1]:W[2]], ap(W), [W], [], "sd%d" % q)
            add("DC%d" % q, ["AR"], lambda R=R, W=W, C=C: gcopy("s", ("DC",) + R, W, C))
            add("UP%d" % q, ["DC%d" % q, ZL if CFG.get("ONE") else "Z%d" % min(h for h, p in enumerate(SENT) if c1 <= p[1])], do_up)
            add("SC%d" % q, ["UP%d" % q], do_sc)
        if last:
            add("YZ", [ZL], lambda: dma("s", T.yz[:, :], T[XN][:, 4096:4608], [(XN, 4096, 4608)], [], "sz"))

            def back(ks):
                return [(("R%d" % h, 7 - k, 135 - k), cols("EH", k), ("bU", h, 256, 8)) for k in ks for h in range(8)]

            def do_ye0():
                ts(("EH", 0, 224), (EN, 0, 224), -3232.0, None, OP.add)
                for k in range(7):
                    mm(cols("bU", 0, 8), [(M("ON"), ("K2", 0, 256))] * (k == 0) + back([k]), k == 0, False)

            def do_ye1():
                mm(cols("bU", 0, 8), back([7]), False, True)
                act(("YE", 0, 256), cols("bU", 0, 8), AF.Copy)
                dma("s", T.ye[:, :], T.YE[:, :], [("YE", 0, 256)], [], "se")
            def do_ye(h0):
                b = ("bM", "bU")[h0 // 4]
                for h in range(h0, h0 + 4):
                    mm(cols(b, h), [(("R%d" % h, 7 - k, 135 - k), cols("EH", k)) for k in range(8)])
                for h in range(h0, h0 + 4):
                    act(("YE", h, 256, 8), cols(b, h), AF.Identity, bias=2048.0)
                if h0:
                    dma("s", T.ye[:, :], T.YE[:, :], [("YE", 0, 256)], [], "se")
            add("YH", ["SH"], lambda: ts(("EH", 0, 224), (EN, 0, 224), -3232.0, None, OP.add))
            add("YE0", ["HN", "YH"], lambda: do_ye(0))
            add("YE1", ["YE0"], lambda: do_ye(4))
            ORDER = ORDER[:ORDER.index("LAST") + 1] + CFG["END"].split()
            for n in set(tasks) - set(ORDER) - {o.strip(".") for o in ORDER}:
                del tasks[n]

        def do_pt():
            emit("s", [lambda e: e.activation(T.AJ[:, 0:32], T.bM[:, 256:288], AF.Copy, scale=1.0 / 512, accum_out=T.AR[:, 0:1])],
                 [("bM", 256, 288)], [("AJ", 0, 32), ("AR", 0, 1)])
            act(("AR", 1, 2), ("AR", 0, 1), AF.Identity, bias=MID, scale=0.5)
            act(("AR", 2, 3), ("AR", 1, 2), AF.Identity, bias=2 * MID, scale=-2.0)
            emit("s", [lambda e: e.activation(T.PB[64:128, :], T.ON[64:128, :], AF.Abs, bias=T.AR[64:128, 0:1], scale=T.AR[64:128, 2:3])],
                 [M("ON"), ("AR", 0, 3)], [M("PB")])
        if not last:
            add("PT", ["PA"], do_pt)
            add("SP", ["SH"], lambda: spread_first(EN))

        whole = [o for o in ORDER if o[-1] != "."]
        assert sorted(whole) == sorted(tasks), set(tasks) ^ set(whole)
        steps = {}
        for nm in tasks:
            held[0] = steps[nm] = []
            tasks[nm][1]()
        held[0] = None
        done = []
        if t == 1:
            TAG[2:] = [{n: list(tasks[n][0]) for n in tasks}]
        for n in tasks:
            tasks[n][0][:] = [p for p in tasks[n][0] if p in tasks]
        todo = list(ORDER)
        while todo:
            o = [x for x in todo if all(p in done for p in tasks[x.strip(".")][0])][0]
            todo.remove(o)
            tasks[o.strip(".")][0][:] = []
            nm = o.strip(".")
            TAG[0] = nm
            for _ in range(min(len(steps[nm]), 1) if o != nm else len(steps[nm])):
                steps[nm].pop(0)()
            done.append(o)
        if t == 1:
            TAG[1:2] = [" ".join(done)]
        TAG[0] = "end"
        REC.append(None)
    settle("g", ends)
    settle("g", [(qsem[q], cnt[q], {}) for q in "vstg"])
